import numpy as np
import ml_dtypes


def mxq(x, axis, fmt="e4m3"):
    dtype, down = {"e4m3": (ml_dtypes.float8_e4m3fn, 7), "e5m2": (ml_dtypes.float8_e5m2, 14)}[fmt]
    v = np.moveaxis(np.asarray(x, np.float32).astype(ml_dtypes.bfloat16).astype(np.float64), axis, -1)
    blocks = v.reshape(v.shape[:-1] + (-1, 32))
    amax = np.abs(blocks).max(-1, keepdims=True)
    byte = np.maximum(np.where(amax > 0, np.frexp(amax)[1] - 1 + 127, 0) - down, 1)
    scale = np.exp2(byte - 127.0)
    codes = (blocks / scale).astype(np.float32).astype(dtype).astype(np.float64)
    return np.moveaxis((codes * scale).reshape(v.shape), -1, axis)


WIDE = False


def mx_kscale(k):
    if not WIDE:
        return np.ones(k)
    levels = np.array([24, -24, 12, -12, 0])
    if k % 512:
        return np.exp2(np.random.permutation(np.resize(levels, k // 32))).repeat(32)
    a = np.empty((k // 512, 16))
    for p in range(k // 512):
        a[p, :8] = np.random.permutation(np.resize(levels, 8))
        for g in range(8):
            far = levels[np.abs(levels - a[p, g]) >= 10]
            a[p, g + 8] = far[np.random.randint(len(far))]
    return np.exp2(a.ravel()).repeat(32)


def f64(x):
    return np.asarray(x).astype(np.float64)


def striped(idx):
    return np.tile(idx.reshape(-1, 16).T, (8, 1)).astype(np.uint16)


def unstriped(offs):
    return offs[:16].T.reshape(-1).astype(np.int64)


E2M1 = np.array([0.0, 0.5, 1.0, 1.5, 2.0, 3.0, 4.0, 6.0, -0.0, -0.5, -1.0, -1.5, -2.0, -3.0, -4.0, -6.0])


def pack_weight(w, fmt):
    k, n = w.shape
    w = f64(np.asarray(w, np.float32).astype(ml_dtypes.bfloat16)).reshape(k // 32, 32, n)
    amax = np.abs(w).max(1)
    if fmt == "e4m3":
        byte = np.frexp(amax)[1] - 1 + 127 - 7
    else:
        mant, ex = np.frexp(amax / 6.0)
        byte = np.where(mant > 0.5, ex, ex - 1) + 127
    byte = np.clip(np.where(amax > 0, byte, 1), 1, 254)
    scaled = (w * np.exp2(127.0 - byte)[:, None, :]).reshape(k, n).astype(np.float32)
    by_word = np.ascontiguousarray(scaled.reshape(k // 512, 128, 4, n).transpose(0, 1, 3, 2))
    if fmt == "e4m3":
        words = by_word.astype(ml_dtypes.float8_e4m3fn).view(np.uint8)
    else:
        c = by_word.astype(ml_dtypes.float4_e2m1fn).view(np.uint8) & 0xF
        words = (c[..., 0::2] | (c[..., 1::2] << 4)).reshape(k // 512, 128, 2 * n)
    return np.ascontiguousarray(words), np.ascontiguousarray(byte.astype(np.uint8).reshape(k // 512, 16, n))


def unpack_weight(words, scales, fmt):
    g, _, n = scales.shape
    words = np.ascontiguousarray(words).reshape(g, 128, n, -1)
    if fmt == "e4m3":
        vals = words.view(ml_dtypes.float8_e4m3fn).astype(np.float64)
    else:
        nib = np.empty((g, 128, n, 4), np.uint8)
        nib[..., 0::2] = words & 0xF
        nib[..., 1::2] = words >> 4
        vals = E2M1[nib]
    vals = vals * np.repeat(np.exp2(scales.astype(np.float64) - 127.0), 8, axis=1)[..., None]
    return vals.transpose(0, 1, 3, 2).reshape(g * 512, n)


def pack_table4(v):
    words, scales = pack_weight(v, "e2m1")
    g, t = words.shape[0] // 2, v.shape[1]
    return np.ascontiguousarray(words.reshape(g, 2, 128, t, 2).transpose(0, 2, 3, 1, 4).reshape(g, 128, t, 4)), scales


def unpack_table4(words, scales):
    g, _, t, _ = words.shape
    return unpack_weight(words.reshape(g, 128, t, 2, 2).transpose(0, 3, 1, 2, 4).reshape(2 * g, 128, 2 * t), scales, "e2m1")


K, M, N, J, T = 1024, 512, 256, 2048, 4096


def setup_inputs():
    n = np.random.standard_normal
    s = mx_kscale(K)[:, None]
    u = mx_kscale(J)[:, None]
    p_tab = pack_table4(0.5 * n((K, T)) / np.sqrt(K) / s)
    p_al = pack_weight(n((J, N)) / np.sqrt(J) / u, "e4m3")
    return {
        "x": (n((K, M)) * s).astype(np.float32),
        "tab_words": p_tab[0],
        "tab_scales": p_tab[1],
        "cw": (np.random.uniform(0.5, 2.0, J) * u[:, 0]).astype(np.float32),
        "cb": (0.3 * n(J)).astype(np.float32),
        "al_words": p_al[0],
        "al_scales": p_al[1],
        "offs": striped(np.random.permutation(T)[:J]),
    }


def reference(x, tab_words, tab_scales, cw, cb, al_words, al_scales, offs):
    idx = unstriped(offs)
    x_ = mxq(f64(x), 0, "e4m3")
    tab_ = unpack_table4(tab_words, tab_scales)[:, idx]
    d = tab_.T @ x_
    h = f64(cw)[:, None] * np.tanh(d + f64(cb)[:, None])
    h_ = mxq(h, 0, "e4m3")
    al_ = unpack_weight(al_words, al_scales, "e4m3")
    y = al_.T @ h_
    return y

@@ -1,0 +1,182 @@
+from contextlib import ExitStack
+
+import concourse.mybir as mybir
+
+K, M, N, J, T = 1024, 512, 256, 2048, 4096
+FLOPS = 2 * K * J * M + 2 * J * N * M
+
+F32 = mybir.dt.float32
+BF16 = mybir.dt.bfloat16
+I32 = mybir.dt.int32
+U32 = mybir.dt.uint32
+U16 = mybir.dt.uint16
+U8 = mybir.dt.uint8
+FP8X4 = mybir.dt.float8_e4m3fn_x4
+FP4X4 = mybir.dt.float4_e2m1fn_x4
+TANH = mybir.ActivationFunctionType.Tanh
+MULT = mybir.AluOpType.mult
+
+P = 128
+PACK = 4
+PASS = P * PACK
+K_PASSES = K // PASS
+J_PASSES = J // PASS
+HALF = M // 2
+LIST_COLS = PASS // 16
+
+
+def tile_list_kernl_tanh_none_kernel(
+    tc, x, tab_words, tab_scales, cw, cb, al_words, al_scales, offs, out
+):
+    nc = tc.nc
+    with ExitStack() as ctx:
+        keep = ctx.enter_context(tc.tile_pool(name="keep", bufs=1))
+        psum = ctx.enter_context(tc.psum_pool(name="psum", bufs=1))
+
+        offsets = keep.tile([P, J // 16], U16, name="offsets")
+        nc.sync.dma_start(offsets[:], offs)
+
+        scale_table = keep.tile([P, T], U8, name="scale_table", align_bytes=64)
+        nc.sync.dma_start(
+            out=scale_table[0:32, :].bitcast(I32),
+            in_=tab_scales.bitcast(I32).rearrange("d q w -> q d w"),
+        )
+        word_table = keep.tile([P, T], I32, name="word_table", align_bytes=64)
+        nc.sync.dma_start(out=word_table[:], in_=tab_words[0].rearrange("p t b -> p (t b)").bitcast(I32))
+
+        x_rows = x.rearrange("(d p i) m -> d p i m", p=P, i=PACK)
+        x_first = keep.tile([P, PACK, M], F32, name="x_first")
+        nc.sync.dma_start(out=x_first[:], in_=x_rows[0])
+        x_raw = {(0, h): x_first[:, :, h * HALF : (h + 1) * HALF] for h in range(2)}
+        for h in range(2):
+            piece = keep.tile([P, PACK, HALF], F32, name="x_second%d" % h)
+            nc.sync.dma_start(out=piece[:], in_=x_rows[1][:, :, h * HALF : (h + 1) * HALF])
+            x_raw[1, h] = piece[:]
+
+        cb_col = keep.tile([P, J_PASSES, PACK], F32, name="cb_col")
+        nc.sync.dma_start(out=cb_col[:], in_=cb.rearrange("(a p i) -> p a i", p=P, i=PACK))
+        cw_col = keep.tile([P, J_PASSES, PACK], F32, name="cw_col")
+        nc.sync.dma_start(out=cw_col[:], in_=cw.rearrange("(a p i) -> p a i", p=P, i=PACK))
+
+        warm = keep.tile([P, 8], F32, name="warm")
+        nc.vector.memset(warm[:], 0.0)
+        warm_out = keep.tile([P, 8], F32, name="warm_out")
+        nc.scalar.activation(warm_out[:], warm[:], TANH)
+
+        nc.vector.memset(scale_table[32:64, :].bitcast(I32), 0)
+        nc.vector.memset(scale_table[64:128, :].bitcast(I32), 0)
+        tab_planes = keep.tile([P, K_PASSES, J], U8, name="tab_planes", align_bytes=64)
+        nc.vector.memset(tab_planes[:].rearrange("p d j -> p (d j)").bitcast(I32), 0)
+
+        picked_scales = keep.tile([P, J], U8, name="picked_scales", tag="before_al_scales", align_bytes=64)
+        nc.vector.tensor_copy(picked_scales[:], scale_table[:].indirect(offsets[:]))
+        sorted_scales = keep.tile([P, J], U8, name="sorted_scales", tag="before_al_words", align_bytes=64)
+        nc.vector.tensor_copy(
+            sorted_scales[:].rearrange("p (a i q) -> p a i q", a=J_PASSES, i=PACK),
+            picked_scales[:].rearrange("p (a q i) -> p a i q", a=J_PASSES, i=PACK),
+        )
+        for quad in range(4):
+            nc.sync.dma_start(
+                out=tab_planes[32 * quad : 32 * quad + 4, :, :].bitcast(I32),
+                in_=sorted_scales[8 * quad : 8 * quad + 8, :].bitcast(I32),
+            )
+
+        al_planes = keep.tile([P, N], U8, name="al_planes", tag="before_al_scales", align_bytes=64)
+        nc.gpsimd.memset(al_planes[:].bitcast(I32), 0)
+        for quad in range(4):
+            nc.sync.dma_start(
+                out=al_planes[32 * quad : 32 * quad + 16, :].bitcast(I32),
+                in_=al_scales[:, 4 * quad : 4 * quad + 4, :].bitcast(I32),
+            )
+        al_codes = keep.tile([P, J_PASSES, N], I32, name="al_codes", tag="before_al_words", align_bytes=64)
+        nc.sync.dma_start(out=al_codes[:], in_=al_words.rearrange("a p n i -> p a (n i)").bitcast(I32))
+
+        tab_codes = [keep.tile([P, K_PASSES * 2 * PASS], U8, name="tab_codes%d" % a, align_bytes=64) for a in range(J_PASSES)]
+
+        def gather_words(picked, first):
+            for u in range(2):
+                a = first + u
+                nc.vector.tensor_copy(
+                    picked[:, u * PASS : (u + 1) * PASS],
+                    word_table[:].bitcast(U32).indirect(offsets[:, a * LIST_COLS : (a + 1) * LIST_COLS]),
+                )
+            for u in range(2):
+                nc.vector.tensor_copy(
+                    tab_codes[first + u][:].bitcast(U16).rearrange("p (d h l q) -> p d h q l", d=2, h=2, l=2),
+                    picked[:, u * PASS : (u + 1) * PASS].bitcast(U16).rearrange("p (q h l d) -> p d h q l", d=2, h=2, l=2),
+                )
+
+        picked_early = keep.tile([P, 2 * PASS], U32, name="picked_early", align_bytes=64)
+        gather_words(picked_early, 0)
+
+        x_codes = [keep.tile([P, M], U32, name="x_codes%d" % d, align_bytes=64) for d in range(K_PASSES)]
+        x_planes = [keep.tile([P, M], U8, name="x_planes%d" % d, align_bytes=64) for d in range(K_PASSES)]
+        for d in range(K_PASSES):
+            grouped = keep.tile([P, M * PACK], BF16, name="x_grouped%d" % d, tag="x_grouped%d" % d, align_bytes=64)
+            for h in range(2):
+                part = grouped[:, h * HALF * PACK : (h + 1) * HALF * PACK]
+                nc.scalar.copy(
+                    part.rearrange("p (c e i) -> p c i e", e=2, i=PACK),
+                    x_raw[d, h].rearrange("p i (c e) -> p c i e", e=2),
+                )
+                nc.vector.quantize_mx(
+                    out=x_codes[d][:, h * HALF : (h + 1) * HALF].bitcast(FP8X4),
+                    scales=x_planes[d][:, h * HALF : (h + 1) * HALF],
+                    in_=part,
+                )
+
+        picked_late = keep.tile([P, 2 * PASS], U32, name="picked_late", tag="x_grouped1", align_bytes=64)
+        gather_words(picked_late, 2)
+
+        y_acc = {(g, h): psum.tile([P, HALF], F32, name="y_acc%d%d" % (g, h)) for g in range(2) for h in range(2)}
+
+        for a in range(J_PASSES):
+            dots = [psum.tile([P, M], F32, name="dots%d_%d" % (a, i), tag="dots%d" % i) for i in range(PACK)]
+            order = [(d, i) for d in range(K_PASSES) for i in range(PACK)] if a == 0 else [(d, i) for i in range(PACK) for d in range(K_PASSES)]
+            for d, i in order:
+                col = (d * PACK + i) * 2 * P
+                nc.tensor.matmul_mx(
+                    out=dots[i][:],
+                    lhsT=tab_codes[a][:, col : col + 2 * P].bitcast(FP4X4),
+                    lhsT_scale=tab_planes[:, d, a * PASS + i * P : a * PASS + (i + 1) * P],
+                    rhs=x_codes[d][:].bitcast(FP8X4),
+                    rhs_scale=x_planes[d][:],
+                    start=(d == 0),
+                    stop=(d == K_PASSES - 1),
+                )
+            kern = keep.tile([P, PACK, M], F32, name="kern%d" % a)
+            for i in range(PACK):
+                nc.scalar.activation(kern[:, i, :], dots[i][:], TANH, bias=cb_col[:, a, i : i + 1])
+            grouped = []
+            for h in range(2):
+                h_grouped = keep.tile([P, HALF * PACK], BF16, name="h_grouped%d%d" % (a, h), align_bytes=64)
+                nc.vector.tensor_tensor(
+                    h_grouped[:].rearrange("p (c e i) -> p c i e", e=2, i=PACK),
+                    kern[:, :, h * HALF : (h + 1) * HALF].rearrange("p i (c e) -> p c i e", e=2),
+                    cw_col[:, a, :].unsqueeze(1).unsqueeze(3).to_broadcast([P, HALF // 2, PACK, 2]),
+                    MULT,
+                )
+                grouped.append(h_grouped)
+            for h in range(2):
+                h_codes = keep.tile([P, HALF], U32, name="h_codes%d%d" % (a, h), align_bytes=64)
+                h_plane = keep.tile([P, HALF], U8, name="h_plane%d%d" % (a, h), align_bytes=64)
+                nc.vector.quantize_mx(out=h_codes[:].bitcast(FP8X4), scales=h_plane[:], in_=grouped[h][:])
+                for g in range(2):
+                    nc.tensor.matmul_mx(
+                        out=y_acc[g, h][:],
+                        lhsT=al_codes[:, a, g * P : (g + 1) * P].bitcast(FP8X4),
+                        lhsT_scale=al_planes[4 * a : P, g * P : (g + 1) * P],
+                        rhs=h_codes[:].bitcast(FP8X4),
+                        rhs_scale=h_plane[:],
+                        start=(a == 0),
+                        stop=(a == J_PASSES - 1),
+                    )
+
+        for h in range(2):
+            for g in range(2):
+                result = keep.tile([P, HALF], F32, name="result%d%d" % (g, h))
+                if h == 1 and g == 1:
+                    nc.vector.tensor_copy(result[:], y_acc[g, h][:])
+                else:
+                    nc.scalar.copy(result[:], y_acc[g, h][:])
+                nc.sync.dma_start(out=out[g * P : (g + 1) * P, h * HALF : (h + 1) * HALF], in_=result[:])

@@ -14,6 +14,8 @@ U8 = mybir.dt.uint8
 FP8X4 = mybir.dt.float8_e4m3fn_x4
 FP4X4 = mybir.dt.float4_e2m1fn_x4
 TANH = mybir.ActivationFunctionType.Tanh
+COPY = mybir.ActivationFunctionType.Copy
+ASSISTED = [(3, 0), (3, 1)]
 MULT = mybir.AluOpType.mult
 
 P = 128
@@ -36,62 +38,79 @@ def tile_list_kernl_tanh_none_kernel(
         offsets = keep.tile([P, J // 16], U16, name="offsets")
         nc.sync.dma_start(offsets[:], offs)
 
-        scale_table = keep.tile([P, T], U8, name="scale_table", align_bytes=64)
+        scale_table = keep.tile([P, T], U8, name="scale_table", tag="scale_table", align_bytes=64)
         nc.sync.dma_start(
             out=scale_table[0:32, :].bitcast(I32),
             in_=tab_scales.bitcast(I32).rearrange("d q w -> q d w"),
         )
+        x_rows = x.rearrange("(d p i) m -> d p i m", p=P, i=PACK)
+        x_first = keep.tile([P, PACK, HALF], F32, name="x_first")
+        nc.sync.dma_start(out=x_first[:], in_=x_rows[0][:, :, 0:HALF])
         word_table = keep.tile([P, T], I32, name="word_table", align_bytes=64)
         nc.sync.dma_start(out=word_table[:], in_=tab_words[0].rearrange("p t b -> p (t b)").bitcast(I32))
-
-        x_rows = x.rearrange("(d p i) m -> d p i m", p=P, i=PACK)
-        x_first = keep.tile([P, PACK, M], F32, name="x_first")
-        nc.sync.dma_start(out=x_first[:], in_=x_rows[0])
-        x_raw = {(0, h): x_first[:, :, h * HALF : (h + 1) * HALF] for h in range(2)}
-        for h in range(2):
-            piece = keep.tile([P, PACK, HALF], F32, name="x_second%d" % h)
-            nc.sync.dma_start(out=piece[:], in_=x_rows[1][:, :, h * HALF : (h + 1) * HALF])
-            x_raw[1, h] = piece[:]
-
-        cb_col = keep.tile([P, J_PASSES, PACK], F32, name="cb_col")
-        nc.sync.dma_start(out=cb_col[:], in_=cb.rearrange("(a p i) -> p a i", p=P, i=PACK))
-        cw_col = keep.tile([P, J_PASSES, PACK], F32, name="cw_col")
-        nc.sync.dma_start(out=cw_col[:], in_=cw.rearrange("(a p i) -> p a i", p=P, i=PACK))
+        x_raw = {(0, 0): x_first[:]}
 
         warm = keep.tile([P, 8], F32, name="warm")
         nc.vector.memset(warm[:], 0.0)
         warm_out = keep.tile([P, 8], F32, name="warm_out")
         nc.scalar.activation(warm_out[:], warm[:], TANH)
 
-        nc.vector.memset(scale_table[32:64, :].bitcast(I32), 0)
+        nc.gpsimd.memset(scale_table[32:64, :].bitcast(I32), 0)
         nc.vector.memset(scale_table[64:128, :].bitcast(I32), 0)
-        tab_planes = keep.tile([P, K_PASSES, J], U8, name="tab_planes", align_bytes=64)
-        nc.vector.memset(tab_planes[:].rearrange("p d j -> p (d j)").bitcast(I32), 0)
+        tab_planes = [keep.tile([P, K_PASSES, J // 2], U8, name="tab_planes%d" % u, align_bytes=64) for u in range(2)]
+        for u in range(2):
+            nc.gpsimd.memset(tab_planes[u][:].rearrange("p d j -> p (d j)").bitcast(I32), 0)
 
-        picked_scales = keep.tile([P, J], U8, name="picked_scales", tag="before_al_scales", align_bytes=64)
-        nc.vector.tensor_copy(picked_scales[:], scale_table[:].indirect(offsets[:]))
-        sorted_scales = keep.tile([P, J], U8, name="sorted_scales", tag="before_al_words", align_bytes=64)
-        nc.vector.tensor_copy(
-            sorted_scales[:].rearrange("p (a i q) -> p a i q", a=J_PASSES, i=PACK),
-            picked_scales[:].rearrange("p (a q i) -> p a i q", a=J_PASSES, i=PACK),
-        )
-        for quad in range(4):
-            nc.sync.dma_start(
-                out=tab_planes[32 * quad : 32 * quad + 4, :, :].bitcast(I32),
-                in_=sorted_scales[8 * quad : 8 * quad + 8, :].bitcast(I32),
+        sorted_scales = [keep.tile([P, J // 2], U8, name="sorted_scales%d" % u, tag="sorted_scales%d" % u, align_bytes=64) for u in range(2)]
+
+        def pick_scales(name, tag, first, count):
+            picked = keep.tile([P, count * PASS], U8, name=name, tag=tag, align_bytes=64)
+            nc.vector.tensor_copy(
+                picked[:], scale_table[:].indirect(offsets[:, first * LIST_COLS : (first + count) * LIST_COLS])
+            )
+            return picked
+
+        def sort_scales(dst, picked):
+            nc.vector.tensor_copy(
+                dst.rearrange("p (a i q) -> p a i q", i=PACK, q=P),
+                picked[:].rearrange("p (a q i) -> p a i q", i=PACK, q=P),
             )
 
-        al_planes = keep.tile([P, N], U8, name="al_planes", tag="before_al_scales", align_bytes=64)
-        nc.gpsimd.memset(al_planes[:].bitcast(I32), 0)
+        early = [pick_scales("picked_scales%d" % a, "picked_scales%d" % a, a, 1) for a in range(2)]
+        for a in range(2):
+            sort_scales(sorted_scales[0][:, a * PASS : (a + 1) * PASS], early[a])
+        late = pick_scales("picked_scales_late", "picked_scales0", 2, 2)
+        sort_scales(sorted_scales[1][:], late)
+
+        def place_scales(u):
+            for quad in range(4):
+                nc.sync.dma_start(
+                    out=tab_planes[u][32 * quad : 32 * quad + 4, :, :].bitcast(I32),
+                    in_=sorted_scales[u][8 * quad : 8 * quad + 8, :].bitcast(I32),
+                )
+
+        place_scales(0)
+        x_rest = keep.tile([P, 3, PACK, HALF], F32, name="x_rest", tag="picked_scales1", align_bytes=64)
+        for n, (d, h) in enumerate([(0, 1), (1, 0), (1, 1)]):
+            nc.sync.dma_start(out=x_rest[:, n, :, :], in_=x_rows[d][:, :, h * HALF : (h + 1) * HALF])
+            x_raw[d, h] = x_rest[:, n, :, :]
+        cb_col = keep.tile([P, J_PASSES, PACK], F32, name="cb_col", tag="scale_table", align_bytes=64)
+        nc.sync.dma_start(out=cb_col[:], in_=cb.rearrange("(a p i) -> p a i", p=P, i=PACK))
+        place_scales(1)
+
+        al_planes = keep.tile([P, N], U8, name="al_planes", tag="picked_scales0", align_bytes=64)
+        nc.vector.memset(al_planes[:].bitcast(I32), 0)
         for quad in range(4):
             nc.sync.dma_start(
                 out=al_planes[32 * quad : 32 * quad + 16, :].bitcast(I32),
                 in_=al_scales[:, 4 * quad : 4 * quad + 4, :].bitcast(I32),
             )
-        al_codes = keep.tile([P, J_PASSES, N], I32, name="al_codes", tag="before_al_words", align_bytes=64)
+        cw_col = keep.tile([P, J_PASSES, PACK], F32, name="cw_col", tag="sorted_scales0", align_bytes=64)
+        nc.sync.dma_start(out=cw_col[:], in_=cw.rearrange("(a p i) -> p a i", p=P, i=PACK))
+        al_codes = keep.tile([P, J_PASSES, N], I32, name="al_codes", tag="sorted_scales1", align_bytes=64)
         nc.sync.dma_start(out=al_codes[:], in_=al_words.rearrange("a p n i -> p a (n i)").bitcast(I32))
 
-        tab_codes = [keep.tile([P, K_PASSES * 2 * PASS], U8, name="tab_codes%d" % a, align_bytes=64) for a in range(J_PASSES)]
+        tab_codes = {}
 
         def gather_words(picked, first):
             for u in range(2):
@@ -100,11 +119,13 @@ def tile_list_kernl_tanh_none_kernel(
                     picked[:, u * PASS : (u + 1) * PASS],
                     word_table[:].bitcast(U32).indirect(offsets[:, a * LIST_COLS : (a + 1) * LIST_COLS]),
                 )
-            for u in range(2):
-                nc.vector.tensor_copy(
-                    tab_codes[first + u][:].bitcast(U16).rearrange("p (d h l q) -> p d h q l", d=2, h=2, l=2),
-                    picked[:, u * PASS : (u + 1) * PASS].bitcast(U16).rearrange("p (q h l d) -> p d h q l", d=2, h=2, l=2),
-                )
+
+        def part_words(picked, a, tag):
+            tab_codes[a] = keep.tile([P, K_PASSES * 2 * PASS], U8, name="tab_codes%d" % a, tag=tag, align_bytes=64)
+            nc.vector.tensor_copy(
+                tab_codes[a][:].bitcast(U16).rearrange("p (d h l q) -> p d h q l", d=2, h=2, l=2),
+                picked[:, (a % 2) * PASS : (a % 2 + 1) * PASS].bitcast(U16).rearrange("p (q h l d) -> p d h q l", d=2, h=2, l=2),
+            )
 
         picked_early = keep.tile([P, 2 * PASS], U32, name="picked_early", align_bytes=64)
         gather_words(picked_early, 0)
@@ -112,9 +133,9 @@ def tile_list_kernl_tanh_none_kernel(
         x_codes = [keep.tile([P, M], U32, name="x_codes%d" % d, align_bytes=64) for d in range(K_PASSES)]
         x_planes = [keep.tile([P, M], U8, name="x_planes%d" % d, align_bytes=64) for d in range(K_PASSES)]
         for d in range(K_PASSES):
-            grouped = keep.tile([P, M * PACK], BF16, name="x_grouped%d" % d, tag="x_grouped%d" % d, align_bytes=64)
             for h in range(2):
-                part = grouped[:, h * HALF * PACK : (h + 1) * HALF * PACK]
+                grouped = keep.tile([P, HALF * PACK], BF16, name="x_grouped%d%d" % (d, h), tag="x_grouped%d%d" % (d, h), align_bytes=64)
+                part = grouped[:]
                 nc.scalar.copy(
                     part.rearrange("p (c e i) -> p c i e", e=2, i=PACK),
                     x_raw[d, h].rearrange("p i (c e) -> p c i e", e=2),
@@ -125,24 +146,30 @@ def tile_list_kernl_tanh_none_kernel(
                     in_=part,
                 )
 
-        picked_late = keep.tile([P, 2 * PASS], U32, name="picked_late", tag="x_grouped1", align_bytes=64)
+        part_words(picked_early, 0, "x_grouped01")
+        part_words(picked_early, 1, "x_grouped10")
+        picked_late = keep.tile([P, 2 * PASS], U32, name="picked_late", tag="x_grouped11", align_bytes=64)
         gather_words(picked_late, 2)
+        part_words(picked_late, 2, "tab_codes2")
+        part_words(picked_late, 3, "tab_codes3")
 
         y_acc = {(g, h): psum.tile([P, HALF], F32, name="y_acc%d%d" % (g, h)) for g in range(2) for h in range(2)}
 
         for a in range(J_PASSES):
             dots = [psum.tile([P, M], F32, name="dots%d_%d" % (a, i), tag="dots%d" % i) for i in range(PACK)]
-            order = [(d, i) for d in range(K_PASSES) for i in range(PACK)] if a == 0 else [(d, i) for i in range(PACK) for d in range(K_PASSES)]
-            for d, i in order:
+            order = [(d, i, d) for i in range(PACK) for d in range(K_PASSES)]
+            if a == 0:
+                order = [(0, 0, 0), (0, 1, 0), (1, 0, 1), (1, 1, 1), (1, 2, 0), (0, 2, 1), (1, 3, 0), (0, 3, 1)]
+            for d, i, step in order:
                 col = (d * PACK + i) * 2 * P
                 nc.tensor.matmul_mx(
                     out=dots[i][:],
                     lhsT=tab_codes[a][:, col : col + 2 * P].bitcast(FP4X4),
-                    lhsT_scale=tab_planes[:, d, a * PASS + i * P : a * PASS + (i + 1) * P],
+                    lhsT_scale=tab_planes[a // 2][:, d, (a % 2) * PASS + i * P : (a % 2) * PASS + (i + 1) * P],
                     rhs=x_codes[d][:].bitcast(FP8X4),
                     rhs_scale=x_planes[d][:],
-                    start=(d == 0),
-                    stop=(d == K_PASSES - 1),
+                    start=(step == 0),
+                    stop=(step == K_PASSES - 1),
                 )
             kern = keep.tile([P, PACK, M], F32, name="kern%d" % a)
             for i in range(PACK):
@@ -150,12 +177,23 @@ def tile_list_kernl_tanh_none_kernel(
             grouped = []
             for h in range(2):
                 h_grouped = keep.tile([P, HALF * PACK], BF16, name="h_grouped%d%d" % (a, h), align_bytes=64)
-                nc.vector.tensor_tensor(
-                    h_grouped[:].rearrange("p (c e i) -> p c i e", e=2, i=PACK),
-                    kern[:, :, h * HALF : (h + 1) * HALF].rearrange("p i (c e) -> p c i e", e=2),
-                    cw_col[:, a, :].unsqueeze(1).unsqueeze(3).to_broadcast([P, HALF // 2, PACK, 2]),
-                    MULT,
-                )
+                if (a, h) in ASSISTED:
+                    rounded = keep.tile([P, PACK, HALF], BF16, name="rounded%d%d" % (a, h))
+                    for i in range(PACK):
+                        nc.scalar.activation(
+                            rounded[:, i, :], kern[:, i, h * HALF : (h + 1) * HALF], COPY, scale=cw_col[:, a, i : i + 1]
+                        )
+                    nc.vector.tensor_copy(
+                        h_grouped[:].rearrange("p (c e i) -> p c i e", e=4, i=PACK),
+                        rounded[:].rearrange("p i (c e) -> p c i e", e=4),
+                    )
+                else:
+                    nc.vector.tensor_tensor(
+                        h_grouped[:].rearrange("p (c e i) -> p c i e", e=2, i=PACK),
+                        kern[:, :, h * HALF : (h + 1) * HALF].rearrange("p i (c e) -> p c i e", e=2),
+                        cw_col[:, a, :].unsqueeze(1).unsqueeze(3).to_broadcast([P, HALF // 2, PACK, 2]),
+                        MULT,
+                    )
                 grouped.append(h_grouped)
             for h in range(2):
                 h_codes = keep.tile([P, HALF], U32, name="h_codes%d%d" % (a, h), align_bytes=64)

@@ -15,7 +15,7 @@ FP8X4 = mybir.dt.float8_e4m3fn_x4
 FP4X4 = mybir.dt.float4_e2m1fn_x4
 TANH = mybir.ActivationFunctionType.Tanh
 COPY = mybir.ActivationFunctionType.Copy
-ASSISTED = [(3, 0), (3, 1)]
+ASSISTED = {(3, 0): 128, (3, 1): 256}
 MULT = mybir.AluOpType.mult
 
 P = 128
@@ -55,13 +55,14 @@ def tile_list_kernl_tanh_none_kernel(
         warm_out = keep.tile([P, 8], F32, name="warm_out")
         nc.scalar.activation(warm_out[:], warm[:], TANH)
 
-        nc.gpsimd.memset(scale_table[32:64, :].bitcast(I32), 0)
+        nc.vector.memset(scale_table[32:64, :].bitcast(I32), 0)
         nc.vector.memset(scale_table[64:128, :].bitcast(I32), 0)
-        tab_planes = [keep.tile([P, K_PASSES, J // 2], U8, name="tab_planes%d" % u, align_bytes=64) for u in range(2)]
+        widths = [PASS, J - PASS]
+        tab_planes = [keep.tile([P, K_PASSES, widths[u]], U8, name="tab_planes%d" % u, align_bytes=64) for u in range(2)]
         for u in range(2):
             nc.gpsimd.memset(tab_planes[u][:].rearrange("p d j -> p (d j)").bitcast(I32), 0)
 
-        sorted_scales = [keep.tile([P, J // 2], U8, name="sorted_scales%d" % u, tag="sorted_scales%d" % u, align_bytes=64) for u in range(2)]
+        sorted_scales = [keep.tile([P, widths[u]], U8, name="sorted_scales%d" % u, tag="sorted_scales%d" % u, align_bytes=64) for u in range(2)]
 
         def pick_scales(name, tag, first, count):
             picked = keep.tile([P, count * PASS], U8, name=name, tag=tag, align_bytes=64)
@@ -77,10 +78,10 @@ def tile_list_kernl_tanh_none_kernel(
             )
 
         early = [pick_scales("picked_scales%d" % a, "picked_scales%d" % a, a, 1) for a in range(2)]
-        for a in range(2):
-            sort_scales(sorted_scales[0][:, a * PASS : (a + 1) * PASS], early[a])
+        sort_scales(sorted_scales[0][:], early[0])
+        sort_scales(sorted_scales[1][:, 0:PASS], early[1])
         late = pick_scales("picked_scales_late", "picked_scales0", 2, 2)
-        sort_scales(sorted_scales[1][:], late)
+        sort_scales(sorted_scales[1][:, PASS:], late)
 
         def place_scales(u):
             for quad in range(4):
@@ -122,10 +123,10 @@ def tile_list_kernl_tanh_none_kernel(
 
         def part_words(picked, a, tag):
             tab_codes[a] = keep.tile([P, K_PASSES * 2 * PASS], U8, name="tab_codes%d" % a, tag=tag, align_bytes=64)
-            nc.vector.tensor_copy(
-                tab_codes[a][:].bitcast(U16).rearrange("p (d h l q) -> p d h q l", d=2, h=2, l=2),
-                picked[:, (a % 2) * PASS : (a % 2 + 1) * PASS].bitcast(U16).rearrange("p (q h l d) -> p d h q l", d=2, h=2, l=2),
-            )
+            dst = tab_codes[a][:].bitcast(U16).rearrange("p (d h l u q) -> p d u h q l", d=2, h=2, l=2, u=2)
+            src = picked[:, (a % 2) * PASS : (a % 2 + 1) * PASS].bitcast(U16).rearrange("p (u q h l d) -> p d u h q l", d=2, h=2, l=2, u=2)
+            for d in range(K_PASSES):
+                nc.vector.tensor_copy(dst[:, d], src[:, d])
 
         picked_early = keep.tile([P, 2 * PASS], U32, name="picked_early", align_bytes=64)
         gather_words(picked_early, 0)
@@ -137,8 +138,8 @@ def tile_list_kernl_tanh_none_kernel(
                 grouped = keep.tile([P, HALF * PACK], BF16, name="x_grouped%d%d" % (d, h), tag="x_grouped%d%d" % (d, h), align_bytes=64)
                 part = grouped[:]
                 nc.scalar.copy(
-                    part.rearrange("p (c e i) -> p c i e", e=2, i=PACK),
-                    x_raw[d, h].rearrange("p i (c e) -> p c i e", e=2),
+                    part.rearrange("p (c e i) -> p c i e", e=4, i=PACK),
+                    x_raw[d, h].rearrange("p i (c e) -> p c i e", e=4),
                 )
                 nc.vector.quantize_mx(
                     out=x_codes[d][:, h * HALF : (h + 1) * HALF].bitcast(FP8X4),
@@ -165,7 +166,7 @@ def tile_list_kernl_tanh_none_kernel(
                 nc.tensor.matmul_mx(
                     out=dots[i][:],
                     lhsT=tab_codes[a][:, col : col + 2 * P].bitcast(FP4X4),
-                    lhsT_scale=tab_planes[a // 2][:, d, (a % 2) * PASS + i * P : (a % 2) * PASS + (i + 1) * P],
+                    lhsT_scale=tab_planes[min(a, 1)][:, d, max(a - 1, 0) * PASS + i * P : max(a - 1, 0) * PASS + (i + 1) * P],
                     rhs=x_codes[d][:].bitcast(FP8X4),
                     rhs_scale=x_planes[d][:],
                     start=(step == 0),
@@ -177,22 +178,23 @@ def tile_list_kernl_tanh_none_kernel(
             grouped = []
             for h in range(2):
                 h_grouped = keep.tile([P, HALF * PACK], BF16, name="h_grouped%d%d" % (a, h), align_bytes=64)
-                if (a, h) in ASSISTED:
-                    rounded = keep.tile([P, PACK, HALF], BF16, name="rounded%d%d" % (a, h))
+                own = HALF - ASSISTED.get((a, h), 0)
+                if own > 0:
+                    nc.vector.tensor_tensor(
+                        h_grouped[:, 0 : own * PACK].rearrange("p (c e i) -> p c i e", e=4, i=PACK),
+                        kern[:, :, h * HALF : h * HALF + own].rearrange("p i (c e) -> p c i e", e=4),
+                        cw_col[:, a, :].unsqueeze(1).unsqueeze(3).to_broadcast([P, own // 4, PACK, 4]),
+                        MULT,
+                    )
+                if own < HALF:
+                    rounded = keep.tile([P, PACK, HALF - own], BF16, name="rounded%d%d" % (a, h))
                     for i in range(PACK):
                         nc.scalar.activation(
-                            rounded[:, i, :], kern[:, i, h * HALF : (h + 1) * HALF], COPY, scale=cw_col[:, a, i : i + 1]
+                            rounded[:, i, :], kern[:, i, h * HALF + own : (h + 1) * HALF], COPY, scale=cw_col[:, a, i : i + 1]
                         )
                     nc.vector.tensor_copy(
-                        h_grouped[:].rearrange("p (c e i) -> p c i e", e=4, i=PACK),
+                        h_grouped[:, own * PACK :].rearrange("p (c e i) -> p c i e", e=4, i=PACK),
                         rounded[:].rearrange("p i (c e) -> p c i e", e=4),
-                    )
-                else:
-                    nc.vector.tensor_tensor(
-                        h_grouped[:].rearrange("p (c e i) -> p c i e", e=2, i=PACK),
-                        kern[:, :, h * HALF : (h + 1) * HALF].rearrange("p i (c e) -> p c i e", e=2),
-                        cw_col[:, a, :].unsqueeze(1).unsqueeze(3).to_broadcast([P, HALF // 2, PACK, 2]),
-                        MULT,
                     )
                 grouped.append(h_grouped)
             for h in range(2):
@@ -217,4 +219,5 @@ def tile_list_kernl_tanh_none_kernel(
                     nc.vector.tensor_copy(result[:], y_acc[g, h][:])
                 else:
                     nc.scalar.copy(result[:], y_acc[g, h][:])
-                nc.sync.dma_start(out=out[g * P : (g + 1) * P, h * HALF : (h + 1) * HALF], in_=result[:])
+                queue = nc.scalar if (h == 1 and g == 0) else nc.sync
+                queue.dma_start(out=out[g * P : (g + 1) * P, h * HALF : (h + 1) * HALF], in_=result[:])

@@ -15,7 +15,7 @@ FP8X4 = mybir.dt.float8_e4m3fn_x4
 FP4X4 = mybir.dt.float4_e2m1fn_x4
 TANH = mybir.ActivationFunctionType.Tanh
 COPY = mybir.ActivationFunctionType.Copy
-ASSISTED = {(3, 0): 128, (3, 1): 256}
+ASSISTED = {(3, 0): 256, (3, 1): 256}
 MULT = mybir.AluOpType.mult
 
 P = 128
@@ -44,11 +44,11 @@ def tile_list_kernl_tanh_none_kernel(
             in_=tab_scales.bitcast(I32).rearrange("d q w -> q d w"),
         )
         x_rows = x.rearrange("(d p i) m -> d p i m", p=P, i=PACK)
-        x_first = keep.tile([P, PACK, HALF], F32, name="x_first")
-        nc.sync.dma_start(out=x_first[:], in_=x_rows[0][:, :, 0:HALF])
         word_table = keep.tile([P, T], I32, name="word_table", align_bytes=64)
         nc.sync.dma_start(out=word_table[:], in_=tab_words[0].rearrange("p t b -> p (t b)").bitcast(I32))
-        x_raw = {(0, 0): x_first[:]}
+        x_first = keep.tile([P, PACK, M], F32, name="x_first", tag="x_first", align_bytes=64)
+        nc.sync.dma_start(out=x_first[:], in_=x_rows[0])
+        x_raw = {(0, h): x_first[:, :, h * HALF : (h + 1) * HALF] for h in range(2)}
 
         warm = keep.tile([P, 8], F32, name="warm")
         nc.vector.memset(warm[:], 0.0)
@@ -74,14 +74,20 @@ def tile_list_kernl_tanh_none_kernel(
         def sort_scales(dst, picked):
             nc.vector.tensor_copy(
                 dst.rearrange("p (a i q) -> p a i q", i=PACK, q=P),
-                picked[:].rearrange("p (a q i) -> p a i q", i=PACK, q=P),
+                picked.rearrange("p (a q i) -> p a i q", i=PACK, q=P),
             )
 
         early = [pick_scales("picked_scales%d" % a, "picked_scales%d" % a, a, 1) for a in range(2)]
-        sort_scales(sorted_scales[0][:], early[0])
-        sort_scales(sorted_scales[1][:, 0:PASS], early[1])
-        late = pick_scales("picked_scales_late", "picked_scales0", 2, 2)
-        sort_scales(sorted_scales[1][:, PASS:], late)
+        sort_scales(sorted_scales[0][:], early[0][:])
+        sort_scales(sorted_scales[1][:, 0:PASS], early[1][:])
+        late = keep.tile([P, 2 * PASS], U8, name="picked_scales_late", tag="picked_scales0", align_bytes=64)
+        for a in (2, 3):
+            nc.vector.tensor_copy(
+                late[:, (a - 2) * PASS : (a - 1) * PASS],
+                scale_table[:].indirect(offsets[:, a * LIST_COLS : (a + 1) * LIST_COLS]),
+            )
+        for a in (2, 3):
+            sort_scales(sorted_scales[1][:, (a - 1) * PASS : a * PASS], late[:, (a - 2) * PASS : (a - 1) * PASS])
 
         def place_scales(u):
             for quad in range(4):
@@ -91,16 +97,16 @@ def tile_list_kernl_tanh_none_kernel(
                 )
 
         place_scales(0)
-        x_rest = keep.tile([P, 3, PACK, HALF], F32, name="x_rest", tag="picked_scales1", align_bytes=64)
-        for n, (d, h) in enumerate([(0, 1), (1, 0), (1, 1)]):
-            nc.sync.dma_start(out=x_rest[:, n, :, :], in_=x_rows[d][:, :, h * HALF : (h + 1) * HALF])
-            x_raw[d, h] = x_rest[:, n, :, :]
+        x_second = keep.tile([P, PACK, M], F32, name="x_second", tag="picked_scales1", align_bytes=64)
+        nc.sync.dma_start(out=x_second[:], in_=x_rows[1])
+        for h in range(2):
+            x_raw[1, h] = x_second[:, :, h * HALF : (h + 1) * HALF]
         cb_col = keep.tile([P, J_PASSES, PACK], F32, name="cb_col", tag="scale_table", align_bytes=64)
         nc.sync.dma_start(out=cb_col[:], in_=cb.rearrange("(a p i) -> p a i", p=P, i=PACK))
         place_scales(1)
 
         al_planes = keep.tile([P, N], U8, name="al_planes", tag="picked_scales0", align_bytes=64)
-        nc.vector.memset(al_planes[:].bitcast(I32), 0)
+        nc.gpsimd.memset(al_planes[:].bitcast(I32), 0)
         for quad in range(4):
             nc.sync.dma_start(
                 out=al_planes[32 * quad : 32 * quad + 16, :].bitcast(I32),
@@ -113,23 +119,25 @@ def tile_list_kernl_tanh_none_kernel(
 
         tab_codes = {}
 
-        def gather_words(picked, first):
-            for u in range(2):
-                a = first + u
-                nc.vector.tensor_copy(
-                    picked[:, u * PASS : (u + 1) * PASS],
-                    word_table[:].bitcast(U32).indirect(offsets[:, a * LIST_COLS : (a + 1) * LIST_COLS]),
-                )
+        picked_words = {}
 
-        def part_words(picked, a, tag):
+        def gather_words(a, tag):
+            picked_words[a] = keep.tile([P, PASS], U32, name="picked_words%d" % a, tag=tag, align_bytes=64)
+            nc.vector.tensor_copy(
+                picked_words[a][:],
+                word_table[:].bitcast(U32).indirect(offsets[:, a * LIST_COLS : (a + 1) * LIST_COLS]),
+            )
+
+        def part_words(a, tag):
             tab_codes[a] = keep.tile([P, K_PASSES * 2 * PASS], U8, name="tab_codes%d" % a, tag=tag, align_bytes=64)
-            dst = tab_codes[a][:].bitcast(U16).rearrange("p (d h l u q) -> p d u h q l", d=2, h=2, l=2, u=2)
-            src = picked[:, (a % 2) * PASS : (a % 2 + 1) * PASS].bitcast(U16).rearrange("p (u q h l d) -> p d u h q l", d=2, h=2, l=2, u=2)
-            for d in range(K_PASSES):
-                nc.vector.tensor_copy(dst[:, d], src[:, d])
+            nc.vector.tensor_copy(
+                tab_codes[a][:].bitcast(U16).rearrange("p (d h l q) -> p d h q l", d=2, h=2, l=2),
+                picked_words[a][:].bitcast(U16).rearrange("p (q h l d) -> p d h q l", d=2, h=2, l=2),
+            )
 
-        picked_early = keep.tile([P, 2 * PASS], U32, name="picked_early", align_bytes=64)
-        gather_words(picked_early, 0)
+        gather_words(0, "picked_words0")
+        gather_words(1, "picked_words1")
+        part_words(0, "tab_codes0")
 
         x_codes = [keep.tile([P, M], U32, name="x_codes%d" % d, align_bytes=64) for d in range(K_PASSES)]
         x_planes = [keep.tile([P, M], U8, name="x_planes%d" % d, align_bytes=64) for d in range(K_PASSES)]
@@ -147,12 +155,11 @@ def tile_list_kernl_tanh_none_kernel(
                     in_=part,
                 )
 
-        part_words(picked_early, 0, "x_grouped01")
-        part_words(picked_early, 1, "x_grouped10")
-        picked_late = keep.tile([P, 2 * PASS], U32, name="picked_late", tag="x_grouped11", align_bytes=64)
-        gather_words(picked_late, 2)
-        part_words(picked_late, 2, "tab_codes2")
-        part_words(picked_late, 3, "tab_codes3")
+        gather_words(2, "x_first")
+        part_words(1, "x_grouped01")
+        part_words(2, "picked_scales1")
+        gather_words(3, "x_grouped11")
+        part_words(3, "tab_codes3")
 
         y_acc = {(g, h): psum.tile([P, HALF], F32, name="y_acc%d%d" % (g, h)) for g in range(2) for h in range(2)}
 

@@ -15,7 +15,6 @@ FP8X4 = mybir.dt.float8_e4m3fn_x4
 FP4X4 = mybir.dt.float4_e2m1fn_x4
 TANH = mybir.ActivationFunctionType.Tanh
 COPY = mybir.ActivationFunctionType.Copy
-ASSISTED = {(3, 0): 256, (3, 1): 256}
 MULT = mybir.AluOpType.mult
 
 P = 128
@@ -24,7 +23,21 @@ PASS = P * PACK
 K_PASSES = K // PASS
 J_PASSES = J // PASS
 HALF = M // 2
+QUARTER = M // 4
 LIST_COLS = PASS // 16
+SCALE_ROWS = 32
+SLOT_BYTES = 2048
+PLANE_AT = [0, 2, 0, 1]
+LATE_X = [(1, 1), (0, 2), (0, 3), (1, 2), (1, 3)]
+WEIGH_PIECES = [
+    [(0, 256, "vector"), (256, 256, "vector")],
+    [(0, 256, "vector"), (256, 256, "vector")],
+    [(0, 512, "scalar")],
+    [(0, 256, "vector"), (256, 128, "vector"), (384, 128, "vector")],
+]
+TANH_PIECES = [[(0, 256), (256, 256)], [(0, 512)], [(0, 512)], [(0, 256), (256, 256)]]
+QUANT_PIECES = [[(0, 256), (256, 256)], [(0, 256), (256, 256)], [(0, 256), (256, 256)], [(0, 256), (256, 128), (384, 128)]]
+OUT_PIECES = [(0, 256), (256, 128), (384, 128)]
 
 
 def tile_list_kernl_tanh_none_kernel(
@@ -33,198 +46,256 @@ def tile_list_kernl_tanh_none_kernel(
     nc = tc.nc
     with ExitStack() as ctx:
         keep = ctx.enter_context(tc.tile_pool(name="keep", bufs=1))
+        reused = ctx.enter_context(tc.tile_pool(name="reused", bufs=1))
         psum = ctx.enter_context(tc.psum_pool(name="psum", bufs=1))
 
+        def placed(shape, dtype, name, slot):
+            return reused.tile(shape, dtype, name=name, align_bytes=64, offset=slot * SLOT_BYTES)
+
+        def tile(shape, dtype, name, tag=None):
+            return keep.tile(shape, dtype, name=name, tag=tag or name, align_bytes=64)
+
+        def interleaved(ap):
+            return ap.rearrange("p (c e i) -> p c i e", e=4, i=PACK)
+
+        def planes(ap):
+            return ap.rearrange("p i (c e) -> p c i e", e=4)
+
+        live = P - SCALE_ROWS
+        scale_table = tile([P, T], U8, "scale_table")
         offsets = keep.tile([P, J // 16], U16, name="offsets")
         nc.sync.dma_start(offsets[:], offs)
-
-        scale_table = keep.tile([P, T], U8, name="scale_table", tag="scale_table", align_bytes=64)
         nc.sync.dma_start(
-            out=scale_table[0:32, :].bitcast(I32),
+            out=scale_table[live:P, :].bitcast(I32),
             in_=tab_scales.bitcast(I32).rearrange("d q w -> q d w"),
         )
+
         x_rows = x.rearrange("(d p i) m -> d p i m", p=P, i=PACK)
-        word_table = keep.tile([P, T], I32, name="word_table", align_bytes=64)
+        x_raw = {}
+
+        def load_x(d, first, count, dst):
+            nc.sync.dma_start(out=dst[:], in_=x_rows[d][:, :, first * QUARTER : (first + count) * QUARTER])
+            x_raw[d, first] = dst
+
+        load_x(0, 0, 2, tile([P, PACK, HALF], F32, "x_early0"))
+        load_x(1, 0, 1, tile([P, PACK, QUARTER], F32, "x_early1"))
+        word_table = tile([P, T], I32, "word_table")
         nc.sync.dma_start(out=word_table[:], in_=tab_words[0].rearrange("p t b -> p (t b)").bitcast(I32))
-        x_first = keep.tile([P, PACK, M], F32, name="x_first", tag="x_first", align_bytes=64)
-        nc.sync.dma_start(out=x_first[:], in_=x_rows[0])
-        x_raw = {(0, h): x_first[:, :, h * HALF : (h + 1) * HALF] for h in range(2)}
 
         warm = keep.tile([P, 8], F32, name="warm")
         nc.vector.memset(warm[:], 0.0)
         warm_out = keep.tile([P, 8], F32, name="warm_out")
         nc.scalar.activation(warm_out[:], warm[:], TANH)
 
-        nc.vector.memset(scale_table[32:64, :].bitcast(I32), 0)
-        nc.vector.memset(scale_table[64:128, :].bitcast(I32), 0)
-        widths = [PASS, J - PASS]
-        tab_planes = [keep.tile([P, K_PASSES, widths[u]], U8, name="tab_planes%d" % u, align_bytes=64) for u in range(2)]
+        nc.vector.memset(scale_table[0:live, :].bitcast(I32), 0)
+        widths = [PASS, 3 * PASS]
+        tab_planes = [tile([P, K_PASSES, widths[u]], U8, "tab_planes%d" % u) for u in range(2)]
         for u in range(2):
             nc.gpsimd.memset(tab_planes[u][:].rearrange("p d j -> p (d j)").bitcast(I32), 0)
 
-        sorted_scales = [keep.tile([P, widths[u]], U8, name="sorted_scales%d" % u, tag="sorted_scales%d" % u, align_bytes=64) for u in range(2)]
+        sorted_scales = tile([P, 3 * PASS], U8, "sorted_scales")
+        picked_first = placed([P, len(LATE_X) * SLOT_BYTES], U8, "picked_first", 0)[:, 0:PASS]
+        picked_rest = tile([P, 3 * PASS], U8, "picked_rest")
 
-        def pick_scales(name, tag, first, count):
-            picked = keep.tile([P, count * PASS], U8, name=name, tag=tag, align_bytes=64)
-            nc.vector.tensor_copy(
-                picked[:], scale_table[:].indirect(offsets[:, first * LIST_COLS : (first + count) * LIST_COLS])
-            )
-            return picked
+        def pick_scales(dst, first, count):
+            nc.vector.tensor_copy(dst, scale_table[:].indirect(offsets[:, first * LIST_COLS : (first + count) * LIST_COLS]))
 
-        def sort_scales(dst, picked):
+        def sort_scales(dst, src):
             nc.vector.tensor_copy(
-                dst.rearrange("p (a i q) -> p a i q", i=PACK, q=P),
-                picked.rearrange("p (a q i) -> p a i q", i=PACK, q=P),
+                dst.rearrange("p (a i q) -> p a i q", i=PACK, q=P), src.rearrange("p (a q i) -> p a i q", i=PACK, q=P)
             )
-
-        early = [pick_scales("picked_scales%d" % a, "picked_scales%d" % a, a, 1) for a in range(2)]
-        sort_scales(sorted_scales[0][:], early[0][:])
-        sort_scales(sorted_scales[1][:, 0:PASS], early[1][:])
-        late = keep.tile([P, 2 * PASS], U8, name="picked_scales_late", tag="picked_scales0", align_bytes=64)
-        for a in (2, 3):
-            nc.vector.tensor_copy(
-                late[:, (a - 2) * PASS : (a - 1) * PASS],
-                scale_table[:].indirect(offsets[:, a * LIST_COLS : (a + 1) * LIST_COLS]),
-            )
-        for a in (2, 3):
-            sort_scales(sorted_scales[1][:, (a - 1) * PASS : a * PASS], late[:, (a - 2) * PASS : (a - 1) * PASS])
 
         def place_scales(u):
             for quad in range(4):
                 nc.sync.dma_start(
                     out=tab_planes[u][32 * quad : 32 * quad + 4, :, :].bitcast(I32),
-                    in_=sorted_scales[u][8 * quad : 8 * quad + 8, :].bitcast(I32),
+                    in_=sorted_scales[live + 8 * quad : live + 8 * quad + 8, 0 : widths[u]].bitcast(I32),
                 )
 
-        place_scales(0)
-        x_second = keep.tile([P, PACK, M], F32, name="x_second", tag="picked_scales1", align_bytes=64)
-        nc.sync.dma_start(out=x_second[:], in_=x_rows[1])
-        for h in range(2):
-            x_raw[1, h] = x_second[:, :, h * HALF : (h + 1) * HALF]
-        cb_col = keep.tile([P, J_PASSES, PACK], F32, name="cb_col", tag="scale_table", align_bytes=64)
-        nc.sync.dma_start(out=cb_col[:], in_=cb.rearrange("(a p i) -> p a i", p=P, i=PACK))
-        place_scales(1)
+        pick_scales(picked_first, 0, 1)
+        pick_scales(picked_rest[:, 0:PASS], 1, 1)
+        sort_scales(sorted_scales[:, 0:PASS], picked_first)
+        pick_scales(picked_rest[:, PASS : 3 * PASS], 2, 2)
+        sort_scales(sorted_scales[:, 2 * PASS : 3 * PASS], picked_rest[:, 0:PASS])
 
-        al_planes = keep.tile([P, N], U8, name="al_planes", tag="picked_scales0", align_bytes=64)
-        nc.gpsimd.memset(al_planes[:].bitcast(I32), 0)
-        for quad in range(4):
-            nc.sync.dma_start(
-                out=al_planes[32 * quad : 32 * quad + 16, :].bitcast(I32),
-                in_=al_scales[:, 4 * quad : 4 * quad + 4, :].bitcast(I32),
+        place_scales(0)
+        for slot, (d, c) in enumerate(LATE_X):
+            load_x(d, c, 1, placed([P, PACK, QUARTER], F32, "x_late%d%d" % (d, c), slot))
+        cb_col = tile([P, J_PASSES, PACK], F32, "cb_col", tag="scale_table")
+        nc.sync.dma_start(out=cb_col[:], in_=cb.rearrange("(a p i) -> p a i", p=P, i=PACK))
+
+        x_codes = [tile([P, M], U32, "x_codes%d" % d) for d in range(K_PASSES)]
+        x_planes = [tile([P, M], U8, "x_planes%d" % d) for d in range(K_PASSES)]
+
+        def quantise_x(d, h, grouped):
+            nc.vector.quantize_mx(
+                out=x_codes[d][:, h * HALF : (h + 1) * HALF].bitcast(FP8X4),
+                scales=x_planes[d][:, h * HALF : (h + 1) * HALF],
+                in_=grouped[:],
             )
-        cw_col = keep.tile([P, J_PASSES, PACK], F32, name="cw_col", tag="sorted_scales0", align_bytes=64)
-        nc.sync.dma_start(out=cw_col[:], in_=cw.rearrange("(a p i) -> p a i", p=P, i=PACK))
-        al_codes = keep.tile([P, J_PASSES, N], I32, name="al_codes", tag="sorted_scales1", align_bytes=64)
-        nc.sync.dma_start(out=al_codes[:], in_=al_words.rearrange("a p n i -> p a (n i)").bitcast(I32))
+
+        def prepare_x(d, h):
+            grouped = tile([P, HALF * PACK], BF16, "x_grouped%d%d" % (d, h))
+            for (pass_, first), raw in x_raw.items():
+                if pass_ == d and first // 2 == h:
+                    at = (first % 2) * QUARTER * PACK
+                    nc.scalar.copy(interleaved(grouped[:, at : at + raw.shape[2] * PACK]), planes(raw[:]))
+            quantise_x(d, h, grouped)
+
+        prepare_x(0, 0)
 
         tab_codes = {}
-
         picked_words = {}
 
-        def gather_words(a, tag):
-            picked_words[a] = keep.tile([P, PASS], U32, name="picked_words%d" % a, tag=tag, align_bytes=64)
+        def gather_words(a, dst):
+            picked_words[a] = dst
             nc.vector.tensor_copy(
                 picked_words[a][:],
                 word_table[:].bitcast(U32).indirect(offsets[:, a * LIST_COLS : (a + 1) * LIST_COLS]),
             )
 
-        def part_words(a, tag):
-            tab_codes[a] = keep.tile([P, K_PASSES * 2 * PASS], U8, name="tab_codes%d" % a, tag=tag, align_bytes=64)
+        def part_words(a, dst):
+            tab_codes[a] = dst
             nc.vector.tensor_copy(
                 tab_codes[a][:].bitcast(U16).rearrange("p (d h l q) -> p d h q l", d=2, h=2, l=2),
                 picked_words[a][:].bitcast(U16).rearrange("p (q h l d) -> p d h q l", d=2, h=2, l=2),
             )
 
-        gather_words(0, "picked_words0")
-        gather_words(1, "picked_words1")
-        part_words(0, "tab_codes0")
+        words_shape, codes_shape = [P, PASS], [P, K_PASSES * 2 * PASS]
+        gather_words(0, tile(words_shape, U32, "picked_words0"))
+        part_words(0, tile(codes_shape, U8, "tab_codes0"))
+        prepare_x(1, 0)
+        sort_scales(sorted_scales[:, 0 : 2 * PASS], picked_rest[:, PASS : 3 * PASS])
+        place_scales(1)
+        cw_col = tile([P, J_PASSES, PACK], F32, "cw_col", tag="picked_rest")
+        nc.sync.dma_start(out=cw_col[:], in_=cw.rearrange("(a p i) -> p a i", p=P, i=PACK))
+        prepare_x(0, 1)
+        gather_words(1, placed(words_shape, U32, "picked_words1", LATE_X.index((0, 3))))
+        prepare_x(1, 1)
+        part_words(1, placed(codes_shape, U8, "tab_codes1", LATE_X.index((1, 3))))
+        gather_words(2, tile(words_shape, U32, "picked_words2", tag="x_grouped11"))
+        gather_words(3, placed(words_shape, U32, "picked_words3", LATE_X.index((0, 3))))
+        part_words(2, tile(codes_shape, U8, "tab_codes2"))
+        part_words(3, tile(codes_shape, U8, "tab_codes3"))
 
-        x_codes = [keep.tile([P, M], U32, name="x_codes%d" % d, align_bytes=64) for d in range(K_PASSES)]
-        x_planes = [keep.tile([P, M], U8, name="x_planes%d" % d, align_bytes=64) for d in range(K_PASSES)]
-        for d in range(K_PASSES):
-            for h in range(2):
-                grouped = keep.tile([P, HALF * PACK], BF16, name="x_grouped%d%d" % (d, h), tag="x_grouped%d%d" % (d, h), align_bytes=64)
-                part = grouped[:]
-                nc.scalar.copy(
-                    part.rearrange("p (c e i) -> p c i e", e=4, i=PACK),
-                    x_raw[d, h].rearrange("p i (c e) -> p c i e", e=4),
-                )
-                nc.vector.quantize_mx(
-                    out=x_codes[d][:, h * HALF : (h + 1) * HALF].bitcast(FP8X4),
-                    scales=x_planes[d][:, h * HALF : (h + 1) * HALF],
-                    in_=part,
-                )
+        al_planes = sorted_scales[:, 0:N]
+        al_codes = tile([P, J_PASSES, N], I32, "al_codes", tag="x_grouped10")
+        for quad in range(4):
+            nc.sync.dma_start(
+                out=al_planes[32 * quad : 32 * quad + 16, :].bitcast(I32),
+                in_=al_scales[:, 4 * quad : 4 * quad + 4, :].bitcast(I32),
+            )
+        nc.sync.dma_start(out=al_codes[:], in_=al_words.rearrange("a p n i -> p a (n i)").bitcast(I32))
 
-        gather_words(2, "x_first")
-        part_words(1, "x_grouped01")
-        part_words(2, "picked_scales1")
-        gather_words(3, "x_grouped11")
-        part_words(3, "tab_codes3")
+        def first_product(dst, a, i, d, cols):
+            col = (d * PACK + i) * 2 * P
+            first = PLANE_AT[a] * PASS + i * P
+            nc.tensor.matmul_mx(
+                out=dst,
+                lhsT=tab_codes[a][:, col : col + 2 * P].bitcast(FP4X4),
+                lhsT_scale=tab_planes[min(a, 1)][:, d, first : first + P],
+                rhs=x_codes[d][:, cols].bitcast(FP8X4),
+                rhs_scale=x_planes[d][:, cols],
+                start=(d == 0),
+                stop=(d == K_PASSES - 1),
+            )
 
-        y_acc = {(g, h): psum.tile([P, HALF], F32, name="y_acc%d%d" % (g, h)) for g in range(2) for h in range(2)}
-
+        h_codes = [tile([P, M], U32, "h_codes%d" % a) for a in range(J_PASSES)]
+        h_planes = [tile([P, M], U8, "h_planes%d" % a) for a in range(J_PASSES)]
         for a in range(J_PASSES):
-            dots = [psum.tile([P, M], F32, name="dots%d_%d" % (a, i), tag="dots%d" % i) for i in range(PACK)]
-            order = [(d, i, d) for i in range(PACK) for d in range(K_PASSES)]
+            dots = {}
             if a == 0:
-                order = [(0, 0, 0), (0, 1, 0), (1, 0, 1), (1, 1, 1), (1, 2, 0), (0, 2, 1), (1, 3, 0), (0, 3, 1)]
-            for d, i, step in order:
-                col = (d * PACK + i) * 2 * P
-                nc.tensor.matmul_mx(
-                    out=dots[i][:],
-                    lhsT=tab_codes[a][:, col : col + 2 * P].bitcast(FP4X4),
-                    lhsT_scale=tab_planes[min(a, 1)][:, d, max(a - 1, 0) * PASS + i * P : max(a - 1, 0) * PASS + (i + 1) * P],
-                    rhs=x_codes[d][:].bitcast(FP8X4),
-                    rhs_scale=x_planes[d][:],
-                    start=(step == 0),
-                    stop=(step == K_PASSES - 1),
-                )
-            kern = keep.tile([P, PACK, M], F32, name="kern%d" % a)
-            for i in range(PACK):
-                nc.scalar.activation(kern[:, i, :], dots[i][:], TANH, bias=cb_col[:, a, i : i + 1])
-            grouped = []
-            for h in range(2):
-                h_grouped = keep.tile([P, HALF * PACK], BF16, name="h_grouped%d%d" % (a, h), align_bytes=64)
-                own = HALF - ASSISTED.get((a, h), 0)
-                if own > 0:
-                    nc.vector.tensor_tensor(
-                        h_grouped[:, 0 : own * PACK].rearrange("p (c e i) -> p c i e", e=4, i=PACK),
-                        kern[:, :, h * HALF : h * HALF + own].rearrange("p i (c e) -> p c i e", e=4),
-                        cw_col[:, a, :].unsqueeze(1).unsqueeze(3).to_broadcast([P, own // 4, PACK, 4]),
-                        MULT,
-                    )
-                if own < HALF:
-                    rounded = keep.tile([P, PACK, HALF - own], BF16, name="rounded%d%d" % (a, h))
+                for h in range(2):
                     for i in range(PACK):
-                        nc.scalar.activation(
-                            rounded[:, i, :], kern[:, i, h * HALF + own : (h + 1) * HALF], COPY, scale=cw_col[:, a, i : i + 1]
-                        )
-                    nc.vector.tensor_copy(
-                        h_grouped[:, own * PACK :].rearrange("p (c e i) -> p c i e", e=4, i=PACK),
-                        rounded[:].rearrange("p i (c e) -> p c i e", e=4),
-                    )
-                grouped.append(h_grouped)
-            for h in range(2):
-                h_codes = keep.tile([P, HALF], U32, name="h_codes%d%d" % (a, h), align_bytes=64)
-                h_plane = keep.tile([P, HALF], U8, name="h_plane%d%d" % (a, h), align_bytes=64)
-                nc.vector.quantize_mx(out=h_codes[:].bitcast(FP8X4), scales=h_plane[:], in_=grouped[h][:])
-                for g in range(2):
-                    nc.tensor.matmul_mx(
-                        out=y_acc[g, h][:],
-                        lhsT=al_codes[:, a, g * P : (g + 1) * P].bitcast(FP8X4),
-                        lhsT_scale=al_planes[4 * a : P, g * P : (g + 1) * P],
-                        rhs=h_codes[:].bitcast(FP8X4),
-                        rhs_scale=h_plane[:],
-                        start=(a == 0),
-                        stop=(a == J_PASSES - 1),
-                    )
+                        half = psum.tile([P, HALF], F32, name="dots0_%d%d" % (h, i), tag="bank%d" % (4 * h + i))
+                        for c in range(2):
+                            for d in range(K_PASSES):
+                                at = h * HALF + c * QUARTER
+                                first_product(half[:, c * QUARTER : (c + 1) * QUARTER], a, i, d, slice(at, at + QUARTER))
+                        dots[i, h * HALF] = half[:]
+            else:
+                for i in range(PACK):
+                    whole = psum.tile([P, M], F32, name="dots%d_%d" % (a, i), tag="bank%d" % (4 * ((a + 1) % 2) + i))
+                    for d in range(K_PASSES):
+                        first_product(whole[:], a, i, d, slice(0, M))
+                    for m0, width in TANH_PIECES[a]:
+                        dots[i, m0] = whole[:, m0 : m0 + width]
 
-        for h in range(2):
+            kern = {}
+            for m0, width in TANH_PIECES[a]:
+                piece = tile([P, PACK, width], F32, "kern%d_%d" % (a, m0))
+                for i in range(PACK):
+                    nc.scalar.activation(piece[:, i, :], dots[i, m0], TANH, bias=cb_col[:, a, i : i + 1])
+                for w0, w, engine in WEIGH_PIECES[a]:
+                    if m0 <= w0 < m0 + width:
+                        kern[w0] = piece[:, :, w0 - m0 : w0 - m0 + w]
+                        if engine == "scalar":
+                            rounded = tile([P, PACK, w], BF16, "rounded%d_%d" % (a, w0))
+                            for i in range(PACK):
+                                nc.scalar.activation(rounded[:, i, :], kern[w0][:, i, :], COPY, scale=cw_col[:, a, i : i + 1])
+                            kern[w0] = rounded[:]
+
+            h_grouped = {}
+            for q0, qw in QUANT_PIECES[a]:
+                h_grouped[q0] = tile([P, qw * PACK], BF16, "h_grouped%d_%d" % (a, q0))
+            def weigh(q0, qw):
+                for w0, w, engine in WEIGH_PIECES[a]:
+                    lo, hi = max(q0, w0), min(q0 + qw, w0 + w)
+                    if lo >= hi:
+                        continue
+                    dst = interleaved(h_grouped[q0][:, (lo - q0) * PACK : (hi - q0) * PACK])
+                    src = planes(kern[w0][:, :, lo - w0 : hi - w0])
+                    if engine == "scalar":
+                        nc.vector.tensor_copy(dst, src)
+                    else:
+                        weights = cw_col[:, a, :].unsqueeze(1).unsqueeze(3).to_broadcast([P, (hi - lo) // 4, PACK, 4])
+                        nc.vector.tensor_tensor(dst, src, weights, MULT)
+
+            def quantise_h(q0, qw):
+                nc.vector.quantize_mx(
+                    out=h_codes[a][:, q0 : q0 + qw].bitcast(FP8X4), scales=h_planes[a][:, q0 : q0 + qw], in_=h_grouped[q0][:]
+                )
+
+            pieces = QUANT_PIECES[a]
+            weigh(*pieces[0])
+            for before, piece_now in zip(pieces, pieces[1:]):
+                weigh(*piece_now)
+                quantise_h(*before)
+            quantise_h(*pieces[-1])
+
+        y_left = psum.tile([P, 2, HALF], F32, name="y_left", tag="bank4")
+        y_third = psum.tile([P, 2, QUARTER], F32, name="y_third", tag="bank5")
+        y_last = [psum.tile([P, QUARTER], F32, name="y_last%d" % g, tag="bank%d" % (6 + g)) for g in range(2)]
+
+        def second_product(dst, a, g, cols, start, stop):
+            nc.tensor.matmul_mx(
+                out=dst,
+                lhsT=al_codes[:, a, g * P : (g + 1) * P].bitcast(FP8X4),
+                lhsT_scale=al_planes[4 * a : P, g * P : (g + 1) * P],
+                rhs=h_codes[a][:, cols].bitcast(FP8X4),
+                rhs_scale=h_planes[a][:, cols],
+                start=start,
+                stop=stop,
+            )
+
+        last = J_PASSES - 1
+        for a in range(J_PASSES):
             for g in range(2):
-                result = keep.tile([P, HALF], F32, name="result%d%d" % (g, h))
-                if h == 1 and g == 1:
-                    nc.vector.tensor_copy(result[:], y_acc[g, h][:])
-                else:
-                    nc.scalar.copy(result[:], y_acc[g, h][:])
-                queue = nc.scalar if (h == 1 and g == 0) else nc.sync
-                queue.dma_start(out=out[g * P : (g + 1) * P, h * HALF : (h + 1) * HALF], in_=result[:])
+                second_product(y_left[:, g, :], a, g, slice(0, HALF), a == 0 and g == 0, a == last and g == 1)
+            for g in range(2):
+                second_product(y_third[:, g, :], a, g, slice(HALF, HALF + QUARTER), a == 0 and g == 0, a == last and g == 1)
+            for g in range(2):
+                second_product(y_last[g][:], a, g, slice(HALF + QUARTER, M), a == 0, a == last)
+
+        out_rows = out.rearrange("(g p) m -> p g m", p=P)
+        result_left = keep.tile([P, 2, HALF], F32, name="result_left")
+        nc.scalar.copy(result_left[:], y_left[:])
+        nc.sync.dma_start(out=out_rows[:, :, 0:HALF], in_=result_left[:])
+        result_third = keep.tile([P, 2, QUARTER], F32, name="result_third")
+        nc.scalar.copy(result_third[:], y_third[:])
+        nc.sync.dma_start(out=out_rows[:, :, HALF : HALF + QUARTER], in_=result_third[:])
+        result_last = [keep.tile([P, QUARTER], F32, name="result_last%d" % g) for g in range(2)]
+        nc.scalar.copy(result_last[0][:], y_last[0][:])
+        nc.scalar.dma_start(out=out_rows[:, 0, HALF + QUARTER : M], in_=result_last[0][:])
+        nc.vector.tensor_copy(result_last[1][:], y_last[1][:])
+        nc.sync.dma_start(out=out_rows[:, 1, HALF + QUARTER : M], in_=result_last[1][:])

@@ -26,9 +26,9 @@ HALF = M // 2
 QUARTER = M // 4
 LIST_COLS = PASS // 16
 SCALE_ROWS = 32
-SLOT_BYTES = 2048
+SLOT_BYTES = 4096
 PLANE_AT = [0, 2, 0, 1]
-LATE_X = [(1, 1), (0, 2), (0, 3), (1, 2), (1, 3)]
+LATE_X = [(0, 2), (1, 2)]
 WEIGH_PIECES = [
     [(0, 256, "vector"), (256, 256, "vector")],
     [(0, 256, "vector"), (256, 256, "vector")],
@@ -77,10 +77,10 @@ def tile_list_kernl_tanh_none_kernel(
             nc.sync.dma_start(out=dst[:], in_=x_rows[d][:, :, first * QUARTER : (first + count) * QUARTER])
             x_raw[d, first] = dst
 
-        load_x(0, 0, 2, tile([P, PACK, HALF], F32, "x_early0"))
-        load_x(1, 0, 1, tile([P, PACK, QUARTER], F32, "x_early1"))
         word_table = tile([P, T], I32, "word_table")
         nc.sync.dma_start(out=word_table[:], in_=tab_words[0].rearrange("p t b -> p (t b)").bitcast(I32))
+        for d in range(K_PASSES):
+            load_x(d, 0, 2, tile([P, PACK, HALF], F32, "x_left%d" % d))
 
         warm = keep.tile([P, 8], F32, name="warm")
         nc.vector.memset(warm[:], 0.0)
@@ -120,7 +120,7 @@ def tile_list_kernl_tanh_none_kernel(
 
         place_scales(0)
         for slot, (d, c) in enumerate(LATE_X):
-            load_x(d, c, 1, placed([P, PACK, QUARTER], F32, "x_late%d%d" % (d, c), slot))
+            load_x(d, c, 2, placed([P, PACK, HALF], F32, "x_late%d%d" % (d, c), slot))
         cb_col = tile([P, J_PASSES, PACK], F32, "cb_col", tag="scale_table")
         nc.sync.dma_start(out=cb_col[:], in_=cb.rearrange("(a p i) -> p a i", p=P, i=PACK))
 
@@ -142,7 +142,6 @@ def tile_list_kernl_tanh_none_kernel(
                     nc.scalar.copy(interleaved(grouped[:, at : at + raw.shape[2] * PACK]), planes(raw[:]))
             quantise_x(d, h, grouped)
 
-        prepare_x(0, 0)
 
         tab_codes = {}
         picked_words = {}
@@ -163,18 +162,19 @@ def tile_list_kernl_tanh_none_kernel(
 
         words_shape, codes_shape = [P, PASS], [P, K_PASSES * 2 * PASS]
         gather_words(0, tile(words_shape, U32, "picked_words0"))
-        part_words(0, tile(codes_shape, U8, "tab_codes0"))
-        prepare_x(1, 0)
         sort_scales(sorted_scales[:, 0 : 2 * PASS], picked_rest[:, PASS : 3 * PASS])
         place_scales(1)
         cw_col = tile([P, J_PASSES, PACK], F32, "cw_col", tag="picked_rest")
         nc.sync.dma_start(out=cw_col[:], in_=cw.rearrange("(a p i) -> p a i", p=P, i=PACK))
+        prepare_x(0, 0)
+        part_words(0, tile(codes_shape, U8, "tab_codes0", tag="x_left0"))
+        prepare_x(1, 0)
+        gather_words(1, tile(words_shape, U32, "picked_words1", tag="x_left1"))
         prepare_x(0, 1)
-        gather_words(1, placed(words_shape, U32, "picked_words1", LATE_X.index((0, 3))))
+        part_words(1, placed(codes_shape, U8, "tab_codes1", 0))
         prepare_x(1, 1)
-        part_words(1, placed(codes_shape, U8, "tab_codes1", LATE_X.index((1, 3))))
-        gather_words(2, tile(words_shape, U32, "picked_words2", tag="x_grouped11"))
-        gather_words(3, placed(words_shape, U32, "picked_words3", LATE_X.index((0, 3))))
+        gather_words(2, placed(words_shape, U32, "picked_words2", 1))
+        gather_words(3, tile(words_shape, U32, "picked_words3", tag="x_grouped11"))
         part_words(2, tile(codes_shape, U8, "tab_codes2"))
         part_words(3, tile(codes_shape, U8, "tab_codes3"))
 

@@ -27,13 +27,13 @@ QUARTER = M // 4
 LIST_COLS = PASS // 16
 SCALE_ROWS = 32
 SLOT_BYTES = 4096
-PLANE_AT = [0, 2, 0, 1]
+PLANE_AT = [0, 0, 1, 2]
 LATE_X = [(0, 2), (1, 2)]
 WEIGH_PIECES = [
     [(0, 256, "vector"), (256, 256, "vector")],
     [(0, 256, "vector"), (256, 256, "vector")],
-    [(0, 512, "scalar")],
-    [(0, 256, "vector"), (256, 128, "vector"), (384, 128, "vector")],
+    [(0, 256, "vector"), (256, 256, "vector")],
+    [(0, 256, "scalar"), (256, 256, "scalar")],
 ]
 TANH_PIECES = [[(0, 256), (256, 256)], [(0, 512)], [(0, 512)], [(0, 256), (256, 256)]]
 QUANT_PIECES = [[(0, 256), (256, 256)], [(0, 256), (256, 256)], [(0, 256), (256, 256)], [(0, 256), (256, 128), (384, 128)]]
@@ -93,7 +93,7 @@ def tile_list_kernl_tanh_none_kernel(
         for u in range(2):
             nc.gpsimd.memset(tab_planes[u][:].rearrange("p d j -> p (d j)").bitcast(I32), 0)
 
-        sorted_scales = tile([P, 3 * PASS], U8, "sorted_scales")
+        sorted_scales = tile([P, J], U8, "sorted_scales")
         picked_first = placed([P, len(LATE_X) * SLOT_BYTES], U8, "picked_first", 0)[:, 0:PASS]
         picked_rest = tile([P, 3 * PASS], U8, "picked_rest")
 
@@ -106,17 +106,18 @@ def tile_list_kernl_tanh_none_kernel(
             )
 
         def place_scales(u):
-            for quad in range(4):
+            for quad in (0, 2, 1, 3):
                 nc.sync.dma_start(
                     out=tab_planes[u][32 * quad : 32 * quad + 4, :, :].bitcast(I32),
-                    in_=sorted_scales[live + 8 * quad : live + 8 * quad + 8, 0 : widths[u]].bitcast(I32),
+                    in_=sorted_scales[live + 8 * quad : live + 8 * quad + 8, u * PASS : u * PASS + widths[u]].bitcast(I32),
                 )
 
         pick_scales(picked_first, 0, 1)
         pick_scales(picked_rest[:, 0:PASS], 1, 1)
         sort_scales(sorted_scales[:, 0:PASS], picked_first)
         pick_scales(picked_rest[:, PASS : 3 * PASS], 2, 2)
-        sort_scales(sorted_scales[:, 2 * PASS : 3 * PASS], picked_rest[:, 0:PASS])
+        sort_scales(sorted_scales[:, PASS : 2 * PASS], picked_rest[:, 0:PASS])
+        sort_scales(sorted_scales[:, 2 * PASS : 4 * PASS], picked_rest[:, PASS : 3 * PASS])
 
         place_scales(0)
         for slot, (d, c) in enumerate(LATE_X):
@@ -162,24 +163,23 @@ def tile_list_kernl_tanh_none_kernel(
 
         words_shape, codes_shape = [P, PASS], [P, K_PASSES * 2 * PASS]
         gather_words(0, tile(words_shape, U32, "picked_words0"))
-        sort_scales(sorted_scales[:, 0 : 2 * PASS], picked_rest[:, PASS : 3 * PASS])
         place_scales(1)
         cw_col = tile([P, J_PASSES, PACK], F32, "cw_col", tag="picked_rest")
         nc.sync.dma_start(out=cw_col[:], in_=cw.rearrange("(a p i) -> p a i", p=P, i=PACK))
+        gather_words(1, tile(words_shape, U32, "picked_words1"))
         prepare_x(0, 0)
         part_words(0, tile(codes_shape, U8, "tab_codes0", tag="x_left0"))
         prepare_x(1, 0)
-        gather_words(1, tile(words_shape, U32, "picked_words1", tag="x_left1"))
+        part_words(1, tile(codes_shape, U8, "tab_codes1", tag="x_left1"))
+        gather_words(2, tile(words_shape, U32, "picked_words2", tag="x_grouped10"))
         prepare_x(0, 1)
-        part_words(1, placed(codes_shape, U8, "tab_codes1", 0))
         prepare_x(1, 1)
-        gather_words(2, placed(words_shape, U32, "picked_words2", 1))
-        gather_words(3, tile(words_shape, U32, "picked_words3", tag="x_grouped11"))
-        part_words(2, tile(codes_shape, U8, "tab_codes2"))
+        gather_words(3, placed(words_shape, U32, "picked_words3", 1))
+        part_words(2, tile(codes_shape, U8, "tab_codes2", tag="x_grouped11"))
         part_words(3, tile(codes_shape, U8, "tab_codes3"))
 
-        al_planes = sorted_scales[:, 0:N]
-        al_codes = tile([P, J_PASSES, N], I32, "al_codes", tag="x_grouped10")
+        al_planes = sorted_scales[:, PASS : PASS + N]
+        al_codes = tile([P, J_PASSES, N], I32, "al_codes", tag="picked_words0")
         for quad in range(4):
             nc.sync.dma_start(
                 out=al_planes[32 * quad : 32 * quad + 16, :].bitcast(I32),
@@ -202,6 +202,13 @@ def tile_list_kernl_tanh_none_kernel(
 
         h_codes = [tile([P, M], U32, "h_codes%d" % a) for a in range(J_PASSES)]
         h_planes = [tile([P, M], U8, "h_planes%d" % a) for a in range(J_PASSES)]
+
+        def quantise_h(a, grouped, q0, qw):
+            nc.vector.quantize_mx(
+                out=h_codes[a][:, q0 : q0 + qw].bitcast(FP8X4), scales=h_planes[a][:, q0 : q0 + qw], in_=grouped[:]
+            )
+
+        waiting = []
         for a in range(J_PASSES):
             dots = {}
             if a == 0:
@@ -251,17 +258,21 @@ def tile_list_kernl_tanh_none_kernel(
                         weights = cw_col[:, a, :].unsqueeze(1).unsqueeze(3).to_broadcast([P, (hi - lo) // 4, PACK, 4])
                         nc.vector.tensor_tensor(dst, src, weights, MULT)
 
-            def quantise_h(q0, qw):
-                nc.vector.quantize_mx(
-                    out=h_codes[a][:, q0 : q0 + qw].bitcast(FP8X4), scales=h_planes[a][:, q0 : q0 + qw], in_=h_grouped[q0][:]
-                )
 
             pieces = QUANT_PIECES[a]
             weigh(*pieces[0])
-            for before, piece_now in zip(pieces, pieces[1:]):
-                weigh(*piece_now)
-                quantise_h(*before)
-            quantise_h(*pieces[-1])
+            if waiting:
+                quantise_h(*waiting.pop())
+            if a < J_PASSES - 1:
+                weigh(*pieces[1])
+                quantise_h(a, h_grouped[0], *pieces[0])
+                waiting.append((a, h_grouped[pieces[1][0]], *pieces[1]))
+            else:
+                quantise_h(a, h_grouped[0], *pieces[0])
+                for piece_now in pieces[1:]:
+                    weigh(*piece_now)
+                for piece_now in pieces[1:]:
+                    quantise_h(a, h_grouped[piece_now[0]], *piece_now)
 
         y_left = psum.tile([P, 2, HALF], F32, name="y_left", tag="bank4")
         y_third = psum.tile([P, 2, QUARTER], F32, name="y_third", tag="bank5")

@@ -1,6 +1,7 @@
 from contextlib import ExitStack
 
 import concourse.mybir as mybir
+from concourse.masks import make_identity
 
 K, M, N, J, T = 1024, 512, 256, 2048, 4096
 FLOPS = 2 * K * J * M + 2 * J * N * M
@@ -29,14 +30,16 @@ SCALE_ROWS = 32
 SLOT_BYTES = 4096
 PLANE_AT = [0, 0, 1, 2]
 LATE_X = [(0, 2), (1, 2)]
+SIDE = 96
 WEIGH_PIECES = [
-    [(0, 256, "vector"), (256, 256, "vector")],
-    [(0, 256, "vector"), (256, 256, "vector")],
-    [(0, 256, "vector"), (256, 256, "vector")],
+    [(0, SIDE, "gpsimd"), (SIDE, 256 - SIDE, "vector"), (256, 256, "vector")],
+    [(0, SIDE, "gpsimd"), (SIDE, 256 - SIDE, "vector"), (256, 256, "vector")],
+    [(0, SIDE, "gpsimd"), (SIDE, 256 - SIDE, "vector"), (256, 256, "vector")],
     [(0, 256, "scalar"), (256, 256, "scalar")],
 ]
 TANH_PIECES = [[(0, 256), (256, 256)], [(0, 512)], [(0, 512)], [(0, 256), (256, 256)]]
 QUANT_PIECES = [[(0, 256), (256, 256)], [(0, 256), (256, 256)], [(0, 256), (256, 256)], [(0, 256), (256, 128), (384, 128)]]
+DOT_BANKS = 7
 OUT_PIECES = [(0, 256), (256, 128), (384, 128)]
 
 
@@ -92,6 +95,15 @@ def tile_list_kernl_tanh_none_kernel(
         tab_planes = [tile([P, K_PASSES, widths[u]], U8, "tab_planes%d" % u) for u in range(2)]
         for u in range(2):
             nc.gpsimd.memset(tab_planes[u][:].rearrange("p d j -> p (d j)").bitcast(I32), 0)
+
+        identity = tile([P, P], F32, "identity")
+        make_identity(nc, identity[:])
+        cw_rows = tile([P, PASS], F32, "cw_rows")
+        nc.gpsimd.memset(cw_rows[:], 0.0)
+        nc.sync.dma_start(out=cw_rows[0:J_PASSES, :], in_=cw.rearrange("(a j) -> a j", a=J_PASSES))
+        cw_psum = psum.tile([P, PACK, P], F32, name="cw_psum", tag="bank7")
+        for i in range(PACK):
+            nc.tensor.transpose(cw_psum[:, i, :], cw_rows[:].rearrange("p (q i) -> p i q", i=PACK)[:, i, :], identity[:])
 
         sorted_scales = tile([P, J], U8, "sorted_scales")
         picked_first = placed([P, len(LATE_X) * SLOT_BYTES], U8, "picked_first", 0)[:, 0:PASS]
@@ -208,13 +220,13 @@ def tile_list_kernl_tanh_none_kernel(
                 out=h_codes[a][:, q0 : q0 + qw].bitcast(FP8X4), scales=h_planes[a][:, q0 : q0 + qw], in_=grouped[:]
             )
 
-        waiting = []
+        h_ring = placed([P, (3 * M - 2 * SIDE) * PACK], BF16, "h_ring", 1)
         for a in range(J_PASSES):
             dots = {}
             if a == 0:
                 for h in range(2):
                     for i in range(PACK):
-                        half = psum.tile([P, HALF], F32, name="dots0_%d%d" % (h, i), tag="bank%d" % (4 * h + i))
+                        half = psum.tile([P, HALF], F32, name="dots0_%d%d" % (h, i), tag="bank%d" % ((4 * h + i) % DOT_BANKS))
                         for c in range(2):
                             for d in range(K_PASSES):
                                 at = h * HALF + c * QUARTER
@@ -222,7 +234,7 @@ def tile_list_kernl_tanh_none_kernel(
                         dots[i, h * HALF] = half[:]
             else:
                 for i in range(PACK):
-                    whole = psum.tile([P, M], F32, name="dots%d_%d" % (a, i), tag="bank%d" % (4 * ((a + 1) % 2) + i))
+                    whole = psum.tile([P, M], F32, name="dots%d_%d" % (a, i), tag="bank%d" % ((4 * (a + 1) + i) % DOT_BANKS))
                     for d in range(K_PASSES):
                         first_product(whole[:], a, i, d, slice(0, M))
                     for m0, width in TANH_PIECES[a]:
@@ -244,7 +256,12 @@ def tile_list_kernl_tanh_none_kernel(
 
             h_grouped = {}
             for q0, qw in QUANT_PIECES[a]:
-                h_grouped[q0] = tile([P, qw * PACK], BF16, "h_grouped%d_%d" % (a, q0))
+                if a < J_PASSES - 1:
+                    at = (a * (M - SIDE) + q0) * PACK
+                    h_grouped[q0] = h_ring[:, at : at + qw * PACK]
+                else:
+                    h_grouped[q0] = tile([P, qw * PACK], BF16, "h_grouped%d_%d" % (a, q0))
+
             def weigh(q0, qw):
                 for w0, w, engine in WEIGH_PIECES[a]:
                     lo, hi = max(q0, w0), min(q0 + qw, w0 + w)
@@ -254,29 +271,39 @@ def tile_list_kernl_tanh_none_kernel(
                     src = planes(kern[w0][:, :, lo - w0 : hi - w0])
                     if engine == "scalar":
                         nc.vector.tensor_copy(dst, src)
+                    elif engine == "gpsimd":
+                        nc.gpsimd.tensor_tensor(
+                            h_grouped[q0][:, (lo - q0) * PACK : (hi - q0) * PACK].rearrange("p (m i) -> p m i", i=PACK),
+                            kern[w0][:, :, lo - w0 : hi - w0].rearrange("p i m -> p m i"),
+                            cw_col[:, a, :].unsqueeze(1).to_broadcast([P, hi - lo, PACK]),
+                            MULT,
+                        )
                     else:
-                        weights = cw_col[:, a, :].unsqueeze(1).unsqueeze(3).to_broadcast([P, (hi - lo) // 4, PACK, 4])
+                        weights = cw_psum[:, :, a].unsqueeze(1).unsqueeze(3).to_broadcast([P, (hi - lo) // 4, PACK, 4])
                         nc.vector.tensor_tensor(dst, src, weights, MULT)
 
 
             pieces = QUANT_PIECES[a]
-            weigh(*pieces[0])
-            if waiting:
-                quantise_h(*waiting.pop())
             if a < J_PASSES - 1:
-                weigh(*pieces[1])
+                for piece_now in pieces:
+                    weigh(*piece_now)
                 quantise_h(a, h_grouped[0], *pieces[0])
-                waiting.append((a, h_grouped[pieces[1][0]], *pieces[1]))
+                if a < J_PASSES - 2:
+                    quantise_h(a, h_grouped[HALF], *pieces[1])
+                else:
+                    waiting = (a, h_grouped[HALF], *pieces[1])
             else:
+                weigh(*pieces[0])
+                quantise_h(*waiting)
                 quantise_h(a, h_grouped[0], *pieces[0])
                 for piece_now in pieces[1:]:
                     weigh(*piece_now)
                 for piece_now in pieces[1:]:
                     quantise_h(a, h_grouped[piece_now[0]], *piece_now)
 
-        y_left = psum.tile([P, 2, HALF], F32, name="y_left", tag="bank4")
-        y_third = psum.tile([P, 2, QUARTER], F32, name="y_third", tag="bank5")
-        y_last = [psum.tile([P, QUARTER], F32, name="y_last%d" % g, tag="bank%d" % (6 + g)) for g in range(2)]
+        y_left = psum.tile([P, 2, HALF], F32, name="y_left", tag="bank6")
+        y_third = psum.tile([P, 2, QUARTER], F32, name="y_third", tag="bank0")
+        y_last = [psum.tile([P, QUARTER], F32, name="y_last%d" % g, tag="bank%d" % (1 + g)) for g in range(2)]
 
         def second_product(dst, a, g, cols, start, stop):
             nc.tensor.matmul_mx(
@@ -290,13 +317,19 @@ def tile_list_kernl_tanh_none_kernel(
             )
 
         last = J_PASSES - 1
-        for a in range(J_PASSES):
+        def add_group(a, last_halves):
             for g in range(2):
                 second_product(y_left[:, g, :], a, g, slice(0, HALF), a == 0 and g == 0, a == last and g == 1)
             for g in range(2):
                 second_product(y_third[:, g, :], a, g, slice(HALF, HALF + QUARTER), a == 0 and g == 0, a == last and g == 1)
-            for g in range(2):
+            for g in last_halves:
                 second_product(y_last[g][:], a, g, slice(HALF + QUARTER, M), a == 0, a == last)
+
+        for a in range(last):
+            add_group(a, [0])
+        for a in range(last):
+            second_product(y_last[1][:], a, 1, slice(HALF + QUARTER, M), a == 0, False)
+        add_group(last, [0, 1])
 
         out_rows = out.rearrange("(g p) m -> p g m", p=P)
         result_left = keep.tile([P, 2, HALF], F32, name="result_left")

@@ -28,11 +28,10 @@ QUARTER = M // 4
 LIST_COLS = PASS // 16
 SCALE_ROWS = 32
 SLOT_BYTES = 4096
-PLANE_AT = [0, 0, 1, 2]
 LATE_X = [(0, 2), (1, 2)]
-SIDE = 96
+SIDE = 104
 WEIGH_PIECES = [
-    [(0, SIDE, "gpsimd"), (SIDE, 256 - SIDE, "vector"), (256, 256, "vector")],
+    [(0, 256, "vector"), (256, 256, "vector")],
     [(0, SIDE, "gpsimd"), (SIDE, 256 - SIDE, "vector"), (256, 256, "vector")],
     [(0, SIDE, "gpsimd"), (SIDE, 256 - SIDE, "vector"), (256, 256, "vector")],
     [(0, 256, "scalar"), (256, 256, "scalar")],
@@ -40,7 +39,6 @@ WEIGH_PIECES = [
 TANH_PIECES = [[(0, 256), (256, 256)], [(0, 512)], [(0, 512)], [(0, 256), (256, 256)]]
 QUANT_PIECES = [[(0, 256), (256, 256)], [(0, 256), (256, 256)], [(0, 256), (256, 256)], [(0, 256), (256, 128), (384, 128)]]
 DOT_BANKS = 7
-OUT_PIECES = [(0, 256), (256, 128), (384, 128)]
 
 
 def tile_list_kernl_tanh_none_kernel(
@@ -91,10 +89,11 @@ def tile_list_kernl_tanh_none_kernel(
         nc.scalar.activation(warm_out[:], warm[:], TANH)
 
         nc.vector.memset(scale_table[0:live, :].bitcast(I32), 0)
-        widths = [PASS, 3 * PASS]
-        tab_planes = [tile([P, K_PASSES, widths[u]], U8, "tab_planes%d" % u) for u in range(2)]
+        tab_planes = [tile([P, K_PASSES, 2 * PASS], U8, "tab_planes%d" % u) for u in range(2)]
         for u in range(2):
             nc.gpsimd.memset(tab_planes[u][:].rearrange("p d j -> p (d j)").bitcast(I32), 0)
+        spread_scales = tile([P, PASS], U8, "spread_scales")
+        nc.gpsimd.memset(spread_scales[0:64, :].bitcast(I32), 0)
 
         identity = tile([P, P], F32, "identity")
         make_identity(nc, identity[:])
@@ -105,9 +104,9 @@ def tile_list_kernl_tanh_none_kernel(
         for i in range(PACK):
             nc.tensor.transpose(cw_psum[:, i, :], cw_rows[:].rearrange("p (q i) -> p i q", i=PACK)[:, i, :], identity[:])
 
-        sorted_scales = tile([P, J], U8, "sorted_scales")
-        picked_first = placed([P, len(LATE_X) * SLOT_BYTES], U8, "picked_first", 0)[:, 0:PASS]
-        picked_rest = tile([P, 3 * PASS], U8, "picked_rest")
+        picked_early = placed([P, len(LATE_X) * SLOT_BYTES], U8, "picked_early", 0)[:, 0 : 2 * PASS]
+        picked_late = tile([P, 2 * PASS], U8, "picked_late")
+        sorted_early = tile([P, 2 * PASS], U8, "sorted_early")
 
         def pick_scales(dst, first, count):
             nc.vector.tensor_copy(dst, scale_table[:].indirect(offsets[:, first * LIST_COLS : (first + count) * LIST_COLS]))
@@ -117,23 +116,25 @@ def tile_list_kernl_tanh_none_kernel(
                 dst.rearrange("p (a i q) -> p a i q", i=PACK, q=P), src.rearrange("p (a q i) -> p a i q", i=PACK, q=P)
             )
 
-        def place_scales(u):
+        def place_scales(dst, src, first, rows):
             for quad in (0, 2, 1, 3):
                 nc.sync.dma_start(
-                    out=tab_planes[u][32 * quad : 32 * quad + 4, :, :].bitcast(I32),
-                    in_=sorted_scales[live + 8 * quad : live + 8 * quad + 8, u * PASS : u * PASS + widths[u]].bitcast(I32),
+                    out=dst[32 * quad : 32 * quad + 4, :, :].bitcast(I32),
+                    in_=src[first + rows * quad : first + rows * (quad + 1), :].bitcast(I32),
                 )
 
-        pick_scales(picked_first, 0, 1)
-        pick_scales(picked_rest[:, 0:PASS], 1, 1)
-        sort_scales(sorted_scales[:, 0:PASS], picked_first)
-        pick_scales(picked_rest[:, PASS : 3 * PASS], 2, 2)
-        sort_scales(sorted_scales[:, PASS : 2 * PASS], picked_rest[:, 0:PASS])
-        sort_scales(sorted_scales[:, 2 * PASS : 4 * PASS], picked_rest[:, PASS : 3 * PASS])
+        pick_scales(picked_early, 0, 2)
+        pick_scales(picked_late[:, 0:PASS], 2, 1)
+        sort_scales(sorted_early[:], picked_early)
+        pick_scales(picked_late[:, PASS : 2 * PASS], 3, 1)
 
-        place_scales(0)
+        place_scales(tab_planes[0], sorted_early, live, 8)
         for slot, (d, c) in enumerate(LATE_X):
             load_x(d, c, 2, placed([P, PACK, HALF], F32, "x_late%d%d" % (d, c), slot))
+        nc.sync.dma_start(
+            out=spread_scales[64:P, :].bitcast(I32),
+            in_=picked_late[live:P, :].bitcast(I32).rearrange("p (a w) -> p a w", a=2),
+        )
         cb_col = tile([P, J_PASSES, PACK], F32, "cb_col", tag="scale_table")
         nc.sync.dma_start(out=cb_col[:], in_=cb.rearrange("(a p i) -> p a i", p=P, i=PACK))
 
@@ -175,8 +176,7 @@ def tile_list_kernl_tanh_none_kernel(
 
         words_shape, codes_shape = [P, PASS], [P, K_PASSES * 2 * PASS]
         gather_words(0, tile(words_shape, U32, "picked_words0"))
-        place_scales(1)
-        cw_col = tile([P, J_PASSES, PACK], F32, "cw_col", tag="picked_rest")
+        cw_col = tile([P, J_PASSES, PACK], F32, "cw_col", tag="picked_late")
         nc.sync.dma_start(out=cw_col[:], in_=cw.rearrange("(a p i) -> p a i", p=P, i=PACK))
         gather_words(1, tile(words_shape, U32, "picked_words1"))
         prepare_x(0, 0)
@@ -184,13 +184,16 @@ def tile_list_kernl_tanh_none_kernel(
         prepare_x(1, 0)
         part_words(1, tile(codes_shape, U8, "tab_codes1", tag="x_left1"))
         gather_words(2, tile(words_shape, U32, "picked_words2", tag="x_grouped10"))
+        sorted_late = tile([P, PASS], U8, "sorted_late")
+        sort_scales(sorted_late[:], spread_scales[:])
+        place_scales(tab_planes[1][:].rearrange("p d (a w) -> p (d a) w", a=2), sorted_late, 64, 16)
         prepare_x(0, 1)
         prepare_x(1, 1)
         gather_words(3, placed(words_shape, U32, "picked_words3", 1))
         part_words(2, tile(codes_shape, U8, "tab_codes2", tag="x_grouped11"))
         part_words(3, tile(codes_shape, U8, "tab_codes3"))
 
-        al_planes = sorted_scales[:, PASS : PASS + N]
+        al_planes = sorted_late[:, 0:N]
         al_codes = tile([P, J_PASSES, N], I32, "al_codes", tag="picked_words0")
         for quad in range(4):
             nc.sync.dma_start(
@@ -201,11 +204,11 @@ def tile_list_kernl_tanh_none_kernel(
 
         def first_product(dst, a, i, d, cols):
             col = (d * PACK + i) * 2 * P
-            first = PLANE_AT[a] * PASS + i * P
+            first = (a % 2) * PASS + i * P
             nc.tensor.matmul_mx(
                 out=dst,
                 lhsT=tab_codes[a][:, col : col + 2 * P].bitcast(FP4X4),
-                lhsT_scale=tab_planes[min(a, 1)][:, d, first : first + P],
+                lhsT_scale=tab_planes[a // 2][:, d, first : first + P],
                 rhs=x_codes[d][:, cols].bitcast(FP8X4),
                 rhs_scale=x_planes[d][:, cols],
                 start=(d == 0),
@@ -220,7 +223,6 @@ def tile_list_kernl_tanh_none_kernel(
                 out=h_codes[a][:, q0 : q0 + qw].bitcast(FP8X4), scales=h_planes[a][:, q0 : q0 + qw], in_=grouped[:]
             )
 
-        h_ring = placed([P, (3 * M - 2 * SIDE) * PACK], BF16, "h_ring", 1)
         for a in range(J_PASSES):
             dots = {}
             if a == 0:
@@ -256,11 +258,8 @@ def tile_list_kernl_tanh_none_kernel(
 
             h_grouped = {}
             for q0, qw in QUANT_PIECES[a]:
-                if a < J_PASSES - 1:
-                    at = (a * (M - SIDE) + q0) * PACK
-                    h_grouped[q0] = h_ring[:, at : at + qw * PACK]
-                else:
-                    h_grouped[q0] = tile([P, qw * PACK], BF16, "h_grouped%d_%d" % (a, q0))
+                shared = (a, q0) in [(0, HALF), (1, 0), (2, 0)]
+                h_grouped[q0] = tile([P, qw * PACK], BF16, "h_grouped%d_%d" % (a, q0), tag="h_shared" if shared else None)
 
             def weigh(q0, qw):
                 for w0, w, engine in WEIGH_PIECES[a]:
@@ -285,13 +284,14 @@ def tile_list_kernl_tanh_none_kernel(
 
             pieces = QUANT_PIECES[a]
             if a < J_PASSES - 1:
-                for piece_now in pieces:
-                    weigh(*piece_now)
-                quantise_h(a, h_grouped[0], *pieces[0])
+                first_piece, second_piece = pieces if a == 0 else reversed(pieces)
+                weigh(*first_piece)
+                weigh(*second_piece)
+                quantise_h(a, h_grouped[first_piece[0]], *first_piece)
                 if a < J_PASSES - 2:
-                    quantise_h(a, h_grouped[HALF], *pieces[1])
+                    quantise_h(a, h_grouped[second_piece[0]], *second_piece)
                 else:
-                    waiting = (a, h_grouped[HALF], *pieces[1])
+                    waiting = (a, h_grouped[second_piece[0]], *second_piece)
             else:
                 weigh(*pieces[0])
                 quantise_h(*waiting)

@@ -34,7 +34,7 @@ WEIGH_PIECES = [
     [(0, 256, "vector"), (256, 256, "vector")],
     [(0, SIDE, "gpsimd"), (SIDE, 256 - SIDE, "vector"), (256, 256, "vector")],
     [(0, SIDE, "gpsimd"), (SIDE, 256 - SIDE, "vector"), (256, 256, "vector")],
-    [(0, 256, "scalar"), (256, 256, "scalar")],
+    [(0, 256, "vector"), (256, 256, "scalar")],
 ]
 TANH_PIECES = [[(0, 256), (256, 256)], [(0, 512)], [(0, 512)], [(0, 256), (256, 256)]]
 QUANT_PIECES = [[(0, 256), (256, 256)], [(0, 256), (256, 256)], [(0, 256), (256, 256)], [(0, 256), (256, 128), (384, 128)]]
@@ -96,13 +96,8 @@ def tile_list_kernl_tanh_none_kernel(
         nc.gpsimd.memset(spread_scales[0:64, :].bitcast(I32), 0)
 
         identity = tile([P, P], F32, "identity")
-        make_identity(nc, identity[:])
-        cw_rows = tile([P, PASS], F32, "cw_rows")
-        nc.gpsimd.memset(cw_rows[:], 0.0)
-        nc.sync.dma_start(out=cw_rows[0:J_PASSES, :], in_=cw.rearrange("(a j) -> a j", a=J_PASSES))
-        cw_psum = psum.tile([P, PACK, P], F32, name="cw_psum", tag="bank7")
-        for i in range(PACK):
-            nc.tensor.transpose(cw_psum[:, i, :], cw_rows[:].rearrange("p (q i) -> p i q", i=PACK)[:, i, :], identity[:])
+        nc.vector.memset(identity[:], 0.0)
+        make_identity(nc, identity[:], nomemset=True)
 
         picked_early = placed([P, len(LATE_X) * SLOT_BYTES], U8, "picked_early", 0)[:, 0 : 2 * PASS]
         picked_late = tile([P, 2 * PASS], U8, "picked_late")
@@ -194,7 +189,7 @@ def tile_list_kernl_tanh_none_kernel(
         part_words(3, tile(codes_shape, U8, "tab_codes3"))
 
         al_planes = sorted_late[:, 0:N]
-        al_codes = tile([P, J_PASSES, N], I32, "al_codes", tag="picked_words0")
+        al_codes = tile([P, J_PASSES, N], I32, "al_codes", tag="x_grouped01")
         for quad in range(4):
             nc.sync.dma_start(
                 out=al_planes[32 * quad : 32 * quad + 16, :].bitcast(I32),
@@ -256,6 +251,13 @@ def tile_list_kernl_tanh_none_kernel(
                                 nc.scalar.activation(rounded[:, i, :], kern[w0][:, i, :], COPY, scale=cw_col[:, a, i : i + 1])
                             kern[w0] = rounded[:]
 
+            if a == 1:
+                cw_rows = x_raw[LATE_X[0]][:].rearrange("p i m -> p (i m)")[:, 0:PASS]
+                nc.sync.dma_start(out=cw_rows[0:J_PASSES, :], in_=cw.rearrange("(a j) -> a j", a=J_PASSES))
+                cw_psum = psum.tile([P, PACK, P], F32, name="cw_psum", tag="bank7")
+                for i in range(PACK):
+                    nc.tensor.transpose(cw_psum[:, i, :], cw_rows.rearrange("p (q i) -> p i q", i=PACK)[:, i, :], identity[:])
+
             h_grouped = {}
             for q0, qw in QUANT_PIECES[a]:
                 shared = (a, q0) in [(0, HALF), (1, 0), (2, 0)]
@@ -278,7 +280,8 @@ def tile_list_kernl_tanh_none_kernel(
                             MULT,
                         )
                     else:
-                        weights = cw_psum[:, :, a].unsqueeze(1).unsqueeze(3).to_broadcast([P, (hi - lo) // 4, PACK, 4])
+                        column = cw_psum[:, :, a] if a in (1, 2) else cw_col[:, a, :]
+                        weights = column.unsqueeze(1).unsqueeze(3).to_broadcast([P, (hi - lo) // 4, PACK, 4])
                         nc.vector.tensor_tensor(dst, src, weights, MULT)
 
 
@@ -332,9 +335,10 @@ def tile_list_kernl_tanh_none_kernel(
         add_group(last, [0, 1])
 
         out_rows = out.rearrange("(g p) m -> p g m", p=P)
-        result_left = keep.tile([P, 2, HALF], F32, name="result_left")
-        nc.scalar.copy(result_left[:], y_left[:])
-        nc.sync.dma_start(out=out_rows[:, :, 0:HALF], in_=result_left[:])
+        for g in range(2):
+            result_left = keep.tile([P, HALF], F32, name="result_left%d" % g)
+            nc.scalar.copy(result_left[:], y_left[:, g, :])
+            nc.sync.dma_start(out=out_rows[:, g, 0:HALF], in_=result_left[:])
         result_third = keep.tile([P, 2, QUARTER], F32, name="result_third")
         nc.scalar.copy(result_third[:], y_third[:])
         nc.sync.dma_start(out=out_rows[:, :, HALF : HALF + QUARTER], in_=result_third[:])

@@ -30,10 +30,11 @@ SCALE_ROWS = 32
 SLOT_BYTES = 4096
 LATE_X = [(0, 2), (1, 2)]
 SIDE = 104
+LATE_SIDE = 160
 WEIGH_PIECES = [
     [(0, 256, "vector"), (256, 256, "vector")],
     [(0, SIDE, "gpsimd"), (SIDE, 256 - SIDE, "vector"), (256, 256, "vector")],
-    [(0, SIDE, "gpsimd"), (SIDE, 256 - SIDE, "vector"), (256, 256, "vector")],
+    [(0, 256, "vector"), (256, LATE_SIDE, "gpsimd"), (256 + LATE_SIDE, 256 - LATE_SIDE, "vector")],
     [(0, 256, "vector"), (256, 256, "scalar")],
 ]
 TANH_PIECES = [[(0, 256), (256, 256)], [(0, 512)], [(0, 512)], [(0, 256), (256, 256)]]
@@ -220,10 +221,10 @@ def tile_list_kernl_tanh_none_kernel(
 
         for a in range(J_PASSES):
             dots = {}
-            if a == 0:
+            if a in (0, J_PASSES - 1):
                 for h in range(2):
                     for i in range(PACK):
-                        half = psum.tile([P, HALF], F32, name="dots0_%d%d" % (h, i), tag="bank%d" % ((4 * h + i) % DOT_BANKS))
+                        half = psum.tile([P, HALF], F32, name="dots%d_%d%d" % (a, h, i), tag="bank%d" % ((4 * (h if a == 0 else a + 1) + i) % DOT_BANKS))
                         for c in range(2):
                             for d in range(K_PASSES):
                                 at = h * HALF + c * QUARTER
@@ -260,17 +261,20 @@ def tile_list_kernl_tanh_none_kernel(
 
             h_grouped = {}
             for q0, qw in QUANT_PIECES[a]:
-                shared = (a, q0) in [(0, HALF), (1, 0), (2, 0)]
+                shared = (a, q0) in [(0, HALF), (1, 0), (2, HALF)]
                 h_grouped[q0] = tile([P, qw * PACK], BF16, "h_grouped%d_%d" % (a, q0), tag="h_shared" if shared else None)
 
-            def weigh(q0, qw):
+            def weigh(q0, qw, engines=("vector", "scalar", "gpsimd"), group=(a, kern, h_grouped)):
+                a, kern, h_grouped = group
                 for w0, w, engine in WEIGH_PIECES[a]:
                     lo, hi = max(q0, w0), min(q0 + qw, w0 + w)
-                    if lo >= hi:
+                    if lo >= hi or engine not in engines:
                         continue
                     dst = interleaved(h_grouped[q0][:, (lo - q0) * PACK : (hi - q0) * PACK])
                     src = planes(kern[w0][:, :, lo - w0 : hi - w0])
-                    if engine == "scalar":
+                    if engine == "scalar" and lo == HALF + QUARTER:
+                        nc.scalar.copy(dst, src)
+                    elif engine == "scalar":
                         nc.vector.tensor_copy(dst, src)
                     elif engine == "gpsimd":
                         nc.gpsimd.tensor_tensor(
@@ -280,25 +284,28 @@ def tile_list_kernl_tanh_none_kernel(
                             MULT,
                         )
                     else:
-                        column = cw_psum[:, :, a] if a in (1, 2) else cw_col[:, a, :]
+                        column = cw_psum[:, :, a] if a > 0 else cw_col[:, a, :]
                         weights = column.unsqueeze(1).unsqueeze(3).to_broadcast([P, (hi - lo) // 4, PACK, 4])
                         nc.vector.tensor_tensor(dst, src, weights, MULT)
 
 
             pieces = QUANT_PIECES[a]
-            if a < J_PASSES - 1:
-                first_piece, second_piece = pieces if a == 0 else reversed(pieces)
-                weigh(*first_piece)
-                weigh(*second_piece)
-                quantise_h(a, h_grouped[first_piece[0]], *first_piece)
-                if a < J_PASSES - 2:
-                    quantise_h(a, h_grouped[second_piece[0]], *second_piece)
-                else:
-                    waiting = (a, h_grouped[second_piece[0]], *second_piece)
+            if a < 2:
+                ordered = pieces if a == 0 else pieces[::-1]
+                for piece_now in ordered:
+                    weigh(*piece_now)
+                for piece_now in ordered:
+                    quantise_h(a, h_grouped[piece_now[0]], *piece_now)
+            elif a == 2:
+                weigh(*pieces[0])
+                weigh(*pieces[1], engines=("gpsimd",))
+                held = (a, kern, h_grouped)
             else:
                 weigh(*pieces[0])
-                quantise_h(*waiting)
+                weigh(HALF, HALF, engines=("vector",), group=held)
+                quantise_h(2, held[2][0], 0, HALF)
                 quantise_h(a, h_grouped[0], *pieces[0])
+                quantise_h(2, held[2][HALF], HALF, HALF)
                 for piece_now in pieces[1:]:
                     weigh(*piece_now)
                 for piece_now in pieces[1:]:
@@ -320,19 +327,29 @@ def tile_list_kernl_tanh_none_kernel(
             )
 
         last = J_PASSES - 1
-        def add_group(a, last_halves):
+        def add_left(a):
             for g in range(2):
                 second_product(y_left[:, g, :], a, g, slice(0, HALF), a == 0 and g == 0, a == last and g == 1)
+
+        def add_third(a):
             for g in range(2):
                 second_product(y_third[:, g, :], a, g, slice(HALF, HALF + QUARTER), a == 0 and g == 0, a == last and g == 1)
-            for g in last_halves:
-                second_product(y_last[g][:], a, g, slice(HALF + QUARTER, M), a == 0, a == last)
 
-        for a in range(last):
-            add_group(a, [0])
-        for a in range(last):
-            second_product(y_last[1][:], a, 1, slice(HALF + QUARTER, M), a == 0, False)
-        add_group(last, [0, 1])
+        def add_last(a, g):
+            second_product(y_last[g][:], a, g, slice(HALF + QUARTER, M), a == 0, a == last)
+
+        for a in range(2):
+            add_left(a)
+            add_third(a)
+            add_last(a, 0)
+        add_left(2)
+        add_left(3)
+        for a in range(2):
+            add_last(a, 1)
+        for a in (2, 3):
+            add_third(a)
+            for g in range(2):
+                add_last(a, g)
 
         out_rows = out.rearrange("(g p) m -> p g m", p=P)
         for g in range(2):

@@ -22,24 +22,22 @@ P = 128
 PACK = 4
 PASS = P * PACK
 K_PASSES = K // PASS
-J_PASSES = J // PASS
+GROUPS = J // PASS
 HALF = M // 2
 QUARTER = M // 4
+LEFT = slice(0, HALF)
+RIGHT = slice(HALF, M)
+THIRD = slice(HALF, HALF + QUARTER)
+FOURTH = slice(HALF + QUARTER, M)
 LIST_COLS = PASS // 16
-SCALE_ROWS = 32
-SLOT_BYTES = 4096
-LATE_X = [(0, 2), (1, 2)]
-SIDE = 104
-LATE_SIDE = 160
-WEIGH_PIECES = [
-    [(0, 256, "vector"), (256, 256, "vector")],
-    [(0, SIDE, "gpsimd"), (SIDE, 256 - SIDE, "vector"), (256, 256, "vector")],
-    [(0, 256, "vector"), (256, LATE_SIDE, "gpsimd"), (256 + LATE_SIDE, 256 - LATE_SIDE, "vector")],
-    [(0, 256, "vector"), (256, 256, "scalar")],
-]
-TANH_PIECES = [[(0, 256), (256, 256)], [(0, 512)], [(0, 512)], [(0, 256), (256, 256)]]
-QUANT_PIECES = [[(0, 256), (256, 256)], [(0, 256), (256, 256)], [(0, 256), (256, 256)], [(0, 256), (256, 128), (384, 128)]]
+RUN = 4
+SCALE_ROWS = K // 32
+FIRST_LIVE = P - SCALE_ROWS
+SPREAD_AT = 64
+SLOT_BYTES = PACK * HALF * 4
 DOT_BANKS = 7
+CW_STEP = 4
+GPSIMD_COLS = {1: 104, 2: 160}
 
 
 def tile_list_kernl_tanh_none_kernel(
@@ -51,61 +49,68 @@ def tile_list_kernl_tanh_none_kernel(
         reused = ctx.enter_context(tc.tile_pool(name="reused", bufs=1))
         psum = ctx.enter_context(tc.psum_pool(name="psum", bufs=1))
 
-        def placed(shape, dtype, name, slot):
-            return reused.tile(shape, dtype, name=name, align_bytes=64, offset=slot * SLOT_BYTES)
-
         def tile(shape, dtype, name, tag=None):
             return keep.tile(shape, dtype, name=name, tag=tag or name, align_bytes=64)
 
+        def tile_in_slot(shape, dtype, name, slot):
+            return reused.tile(shape, dtype, name=name, align_bytes=64, offset=slot * SLOT_BYTES)
+
+        def bank(shape, name, number):
+            return psum.tile(shape, F32, name=name, tag="bank%d" % number)
+
         def interleaved(ap):
-            return ap.rearrange("p (c e i) -> p c i e", e=4, i=PACK)
+            return ap.rearrange("p (c e i) -> p c i e", e=RUN, i=PACK)
 
         def planes(ap):
-            return ap.rearrange("p i (c e) -> p c i e", e=4)
+            return ap.rearrange("p i (c e) -> p c i e", e=RUN)
 
-        live = P - SCALE_ROWS
+        def group_offsets(first, count):
+            return offsets[:, first * LIST_COLS : (first + count) * LIST_COLS]
+
         scale_table = tile([P, T], U8, "scale_table")
         offsets = keep.tile([P, J // 16], U16, name="offsets")
         nc.sync.dma_start(offsets[:], offs)
         nc.sync.dma_start(
-            out=scale_table[live:P, :].bitcast(I32),
+            out=scale_table[FIRST_LIVE:P, :].bitcast(I32),
             in_=tab_scales.bitcast(I32).rearrange("d q w -> q d w"),
         )
-
-        x_rows = x.rearrange("(d p i) m -> d p i m", p=P, i=PACK)
-        x_raw = {}
-
-        def load_x(d, first, count, dst):
-            nc.sync.dma_start(out=dst[:], in_=x_rows[d][:, :, first * QUARTER : (first + count) * QUARTER])
-            x_raw[d, first] = dst
-
         word_table = tile([P, T], I32, "word_table")
         nc.sync.dma_start(out=word_table[:], in_=tab_words[0].rearrange("p t b -> p (t b)").bitcast(I32))
+        x_rows = x.rearrange("(d p i) m -> d p i m", p=P, i=PACK)
+        x_raw = {}
         for d in range(K_PASSES):
-            load_x(d, 0, 2, tile([P, PACK, HALF], F32, "x_left%d" % d))
+            x_raw[d, 0] = tile([P, PACK, HALF], F32, "x_left%d" % d)
+            nc.sync.dma_start(out=x_raw[d, 0][:], in_=x_rows[d][:, :, LEFT])
 
         warm = keep.tile([P, 8], F32, name="warm")
         nc.vector.memset(warm[:], 0.0)
         warm_out = keep.tile([P, 8], F32, name="warm_out")
         nc.scalar.activation(warm_out[:], warm[:], TANH)
 
-        nc.vector.memset(scale_table[0:live, :].bitcast(I32), 0)
+        nc.vector.memset(scale_table[0:FIRST_LIVE, :].bitcast(I32), 0)
         tab_planes = [tile([P, K_PASSES, 2 * PASS], U8, "tab_planes%d" % u) for u in range(2)]
         for u in range(2):
             nc.gpsimd.memset(tab_planes[u][:].rearrange("p d j -> p (d j)").bitcast(I32), 0)
         spread_scales = tile([P, PASS], U8, "spread_scales")
-        nc.gpsimd.memset(spread_scales[0:64, :].bitcast(I32), 0)
+        nc.gpsimd.memset(spread_scales[0:SPREAD_AT, :].bitcast(I32), 0)
 
         identity = tile([P, P], F32, "identity")
         nc.vector.memset(identity[:], 0.0)
         make_identity(nc, identity[:], nomemset=True)
 
-        picked_early = placed([P, len(LATE_X) * SLOT_BYTES], U8, "picked_early", 0)[:, 0 : 2 * PASS]
+        cw_rows = tile([P, PASS], F32, "cw_rows")
+        nc.vector.memset(cw_rows[:], 0.0)
+        nc.sync.dma_start(out=cw_rows[0 : CW_STEP * GROUPS : CW_STEP, :], in_=cw.rearrange("(a j) -> a j", a=GROUPS))
+        cw_psum = bank([P, PACK, P], "cw_psum", DOT_BANKS)
+        for i in range(PACK):
+            nc.tensor.transpose(cw_psum[:, i, :], cw_rows[:].rearrange("p (q i) -> p i q", i=PACK)[:, i, :], identity[:])
+
+        picked_early = tile_in_slot([P, K_PASSES * SLOT_BYTES], U8, "picked_early", 0)[:, 0 : 2 * PASS]
         picked_late = tile([P, 2 * PASS], U8, "picked_late")
         sorted_early = tile([P, 2 * PASS], U8, "sorted_early")
 
         def pick_scales(dst, first, count):
-            nc.vector.tensor_copy(dst, scale_table[:].indirect(offsets[:, first * LIST_COLS : (first + count) * LIST_COLS]))
+            nc.vector.tensor_copy(dst, scale_table[:].indirect(group_offsets(first, count)))
 
         def sort_scales(dst, src):
             nc.vector.tensor_copy(
@@ -124,73 +129,61 @@ def tile_list_kernl_tanh_none_kernel(
         sort_scales(sorted_early[:], picked_early)
         pick_scales(picked_late[:, PASS : 2 * PASS], 3, 1)
 
-        place_scales(tab_planes[0], sorted_early, live, 8)
-        for slot, (d, c) in enumerate(LATE_X):
-            load_x(d, c, 2, placed([P, PACK, HALF], F32, "x_late%d%d" % (d, c), slot))
+        place_scales(tab_planes[0], sorted_early, FIRST_LIVE, 4 * K_PASSES)
+        for d in range(K_PASSES):
+            x_raw[d, 1] = tile_in_slot([P, PACK, HALF], F32, "x_right%d" % d, d)
+            nc.sync.dma_start(out=x_raw[d, 1][:], in_=x_rows[d][:, :, RIGHT])
         nc.sync.dma_start(
-            out=spread_scales[64:P, :].bitcast(I32),
-            in_=picked_late[live:P, :].bitcast(I32).rearrange("p (a w) -> p a w", a=2),
+            out=spread_scales[SPREAD_AT:P, :].bitcast(I32),
+            in_=picked_late[FIRST_LIVE:P, :].bitcast(I32).rearrange("p (a w) -> p a w", a=2),
         )
-        cb_col = tile([P, J_PASSES, PACK], F32, "cb_col", tag="scale_table")
+        cb_col = tile([P, GROUPS, PACK], F32, "cb_col", tag="scale_table")
         nc.sync.dma_start(out=cb_col[:], in_=cb.rearrange("(a p i) -> p a i", p=P, i=PACK))
 
         x_codes = [tile([P, M], U32, "x_codes%d" % d) for d in range(K_PASSES)]
         x_planes = [tile([P, M], U8, "x_planes%d" % d) for d in range(K_PASSES)]
 
-        def quantise_x(d, h, grouped):
-            nc.vector.quantize_mx(
-                out=x_codes[d][:, h * HALF : (h + 1) * HALF].bitcast(FP8X4),
-                scales=x_planes[d][:, h * HALF : (h + 1) * HALF],
-                in_=grouped[:],
-            )
-
-        def prepare_x(d, h):
+        def quantise_x(d, h):
             grouped = tile([P, HALF * PACK], BF16, "x_grouped%d%d" % (d, h))
-            for (pass_, first), raw in x_raw.items():
-                if pass_ == d and first // 2 == h:
-                    at = (first % 2) * QUARTER * PACK
-                    nc.scalar.copy(interleaved(grouped[:, at : at + raw.shape[2] * PACK]), planes(raw[:]))
-            quantise_x(d, h, grouped)
+            nc.scalar.copy(interleaved(grouped[:]), planes(x_raw[d, h][:]))
+            cols = (LEFT, RIGHT)[h]
+            nc.vector.quantize_mx(out=x_codes[d][:, cols].bitcast(FP8X4), scales=x_planes[d][:, cols], in_=grouped[:])
 
-
-        tab_codes = {}
         picked_words = {}
+        tab_codes = {}
 
         def gather_words(a, dst):
             picked_words[a] = dst
-            nc.vector.tensor_copy(
-                picked_words[a][:],
-                word_table[:].bitcast(U32).indirect(offsets[:, a * LIST_COLS : (a + 1) * LIST_COLS]),
-            )
+            nc.vector.tensor_copy(dst[:], word_table[:].bitcast(U32).indirect(group_offsets(a, 1)))
 
         def part_words(a, dst):
             tab_codes[a] = dst
             nc.vector.tensor_copy(
-                tab_codes[a][:].bitcast(U16).rearrange("p (d h l q) -> p d h q l", d=2, h=2, l=2),
+                dst[:].bitcast(U16).rearrange("p (d h l q) -> p d h q l", d=2, h=2, l=2),
                 picked_words[a][:].bitcast(U16).rearrange("p (q h l d) -> p d h q l", d=2, h=2, l=2),
             )
 
         words_shape, codes_shape = [P, PASS], [P, K_PASSES * 2 * PASS]
         gather_words(0, tile(words_shape, U32, "picked_words0"))
-        cw_col = tile([P, J_PASSES, PACK], F32, "cw_col", tag="picked_late")
+        cw_col = tile([P, GROUPS, PACK], F32, "cw_col", tag="sorted_early")
         nc.sync.dma_start(out=cw_col[:], in_=cw.rearrange("(a p i) -> p a i", p=P, i=PACK))
         gather_words(1, tile(words_shape, U32, "picked_words1"))
-        prepare_x(0, 0)
+        quantise_x(0, 0)
         part_words(0, tile(codes_shape, U8, "tab_codes0", tag="x_left0"))
-        prepare_x(1, 0)
+        quantise_x(1, 0)
         part_words(1, tile(codes_shape, U8, "tab_codes1", tag="x_left1"))
         gather_words(2, tile(words_shape, U32, "picked_words2", tag="x_grouped10"))
         sorted_late = tile([P, PASS], U8, "sorted_late")
         sort_scales(sorted_late[:], spread_scales[:])
-        place_scales(tab_planes[1][:].rearrange("p d (a w) -> p (d a) w", a=2), sorted_late, 64, 16)
-        prepare_x(0, 1)
-        prepare_x(1, 1)
-        gather_words(3, placed(words_shape, U32, "picked_words3", 1))
+        place_scales(tab_planes[1][:].rearrange("p d (a w) -> p (d a) w", a=2), sorted_late, SPREAD_AT, 8 * K_PASSES)
+        quantise_x(0, 1)
+        quantise_x(1, 1)
+        gather_words(3, tile_in_slot(words_shape, U32, "picked_words3", 1))
         part_words(2, tile(codes_shape, U8, "tab_codes2", tag="x_grouped11"))
         part_words(3, tile(codes_shape, U8, "tab_codes3"))
 
         al_planes = sorted_late[:, 0:N]
-        al_codes = tile([P, J_PASSES, N], I32, "al_codes", tag="x_grouped01")
+        al_codes = tile([P, GROUPS, N], I32, "al_codes", tag="x_grouped01")
         for quad in range(4):
             nc.sync.dma_start(
                 out=al_planes[32 * quad : 32 * quad + 16, :].bitcast(I32),
@@ -198,124 +191,113 @@ def tile_list_kernl_tanh_none_kernel(
             )
         nc.sync.dma_start(out=al_codes[:], in_=al_words.rearrange("a p n i -> p a (n i)").bitcast(I32))
 
-        def first_product(dst, a, i, d, cols):
-            col = (d * PACK + i) * 2 * P
-            first = (a % 2) * PASS + i * P
-            nc.tensor.matmul_mx(
-                out=dst,
-                lhsT=tab_codes[a][:, col : col + 2 * P].bitcast(FP4X4),
-                lhsT_scale=tab_planes[a // 2][:, d, first : first + P],
-                rhs=x_codes[d][:, cols].bitcast(FP8X4),
-                rhs_scale=x_planes[d][:, cols],
-                start=(d == 0),
-                stop=(d == K_PASSES - 1),
+        h_codes = [tile([P, M], U32, "h_codes%d" % a) for a in range(GROUPS)]
+        h_planes = [tile([P, M], U8, "h_planes%d" % a) for a in range(GROUPS)]
+
+        def dot_products(dst, a, i, cols):
+            for d in range(K_PASSES):
+                word = (d * PACK + i) * 2 * P
+                byte = (a % 2) * PASS + i * P
+                nc.tensor.matmul_mx(
+                    out=dst,
+                    lhsT=tab_codes[a][:, word : word + 2 * P].bitcast(FP4X4),
+                    lhsT_scale=tab_planes[a // 2][:, d, byte : byte + P],
+                    rhs=x_codes[d][:, cols].bitcast(FP8X4),
+                    rhs_scale=x_planes[d][:, cols],
+                    start=(d == 0),
+                    stop=(d == K_PASSES - 1),
+                )
+
+        def dots_whole(a, first_bank):
+            dots = []
+            for i in range(PACK):
+                dots.append(bank([P, M], "dots%d_%d" % (a, i), (first_bank + i) % DOT_BANKS))
+                dot_products(dots[i][:], a, i, slice(0, M))
+            return dots
+
+        def dots_half(a, h, first_bank):
+            dots = []
+            for i in range(PACK):
+                dots.append(bank([P, HALF], "dots%d_%d%d" % (a, h, i), (first_bank + i) % DOT_BANKS))
+                for c in range(2):
+                    at = h * HALF + c * QUARTER
+                    dot_products(dots[i][:, c * QUARTER : (c + 1) * QUARTER], a, i, slice(at, at + QUARTER))
+            return dots
+
+        def tanh(a, dots, name):
+            kern = tile([P, PACK, dots[0].shape[1]], F32, name)
+            for i in range(PACK):
+                nc.scalar.activation(kern[:, i, :], dots[i][:], TANH, bias=cb_col[:, a, i : i + 1])
+            return kern
+
+        def grouped_tile(width, name, tag=None):
+            return tile([P, width * PACK], BF16, name, tag=tag)
+
+        def weigh_on_vector(dst, kern, a):
+            weights = cw_psum[:, :, CW_STEP * a].unsqueeze(1).unsqueeze(3).to_broadcast([P, kern.shape[2] // RUN, PACK, RUN])
+            nc.vector.tensor_tensor(interleaved(dst), planes(kern), weights, MULT)
+
+        def weigh_on_gpsimd(dst, kern, a):
+            nc.gpsimd.tensor_tensor(
+                dst.rearrange("p (m i) -> p m i", i=PACK),
+                kern.rearrange("p i m -> p m i"),
+                cw_col[:, a, :].unsqueeze(1).to_broadcast([P, kern.shape[2], PACK]),
+                MULT,
             )
 
-        h_codes = [tile([P, M], U32, "h_codes%d" % a) for a in range(J_PASSES)]
-        h_planes = [tile([P, M], U8, "h_planes%d" % a) for a in range(J_PASSES)]
+        def quantise_h(a, cols, grouped):
+            nc.vector.quantize_mx(out=h_codes[a][:, cols].bitcast(FP8X4), scales=h_planes[a][:, cols], in_=grouped[:])
 
-        def quantise_h(a, grouped, q0, qw):
-            nc.vector.quantize_mx(
-                out=h_codes[a][:, q0 : q0 + qw].bitcast(FP8X4), scales=h_planes[a][:, q0 : q0 + qw], in_=grouped[:]
-            )
+        dots = [dots_half(0, h, PACK * h) for h in range(2)]
+        kern0 = [tanh(0, dots[h], "kern0_%d" % h) for h in range(2)]
+        left0 = grouped_tile(HALF, "left0")
+        right0 = grouped_tile(HALF, "right0", tag="before_gpsimd")
+        weigh_on_vector(left0[:], kern0[0][:], 0)
+        weigh_on_vector(right0[:], kern0[1][:], 0)
+        quantise_h(0, LEFT, left0)
+        quantise_h(0, RIGHT, right0)
 
-        for a in range(J_PASSES):
-            dots = {}
-            if a in (0, J_PASSES - 1):
-                for h in range(2):
-                    for i in range(PACK):
-                        half = psum.tile([P, HALF], F32, name="dots%d_%d%d" % (a, h, i), tag="bank%d" % ((4 * (h if a == 0 else a + 1) + i) % DOT_BANKS))
-                        for c in range(2):
-                            for d in range(K_PASSES):
-                                at = h * HALF + c * QUARTER
-                                first_product(half[:, c * QUARTER : (c + 1) * QUARTER], a, i, d, slice(at, at + QUARTER))
-                        dots[i, h * HALF] = half[:]
-            else:
-                for i in range(PACK):
-                    whole = psum.tile([P, M], F32, name="dots%d_%d" % (a, i), tag="bank%d" % ((4 * (a + 1) + i) % DOT_BANKS))
-                    for d in range(K_PASSES):
-                        first_product(whole[:], a, i, d, slice(0, M))
-                    for m0, width in TANH_PIECES[a]:
-                        dots[i, m0] = whole[:, m0 : m0 + width]
+        kern1 = tanh(1, dots_whole(1, 2 * PACK), "kern1")
+        left1 = grouped_tile(HALF, "left1", tag="before_gpsimd")
+        right1 = grouped_tile(HALF, "right1")
+        side = GPSIMD_COLS[1]
+        weigh_on_vector(right1[:], kern1[:, :, RIGHT], 1)
+        weigh_on_gpsimd(left1[:, 0 : side * PACK], kern1[:, :, 0:side], 1)
+        weigh_on_vector(left1[:, side * PACK :], kern1[:, :, side:HALF], 1)
+        quantise_h(1, RIGHT, right1)
+        quantise_h(1, LEFT, left1)
 
-            kern = {}
-            for m0, width in TANH_PIECES[a]:
-                piece = tile([P, PACK, width], F32, "kern%d_%d" % (a, m0))
-                for i in range(PACK):
-                    nc.scalar.activation(piece[:, i, :], dots[i, m0], TANH, bias=cb_col[:, a, i : i + 1])
-                for w0, w, engine in WEIGH_PIECES[a]:
-                    if m0 <= w0 < m0 + width:
-                        kern[w0] = piece[:, :, w0 - m0 : w0 - m0 + w]
-                        if engine == "scalar":
-                            rounded = tile([P, PACK, w], BF16, "rounded%d_%d" % (a, w0))
-                            for i in range(PACK):
-                                nc.scalar.activation(rounded[:, i, :], kern[w0][:, i, :], COPY, scale=cw_col[:, a, i : i + 1])
-                            kern[w0] = rounded[:]
+        kern2 = tanh(2, dots_whole(2, 3 * PACK), "kern2")
+        left2 = grouped_tile(HALF, "left2")
+        right2 = grouped_tile(HALF, "right2", tag="before_gpsimd")
+        side = GPSIMD_COLS[2]
+        weigh_on_vector(left2[:], kern2[:, :, LEFT], 2)
+        weigh_on_gpsimd(right2[:, 0 : side * PACK], kern2[:, :, HALF : HALF + side], 2)
 
-            if a == 1:
-                cw_rows = x_raw[LATE_X[0]][:].rearrange("p i m -> p (i m)")[:, 0:PASS]
-                nc.sync.dma_start(out=cw_rows[0:J_PASSES, :], in_=cw.rearrange("(a j) -> a j", a=J_PASSES))
-                cw_psum = psum.tile([P, PACK, P], F32, name="cw_psum", tag="bank7")
-                for i in range(PACK):
-                    nc.tensor.transpose(cw_psum[:, i, :], cw_rows.rearrange("p (q i) -> p i q", i=PACK)[:, i, :], identity[:])
+        dots = [dots_half(3, h, 4 * PACK) for h in range(2)]
+        kern3 = [tanh(3, dots[h], "kern3_%d" % h) for h in range(2)]
+        rounded = tile([P, PACK, HALF], BF16, "rounded")
+        for i in range(PACK):
+            nc.scalar.activation(rounded[:, i, :], kern3[1][:, i, :], COPY, scale=cw_col[:, 3, i : i + 1])
+        left3 = grouped_tile(HALF, "left3")
+        third3 = grouped_tile(QUARTER, "third3")
+        fourth3 = grouped_tile(QUARTER, "fourth3")
+        weigh_on_vector(left3[:], kern3[0][:], 3)
+        weigh_on_vector(right2[:, side * PACK :], kern2[:, :, HALF + side : M], 2)
+        quantise_h(2, LEFT, left2)
+        quantise_h(3, LEFT, left3)
+        quantise_h(2, RIGHT, right2)
+        nc.vector.tensor_copy(interleaved(third3[:]), planes(rounded[:, :, 0:QUARTER]))
+        nc.scalar.copy(interleaved(fourth3[:]), planes(rounded[:, :, QUARTER:HALF]))
+        quantise_h(3, THIRD, third3)
+        quantise_h(3, FOURTH, fourth3)
 
-            h_grouped = {}
-            for q0, qw in QUANT_PIECES[a]:
-                shared = (a, q0) in [(0, HALF), (1, 0), (2, HALF)]
-                h_grouped[q0] = tile([P, qw * PACK], BF16, "h_grouped%d_%d" % (a, q0), tag="h_shared" if shared else None)
+        y_left = bank([P, 2, HALF], "y_left", 6)
+        y_third = bank([P, 2, QUARTER], "y_third", 0)
+        y_fourth = [bank([P, QUARTER], "y_fourth%d" % g, 1 + g) for g in range(2)]
+        last = GROUPS - 1
 
-            def weigh(q0, qw, engines=("vector", "scalar", "gpsimd"), group=(a, kern, h_grouped)):
-                a, kern, h_grouped = group
-                for w0, w, engine in WEIGH_PIECES[a]:
-                    lo, hi = max(q0, w0), min(q0 + qw, w0 + w)
-                    if lo >= hi or engine not in engines:
-                        continue
-                    dst = interleaved(h_grouped[q0][:, (lo - q0) * PACK : (hi - q0) * PACK])
-                    src = planes(kern[w0][:, :, lo - w0 : hi - w0])
-                    if engine == "scalar" and lo == HALF + QUARTER:
-                        nc.scalar.copy(dst, src)
-                    elif engine == "scalar":
-                        nc.vector.tensor_copy(dst, src)
-                    elif engine == "gpsimd":
-                        nc.gpsimd.tensor_tensor(
-                            h_grouped[q0][:, (lo - q0) * PACK : (hi - q0) * PACK].rearrange("p (m i) -> p m i", i=PACK),
-                            kern[w0][:, :, lo - w0 : hi - w0].rearrange("p i m -> p m i"),
-                            cw_col[:, a, :].unsqueeze(1).to_broadcast([P, hi - lo, PACK]),
-                            MULT,
-                        )
-                    else:
-                        column = cw_psum[:, :, a] if a > 0 else cw_col[:, a, :]
-                        weights = column.unsqueeze(1).unsqueeze(3).to_broadcast([P, (hi - lo) // 4, PACK, 4])
-                        nc.vector.tensor_tensor(dst, src, weights, MULT)
-
-
-            pieces = QUANT_PIECES[a]
-            if a < 2:
-                ordered = pieces if a == 0 else pieces[::-1]
-                for piece_now in ordered:
-                    weigh(*piece_now)
-                for piece_now in ordered:
-                    quantise_h(a, h_grouped[piece_now[0]], *piece_now)
-            elif a == 2:
-                weigh(*pieces[0])
-                weigh(*pieces[1], engines=("gpsimd",))
-                held = (a, kern, h_grouped)
-            else:
-                weigh(*pieces[0])
-                weigh(HALF, HALF, engines=("vector",), group=held)
-                quantise_h(2, held[2][0], 0, HALF)
-                quantise_h(a, h_grouped[0], *pieces[0])
-                quantise_h(2, held[2][HALF], HALF, HALF)
-                for piece_now in pieces[1:]:
-                    weigh(*piece_now)
-                for piece_now in pieces[1:]:
-                    quantise_h(a, h_grouped[piece_now[0]], *piece_now)
-
-        y_left = psum.tile([P, 2, HALF], F32, name="y_left", tag="bank6")
-        y_third = psum.tile([P, 2, QUARTER], F32, name="y_third", tag="bank0")
-        y_last = [psum.tile([P, QUARTER], F32, name="y_last%d" % g, tag="bank%d" % (1 + g)) for g in range(2)]
-
-        def second_product(dst, a, g, cols, start, stop):
+        def add_pass(dst, a, g, cols, start, stop):
             nc.tensor.matmul_mx(
                 out=dst,
                 lhsT=al_codes[:, a, g * P : (g + 1) * P].bitcast(FP8X4),
@@ -326,41 +308,36 @@ def tile_list_kernl_tanh_none_kernel(
                 stop=stop,
             )
 
-        last = J_PASSES - 1
-        def add_left(a):
+        def add_shared(y, a, cols):
             for g in range(2):
-                second_product(y_left[:, g, :], a, g, slice(0, HALF), a == 0 and g == 0, a == last and g == 1)
+                add_pass(y[:, g, :], a, g, cols, a == 0 and g == 0, a == last and g == 1)
 
-        def add_third(a):
-            for g in range(2):
-                second_product(y_third[:, g, :], a, g, slice(HALF, HALF + QUARTER), a == 0 and g == 0, a == last and g == 1)
+        def add_fourth(a, g):
+            add_pass(y_fourth[g][:], a, g, FOURTH, a == 0, a == last)
 
-        def add_last(a, g):
-            second_product(y_last[g][:], a, g, slice(HALF + QUARTER, M), a == 0, a == last)
-
-        for a in range(2):
-            add_left(a)
-            add_third(a)
-            add_last(a, 0)
-        add_left(2)
-        add_left(3)
-        for a in range(2):
-            add_last(a, 1)
+        for a in (0, 1):
+            add_shared(y_left, a, LEFT)
+            add_shared(y_third, a, THIRD)
+            add_fourth(a, 0)
         for a in (2, 3):
-            add_third(a)
+            add_shared(y_left, a, LEFT)
+        for a in (0, 1):
+            add_fourth(a, 1)
+        for a in (2, 3):
+            add_shared(y_third, a, THIRD)
             for g in range(2):
-                add_last(a, g)
+                add_fourth(a, g)
 
         out_rows = out.rearrange("(g p) m -> p g m", p=P)
         for g in range(2):
             result_left = keep.tile([P, HALF], F32, name="result_left%d" % g)
             nc.scalar.copy(result_left[:], y_left[:, g, :])
-            nc.sync.dma_start(out=out_rows[:, g, 0:HALF], in_=result_left[:])
+            nc.sync.dma_start(out=out_rows[:, g, LEFT], in_=result_left[:])
         result_third = keep.tile([P, 2, QUARTER], F32, name="result_third")
         nc.scalar.copy(result_third[:], y_third[:])
-        nc.sync.dma_start(out=out_rows[:, :, HALF : HALF + QUARTER], in_=result_third[:])
-        result_last = [keep.tile([P, QUARTER], F32, name="result_last%d" % g) for g in range(2)]
-        nc.scalar.copy(result_last[0][:], y_last[0][:])
-        nc.scalar.dma_start(out=out_rows[:, 0, HALF + QUARTER : M], in_=result_last[0][:])
-        nc.vector.tensor_copy(result_last[1][:], y_last[1][:])
-        nc.sync.dma_start(out=out_rows[:, 1, HALF + QUARTER : M], in_=result_last[1][:])
+        nc.sync.dma_start(out=out_rows[:, :, THIRD], in_=result_third[:])
+        result_fourth = [keep.tile([P, QUARTER], F32, name="result_fourth%d" % g) for g in range(2)]
+        nc.scalar.copy(result_fourth[0][:], y_fourth[0][:])
+        nc.scalar.dma_start(out=out_rows[:, 0, FOURTH], in_=result_fourth[0][:])
+        nc.vector.tensor_copy(result_fourth[1][:], y_fourth[1][:])
+        nc.sync.dma_start(out=out_rows[:, 1, FOURTH], in_=result_fourth[1][:])

@@ -17,6 +17,7 @@ FP4X4 = mybir.dt.float4_e2m1fn_x4
 TANH = mybir.ActivationFunctionType.Tanh
 COPY = mybir.ActivationFunctionType.Copy
 MULT = mybir.AluOpType.mult
+ADD = mybir.AluOpType.add
 
 P = 128
 PACK = 4
@@ -25,19 +26,15 @@ K_PASSES = K // PASS
 GROUPS = J // PASS
 HALF = M // 2
 QUARTER = M // 4
-LEFT = slice(0, HALF)
-RIGHT = slice(HALF, M)
-THIRD = slice(HALF, HALF + QUARTER)
-FOURTH = slice(HALF + QUARTER, M)
 LIST_COLS = PASS // 16
 RUN = 4
 SCALE_ROWS = K // 32
 FIRST_LIVE = P - SCALE_ROWS
-SPREAD_AT = 64
-SLOT_BYTES = PACK * HALF * 4
 DOT_BANKS = 7
-CW_STEP = 4
-GPSIMD_COLS = {1: 104, 2: 160}
+ROW_STEP = 4
+KIB = 1024
+GPSIMD_COLS = (184, 176, 176)
+AT_X_LEFT1, AT_X_FOURTH, AT_X_RIGHT0, AT_X_THIRD, AT_CW = 0, 5, 10, 14, (24, 32, 36)
 
 
 def tile_list_kernl_tanh_none_kernel(
@@ -52,8 +49,8 @@ def tile_list_kernl_tanh_none_kernel(
         def tile(shape, dtype, name, tag=None):
             return keep.tile(shape, dtype, name=name, tag=tag or name, align_bytes=64)
 
-        def tile_in_slot(shape, dtype, name, slot):
-            return reused.tile(shape, dtype, name=name, align_bytes=64, offset=slot * SLOT_BYTES)
+        def tile_at(shape, dtype, name, kib):
+            return reused.tile(shape, dtype, name=name, align_bytes=64, offset=int(kib * KIB))
 
         def bank(shape, name, number):
             return psum.tile(shape, F32, name=name, tag="bank%d" % number)
@@ -63,6 +60,9 @@ def tile_list_kernl_tanh_none_kernel(
 
         def planes(ap):
             return ap.rearrange("p i (c e) -> p c i e", e=RUN)
+
+        def by_slot(ap):
+            return ap.rearrange("p (i m) -> p i m", i=PACK)
 
         def group_offsets(first, count):
             return offsets[:, first * LIST_COLS : (first + count) * LIST_COLS]
@@ -78,36 +78,39 @@ def tile_list_kernl_tanh_none_kernel(
         nc.sync.dma_start(out=word_table[:], in_=tab_words[0].rearrange("p t b -> p (t b)").bitcast(I32))
         x_rows = x.rearrange("(d p i) m -> d p i m", p=P, i=PACK)
         x_raw = {}
+        x_raw[0, 0] = tile([P, PACK, HALF], F32, "x_left0")[:]
+        x_raw[1, 0] = tile_at([P, PACK, HALF], F32, "x_left1", AT_X_LEFT1)[:]
         for d in range(K_PASSES):
-            x_raw[d, 0] = tile([P, PACK, HALF], F32, "x_left%d" % d)
-            nc.sync.dma_start(out=x_raw[d, 0][:], in_=x_rows[d][:, :, LEFT])
+            nc.sync.dma_start(out=x_raw[d, 0], in_=x_rows[d][:, :, 0:HALF])
 
         warm = keep.tile([P, 8], F32, name="warm")
         nc.vector.memset(warm[:], 0.0)
         warm_out = keep.tile([P, 8], F32, name="warm_out")
         nc.scalar.activation(warm_out[:], warm[:], TANH)
 
+        rows = tile([P, PASS], F32, "rows")
+        nc.gpsimd.memset(rows[:], 0.0)
+        for r, vec in enumerate((cw, cb)):
+            first = r * GROUPS * ROW_STEP
+            nc.gpsimd.dma_start(
+                out=rows[first : first + GROUPS * ROW_STEP : ROW_STEP, :], in_=vec.rearrange("(a j) -> a j", a=GROUPS)
+            )
         nc.vector.memset(scale_table[0:FIRST_LIVE, :].bitcast(I32), 0)
         tab_planes = [tile([P, K_PASSES, 2 * PASS], U8, "tab_planes%d" % u) for u in range(2)]
         for u in range(2):
             nc.gpsimd.memset(tab_planes[u][:].rearrange("p d j -> p (d j)").bitcast(I32), 0)
-        spread_scales = tile([P, PASS], U8, "spread_scales")
-        nc.gpsimd.memset(spread_scales[0:SPREAD_AT, :].bitcast(I32), 0)
-
         identity = tile([P, P], F32, "identity")
         nc.vector.memset(identity[:], 0.0)
         make_identity(nc, identity[:], nomemset=True)
-
-        cw_rows = tile([P, PASS], F32, "cw_rows")
-        nc.vector.memset(cw_rows[:], 0.0)
-        nc.sync.dma_start(out=cw_rows[0 : CW_STEP * GROUPS : CW_STEP, :], in_=cw.rearrange("(a j) -> a j", a=GROUPS))
-        cw_psum = bank([P, PACK, P], "cw_psum", DOT_BANKS)
+        turned = bank([P, PACK, P], "turned", DOT_BANKS)
         for i in range(PACK):
-            nc.tensor.transpose(cw_psum[:, i, :], cw_rows[:].rearrange("p (q i) -> p i q", i=PACK)[:, i, :], identity[:])
-
-        picked_early = tile_in_slot([P, K_PASSES * SLOT_BYTES], U8, "picked_early", 0)[:, 0 : 2 * PASS]
-        picked_late = tile([P, 2 * PASS], U8, "picked_late")
-        sorted_early = tile([P, 2 * PASS], U8, "sorted_early")
+            nc.tensor.transpose(turned[:, i, :], rows[:].rearrange("p (q i) -> p i q", i=PACK)[:, i, :], identity[:])
+        cols = tile([P, 2 * GROUPS, PACK], F32, "cols")
+        nc.scalar.copy(cols[:], turned[:, :, 0 : 2 * GROUPS * ROW_STEP : ROW_STEP].rearrange("p i r -> p r i"))
+        cw_own = []
+        for w, width in enumerate((8, 4, 1)):
+            cw_own.append(tile_at([P, width * KIB // 4], F32, "cw_own%d" % w, AT_CW[w])[:, 0:PACK])
+            nc.gpsimd.tensor_copy(cw_own[w], cols[:, w, :])
 
         def pick_scales(dst, first, count):
             nc.vector.tensor_copy(dst, scale_table[:].indirect(group_offsets(first, count)))
@@ -117,37 +120,39 @@ def tile_list_kernl_tanh_none_kernel(
                 dst.rearrange("p (a i q) -> p a i q", i=PACK, q=P), src.rearrange("p (a q i) -> p a i q", i=PACK, q=P)
             )
 
-        def place_scales(dst, src, first, rows):
+        def place_scales(dst, src):
+            rows_a_quad = 4 * K_PASSES
             for quad in (0, 2, 1, 3):
+                at = FIRST_LIVE + rows_a_quad * quad
                 nc.sync.dma_start(
-                    out=dst[32 * quad : 32 * quad + 4, :, :].bitcast(I32),
-                    in_=src[first + rows * quad : first + rows * (quad + 1), :].bitcast(I32),
+                    out=dst[32 * quad : 32 * quad + 4, :, :].bitcast(I32), in_=src[at : at + rows_a_quad, :].bitcast(I32)
                 )
 
-        pick_scales(picked_early, 0, 2)
-        pick_scales(picked_late[:, 0:PASS], 2, 1)
-        sort_scales(sorted_early[:], picked_early)
-        pick_scales(picked_late[:, PASS : 2 * PASS], 3, 1)
-
-        place_scales(tab_planes[0], sorted_early, FIRST_LIVE, 4 * K_PASSES)
-        for d in range(K_PASSES):
-            x_raw[d, 1] = tile_in_slot([P, PACK, HALF], F32, "x_right%d" % d, d)
-            nc.sync.dma_start(out=x_raw[d, 1][:], in_=x_rows[d][:, :, RIGHT])
-        nc.sync.dma_start(
-            out=spread_scales[SPREAD_AT:P, :].bitcast(I32),
-            in_=picked_late[FIRST_LIVE:P, :].bitcast(I32).rearrange("p (a w) -> p a w", a=2),
-        )
-        cb_col = tile([P, GROUPS, PACK], F32, "cb_col", tag="scale_table")
-        nc.sync.dma_start(out=cb_col[:], in_=cb.rearrange("(a p i) -> p a i", p=P, i=PACK))
+        picked01 = tile_at([P, 6 * KIB], U8, "picked01", AT_X_RIGHT0 - 1)[:, 0 : 2 * PASS]
+        picked2 = tile([P, PASS], U8, "picked2")
+        sorted01 = tile([P, 2 * PASS], U8, "sorted01")
+        pick_scales(picked01, 0, 2)
+        pick_scales(picked2[:], 2, 1)
+        sort_scales(sorted01[:], picked01)
+        place_scales(tab_planes[0], sorted01)
+        x_raw[0, 1] = tile_at([P, PACK, HALF], F32, "x_right0", AT_X_RIGHT0)[:]
+        x_third = by_slot(tile_at([P, 5 * KIB // 4], F32, "x_third", AT_X_THIRD)[:, 0 : PACK * QUARTER])
+        x_fourth = by_slot(tile_at([P, 5 * KIB // 4], F32, "x_fourth", AT_X_FOURTH)[:, 0 : PACK * QUARTER])
+        nc.sync.dma_start(out=x_raw[0, 1], in_=x_rows[0][:, :, HALF:M])
+        nc.sync.dma_start(out=x_third, in_=x_rows[1][:, :, HALF : HALF + QUARTER])
+        nc.sync.dma_start(out=x_fourth, in_=x_rows[1][:, :, HALF + QUARTER : M])
 
         x_codes = [tile([P, M], U32, "x_codes%d" % d) for d in range(K_PASSES)]
         x_planes = [tile([P, M], U8, "x_planes%d" % d) for d in range(K_PASSES)]
+        x_grouped = {}
+
+        def cast_x(d, h):
+            x_grouped[d, h] = tile([P, HALF * PACK], BF16, "x_grouped%d%d" % (d, h))
+            nc.scalar.copy(interleaved(x_grouped[d, h][:]), planes(x_raw[d, h]))
 
         def quantise_x(d, h):
-            grouped = tile([P, HALF * PACK], BF16, "x_grouped%d%d" % (d, h))
-            nc.scalar.copy(interleaved(grouped[:]), planes(x_raw[d, h][:]))
-            cols = (LEFT, RIGHT)[h]
-            nc.vector.quantize_mx(out=x_codes[d][:, cols].bitcast(FP8X4), scales=x_planes[d][:, cols], in_=grouped[:])
+            at = slice(h * HALF, (h + 1) * HALF)
+            nc.vector.quantize_mx(out=x_codes[d][:, at].bitcast(FP8X4), scales=x_planes[d][:, at], in_=x_grouped[d, h][:])
 
         picked_words = {}
         tab_codes = {}
@@ -163,27 +168,85 @@ def tile_list_kernl_tanh_none_kernel(
                 picked_words[a][:].bitcast(U16).rearrange("p (q h l d) -> p d h q l", d=2, h=2, l=2),
             )
 
-        words_shape, codes_shape = [P, PASS], [P, K_PASSES * 2 * PASS]
+        h_codes = {}
+        h_planes = {}
+        units_done = []
+
+        def first_stage(a, at, name, kib=None):
+            shape = [P, PACK, at.stop - at.start]
+            dst = tile(shape, F32, name) if kib is None else tile_at(shape, F32, name, kib)
+            for i in range(PACK):
+                number = (PACK * len(units_done) + i) % DOT_BANKS
+                dots = bank([P, shape[2]], "dots_%s_%d" % (name, i), number)
+                for d in range(K_PASSES):
+                    word = (d * PACK + i) * 2 * P
+                    byte = (a % 2) * PASS + i * P
+                    nc.tensor.matmul_mx(
+                        out=dots[:],
+                        lhsT=tab_codes[a][:, word : word + 2 * P].bitcast(FP4X4),
+                        lhsT_scale=tab_planes[a // 2][:, d, byte : byte + P],
+                        rhs=x_codes[d][:, at].bitcast(FP8X4),
+                        rhs_scale=x_planes[d][:, at],
+                        start=(d == 0),
+                        stop=(d == K_PASSES - 1),
+                    )
+                nc.scalar.activation(dst[:, i, :], dots[:], TANH, bias=cols[:, GROUPS + a, i : i + 1])
+            units_done.append(name)
+            return dst
+
+        def weigh_on_vector(dst, src, a):
+            weights = turned[:, :, ROW_STEP * a].unsqueeze(1).unsqueeze(3).to_broadcast([P, src.shape[2] // RUN, PACK, RUN])
+            nc.vector.tensor_tensor(interleaved(dst), planes(src), weights, MULT)
+
+        def weigh_shared(dst, src, a, w):
+            side = GPSIMD_COLS[w]
+            nc.gpsimd.tensor_tensor(
+                dst[:, 0 : side * PACK].rearrange("p (m i) -> p m i", i=PACK),
+                src[:, :, 0:side].rearrange("p i m -> p m i"),
+                cw_own[w].unsqueeze(1).to_broadcast([P, side, PACK]),
+                MULT,
+            )
+            weigh_on_vector(dst[:, side * PACK :], src[:, :, side:HALF], a)
+
+        def quantise_h(key, src, codes=None, plane=None):
+            width = src.shape[1] // PACK
+            name = "%d%d" % key
+            h_codes[key] = codes if codes is not None else tile([P, width], U32, "h_codes" + name)
+            h_planes[key] = plane if plane is not None else tile([P, width], U8, "h_plane" + name)
+            nc.vector.quantize_mx(out=h_codes[key][:].bitcast(FP8X4), scales=h_planes[key][:], in_=src)
+
+        words_shape, codes_shape, grouped_shape = [P, PASS], [P, K_PASSES * 2 * PASS], [P, HALF * PACK]
+        left, right = slice(0, HALF), slice(HALF, M)
         gather_words(0, tile(words_shape, U32, "picked_words0"))
-        cw_col = tile([P, GROUPS, PACK], F32, "cw_col", tag="sorted_early")
-        nc.sync.dma_start(out=cw_col[:], in_=cw.rearrange("(a p i) -> p a i", p=P, i=PACK))
         gather_words(1, tile(words_shape, U32, "picked_words1"))
+        cast_x(0, 0)
         quantise_x(0, 0)
         part_words(0, tile(codes_shape, U8, "tab_codes0", tag="x_left0"))
+        cast_x(1, 0)
         quantise_x(1, 0)
-        part_words(1, tile(codes_shape, U8, "tab_codes1", tag="x_left1"))
-        gather_words(2, tile(words_shape, U32, "picked_words2", tag="x_grouped10"))
-        sorted_late = tile([P, PASS], U8, "sorted_late")
-        sort_scales(sorted_late[:], spread_scales[:])
-        place_scales(tab_planes[1][:].rearrange("p d (a w) -> p (d a) w", a=2), sorted_late, SPREAD_AT, 8 * K_PASSES)
+        part_words(1, tile_at(codes_shape, U8, "tab_codes1", AT_X_LEFT1))
+        picked3 = tile_at([P, PASS], U8, "picked3", AT_X_LEFT1 + 3)
+        pick_scales(picked3[:], 3, 1)
+        cast_x(0, 1)
+        x_grouped[1, 1] = tile(grouped_shape, BF16, "x_grouped11", tag="picked_words1")
+        nc.scalar.copy(interleaved(x_grouped[1, 1][:, 0 : QUARTER * PACK]), planes(x_third))
+        nc.gpsimd.tensor_scalar(
+            x_grouped[1, 1][:, QUARTER * PACK :].rearrange("p (m i) -> p m i", i=PACK),
+            x_fourth.rearrange("p i m -> p m i"),
+            1.0,
+            0.0,
+            MULT,
+            ADD,
+        )
         quantise_x(0, 1)
         quantise_x(1, 1)
-        gather_words(3, tile_in_slot(words_shape, U32, "picked_words3", 1))
-        part_words(2, tile(codes_shape, U8, "tab_codes2", tag="x_grouped11"))
-        part_words(3, tile(codes_shape, U8, "tab_codes3"))
+        sorted23 = tile_at([P, 2 * PASS], U8, "sorted23", AT_X_FOURTH + 4)
+        sort_scales(sorted23[:, 0:PASS], picked2[:])
+        sort_scales(sorted23[:, PASS : 2 * PASS], picked3[:])
+        place_scales(tab_planes[1], sorted23)
 
-        al_planes = sorted_late[:, 0:N]
-        al_codes = tile([P, GROUPS, N], I32, "al_codes", tag="x_grouped01")
+        al_planes = sorted23[:, 0:N]
+        al_codes = tile([P, GROUPS, N], I32, "al_codes", tag="x_grouped10")
         for quad in range(4):
             nc.sync.dma_start(
                 out=al_planes[32 * quad : 32 * quad + 16, :].bitcast(I32),
@@ -191,153 +254,106 @@ def tile_list_kernl_tanh_none_kernel(
             )
         nc.sync.dma_start(out=al_codes[:], in_=al_words.rearrange("a p n i -> p a (n i)").bitcast(I32))
 
-        h_codes = [tile([P, M], U32, "h_codes%d" % a) for a in range(GROUPS)]
-        h_planes = [tile([P, M], U8, "h_planes%d" % a) for a in range(GROUPS)]
+        gather_words(2, tile_at(words_shape, U32, "picked_words2", AT_X_FOURTH))
+        gather_words(3, tile_at(words_shape, U32, "picked_words3", AT_X_FOURTH + 2))
+        kern00 = first_stage(0, left, "kern00", AT_X_THIRD)
+        kern10 = first_stage(1, left, "kern10", AT_X_THIRD + 4)
+        kern01 = first_stage(0, right, "kern01")
+        kern11 = first_stage(1, right, "kern11")
+        grouped00 = tile_at(grouped_shape, BF16, "grouped00", AT_X_LEFT1 + 3)
+        weigh_shared(grouped00, kern00, 0, 0)
 
-        def dot_products(dst, a, i, cols):
-            for d in range(K_PASSES):
-                word = (d * PACK + i) * 2 * P
-                byte = (a % 2) * PASS + i * P
-                nc.tensor.matmul_mx(
-                    out=dst,
-                    lhsT=tab_codes[a][:, word : word + 2 * P].bitcast(FP4X4),
-                    lhsT_scale=tab_planes[a // 2][:, d, byte : byte + P],
-                    rhs=x_codes[d][:, cols].bitcast(FP8X4),
-                    rhs_scale=x_planes[d][:, cols],
-                    start=(d == 0),
-                    stop=(d == K_PASSES - 1),
-                )
+        part_words(2, tile_at(codes_shape, U8, "tab_codes2", AT_CW[0]))
+        part_words(3, tile_at(codes_shape, U8, "tab_codes3", AT_CW[0] + 2))
+        quantise_h((0, 0), grouped00[:])
 
-        def dots_whole(a, first_bank):
-            dots = []
-            for i in range(PACK):
-                dots.append(bank([P, M], "dots%d_%d" % (a, i), (first_bank + i) % DOT_BANKS))
-                dot_products(dots[i][:], a, i, slice(0, M))
-            return dots
+        grouped01 = tile_at(grouped_shape, BF16, "grouped01", AT_CW[0] + 6)
+        weigh_on_vector(grouped01[:], kern01[:], 0)
+        grouped10 = tile_at(grouped_shape, BF16, "grouped10", AT_X_LEFT1 + 3)
+        weigh_shared(grouped10, kern10, 1, 1)
+        grouped11 = tile_at(grouped_shape, BF16, "grouped11", AT_CW[0] + 4)
+        weigh_on_vector(grouped11[:], kern11[:], 1)
 
-        def dots_half(a, h, first_bank):
-            dots = []
-            for i in range(PACK):
-                dots.append(bank([P, HALF], "dots%d_%d%d" % (a, h, i), (first_bank + i) % DOT_BANKS))
-                for c in range(2):
-                    at = h * HALF + c * QUARTER
-                    dot_products(dots[i][:, c * QUARTER : (c + 1) * QUARTER], a, i, slice(at, at + QUARTER))
-            return dots
+        quantise_h((0, 1), grouped01[:], tile_at([P, HALF], U32, "h_codes01", AT_CW[1] + 1))
+        quantise_h((1, 1), grouped11[:], tile_at([P, HALF], U32, "h_codes11", AT_CW[1]))
+        quantise_h((1, 0), grouped10[:])
 
-        def tanh(a, dots, name):
-            kern = tile([P, PACK, dots[0].shape[1]], F32, name)
-            for i in range(PACK):
-                nc.scalar.activation(kern[:, i, :], dots[i][:], TANH, bias=cb_col[:, a, i : i + 1])
-            return kern
-
-        def grouped_tile(width, name, tag=None):
-            return tile([P, width * PACK], BF16, name, tag=tag)
-
-        def weigh_on_vector(dst, kern, a):
-            weights = cw_psum[:, :, CW_STEP * a].unsqueeze(1).unsqueeze(3).to_broadcast([P, kern.shape[2] // RUN, PACK, RUN])
-            nc.vector.tensor_tensor(interleaved(dst), planes(kern), weights, MULT)
-
-        def weigh_on_gpsimd(dst, kern, a):
-            nc.gpsimd.tensor_tensor(
-                dst.rearrange("p (m i) -> p m i", i=PACK),
-                kern.rearrange("p i m -> p m i"),
-                cw_col[:, a, :].unsqueeze(1).to_broadcast([P, kern.shape[2], PACK]),
-                MULT,
-            )
-
-        def quantise_h(a, cols, grouped):
-            nc.vector.quantize_mx(out=h_codes[a][:, cols].bitcast(FP8X4), scales=h_planes[a][:, cols], in_=grouped[:])
-
-        dots = [dots_half(0, h, PACK * h) for h in range(2)]
-        kern0 = [tanh(0, dots[h], "kern0_%d" % h) for h in range(2)]
-        left0 = grouped_tile(HALF, "left0")
-        right0 = grouped_tile(HALF, "right0", tag="before_gpsimd")
-        weigh_on_vector(left0[:], kern0[0][:], 0)
-        weigh_on_vector(right0[:], kern0[1][:], 0)
-        quantise_h(0, LEFT, left0)
-        quantise_h(0, RIGHT, right0)
-
-        kern1 = tanh(1, dots_whole(1, 2 * PACK), "kern1")
-        left1 = grouped_tile(HALF, "left1", tag="before_gpsimd")
-        right1 = grouped_tile(HALF, "right1")
-        side = GPSIMD_COLS[1]
-        weigh_on_vector(right1[:], kern1[:, :, RIGHT], 1)
-        weigh_on_gpsimd(left1[:, 0 : side * PACK], kern1[:, :, 0:side], 1)
-        weigh_on_vector(left1[:, side * PACK :], kern1[:, :, side:HALF], 1)
-        quantise_h(1, RIGHT, right1)
-        quantise_h(1, LEFT, left1)
-
-        kern2 = tanh(2, dots_whole(2, 3 * PACK), "kern2")
-        left2 = grouped_tile(HALF, "left2")
-        right2 = grouped_tile(HALF, "right2", tag="before_gpsimd")
-        side = GPSIMD_COLS[2]
-        weigh_on_vector(left2[:], kern2[:, :, LEFT], 2)
-        weigh_on_gpsimd(right2[:, 0 : side * PACK], kern2[:, :, HALF : HALF + side], 2)
-
-        dots = [dots_half(3, h, 4 * PACK) for h in range(2)]
-        kern3 = [tanh(3, dots[h], "kern3_%d" % h) for h in range(2)]
+        kern2 = first_stage(2, slice(0, M), "kern2")
+        kern30 = first_stage(3, left, "kern30")
+        kern31 = first_stage(3, right, "kern31")
+        grouped20 = tile_at(grouped_shape, BF16, "grouped20", AT_CW[1] + 2)
+        weigh_on_vector(grouped20[:], kern2[:, :, left], 2)
+        grouped21 = tile_at(grouped_shape, BF16, "grouped21", AT_X_LEFT1 + 3)
+        weigh_shared(grouped21, kern2[:, :, right], 2, 2)
+        grouped30 = tile(grouped_shape, BF16, "grouped30")
+        weigh_on_vector(grouped30[:], kern30[:], 3)
         rounded = tile([P, PACK, HALF], BF16, "rounded")
         for i in range(PACK):
-            nc.scalar.activation(rounded[:, i, :], kern3[1][:, i, :], COPY, scale=cw_col[:, 3, i : i + 1])
-        left3 = grouped_tile(HALF, "left3")
-        third3 = grouped_tile(QUARTER, "third3")
-        fourth3 = grouped_tile(QUARTER, "fourth3")
-        weigh_on_vector(left3[:], kern3[0][:], 3)
-        weigh_on_vector(right2[:, side * PACK :], kern2[:, :, HALF + side : M], 2)
-        quantise_h(2, LEFT, left2)
-        quantise_h(3, LEFT, left3)
-        quantise_h(2, RIGHT, right2)
-        nc.vector.tensor_copy(interleaved(third3[:]), planes(rounded[:, :, 0:QUARTER]))
-        nc.scalar.copy(interleaved(fourth3[:]), planes(rounded[:, :, QUARTER:HALF]))
-        quantise_h(3, THIRD, third3)
-        quantise_h(3, FOURTH, fourth3)
+            nc.scalar.activation(rounded[:, i, :], kern31[:, i, :], COPY, scale=cols[:, 3, i : i + 1])
 
-        y_left = bank([P, 2, HALF], "y_left", 6)
-        y_third = bank([P, 2, QUARTER], "y_third", 0)
-        y_fourth = [bank([P, QUARTER], "y_fourth%d" % g, 1 + g) for g in range(2)]
+        quantise_h((2, 0), grouped20[:], tile_at([P, HALF], U32, "h_codes20", AT_CW[2]))
+        quantise_h((3, 0), grouped30[:])
+        quantise_h((2, 1), grouped21[:])
+        third = tile([P, QUARTER * PACK], BF16, "third")
+        fourth = tile([P, QUARTER * PACK], BF16, "fourth")
+        nc.vector.tensor_copy(interleaved(third[:]), planes(rounded[:, :, 0:QUARTER]))
+        nc.scalar.copy(interleaved(fourth[:]), planes(rounded[:, :, QUARTER:HALF]))
+        quantise_h((3, 2), third[:])
+        quantise_h((3, 3), fourth[:])
+
+        y_left = bank([P, 2, HALF], "y_left", 0)
+        y_third = bank([P, 2, QUARTER], "y_third", 1)
+        y_fourth = [bank([P, QUARTER], "y_fourth%d" % g, 2 + g) for g in range(2)]
         last = GROUPS - 1
 
-        def add_pass(dst, a, g, cols, start, stop):
+        def add_pass(dst, a, g, key, cols_of_h, start, stop):
             nc.tensor.matmul_mx(
                 out=dst,
                 lhsT=al_codes[:, a, g * P : (g + 1) * P].bitcast(FP8X4),
                 lhsT_scale=al_planes[4 * a : P, g * P : (g + 1) * P],
-                rhs=h_codes[a][:, cols].bitcast(FP8X4),
-                rhs_scale=h_planes[a][:, cols],
+                rhs=h_codes[key][:, cols_of_h].bitcast(FP8X4),
+                rhs_scale=h_planes[key][:, cols_of_h],
                 start=start,
                 stop=stop,
             )
 
-        def add_shared(y, a, cols):
+        def add_left(a):
             for g in range(2):
-                add_pass(y[:, g, :], a, g, cols, a == 0 and g == 0, a == last and g == 1)
+                add_pass(y_left[:, g, :], a, g, (a, 0), slice(0, HALF), a == 0 and g == 0, a == last and g == 1)
 
-        def add_fourth(a, g):
-            add_pass(y_fourth[g][:], a, g, FOURTH, a == 0, a == last)
+        def quarter_of(a, u):
+            return ((a, 2 + u), slice(0, QUARTER)) if a == last else ((a, 1), slice(u * QUARTER, (u + 1) * QUARTER))
+
+        def add_third(a):
+            key, cols_of_h = quarter_of(a, 0)
+            for g in range(2):
+                add_pass(y_third[:, g, :], a, g, key, cols_of_h, a == 0 and g == 0, a == last and g == 1)
+
+        def add_fourth(a):
+            key, cols_of_h = quarter_of(a, 1)
+            for g in range(2):
+                add_pass(y_fourth[g][:], a, g, key, cols_of_h, a == 0, a == last)
 
         for a in (0, 1):
-            add_shared(y_left, a, LEFT)
-            add_shared(y_third, a, THIRD)
-            add_fourth(a, 0)
+            add_left(a)
+            add_third(a)
+            add_fourth(a)
         for a in (2, 3):
-            add_shared(y_left, a, LEFT)
-        for a in (0, 1):
-            add_fourth(a, 1)
+            add_left(a)
         for a in (2, 3):
-            add_shared(y_third, a, THIRD)
-            for g in range(2):
-                add_fourth(a, g)
+            add_third(a)
+            add_fourth(a)
 
         out_rows = out.rearrange("(g p) m -> p g m", p=P)
         for g in range(2):
             result_left = keep.tile([P, HALF], F32, name="result_left%d" % g)
             nc.scalar.copy(result_left[:], y_left[:, g, :])
-            nc.sync.dma_start(out=out_rows[:, g, LEFT], in_=result_left[:])
+            nc.sync.dma_start(out=out_rows[:, g, 0:HALF], in_=result_left[:])
         result_third = keep.tile([P, 2, QUARTER], F32, name="result_third")
         nc.scalar.copy(result_third[:], y_third[:])
-        nc.sync.dma_start(out=out_rows[:, :, THIRD], in_=result_third[:])
+        nc.sync.dma_start(out=out_rows[:, :, HALF : HALF + QUARTER], in_=result_third[:])
         result_fourth = [keep.tile([P, QUARTER], F32, name="result_fourth%d" % g) for g in range(2)]
         nc.scalar.copy(result_fourth[0][:], y_fourth[0][:])
-        nc.scalar.dma_start(out=out_rows[:, 0, FOURTH], in_=result_fourth[0][:])
+        nc.scalar.dma_start(out=out_rows[:, 0, HALF + QUARTER : M], in_=result_fourth[0][:])
         nc.vector.tensor_copy(result_fourth[1][:], y_fourth[1][:])
-        nc.sync.dma_start(out=out_rows[:, 1, FOURTH], in_=result_fourth[1][:])
+        nc.sync.dma_start(out=out_rows[:, 1, HALF + QUARTER : M], in_=result_fourth[1][:])

@@ -33,8 +33,10 @@ FIRST_LIVE = P - SCALE_ROWS
 DOT_BANKS = 7
 ROW_STEP = 4
 KIB = 1024
-GPSIMD_COLS = (184, 176, 176)
-AT_X_LEFT1, AT_X_FOURTH, AT_X_RIGHT0, AT_X_THIRD, AT_CW = 0, 5, 10, 14, (24, 32, 36)
+SPREAD_AT = 64
+GPSIMD_COLS = (192, 128, 192)
+AT_X_LEFT1, AT_X_FOURTH, AT_X_RIGHT0, AT_X_THIRD, AT_KERN11, AT_KERN2, AT_ROUNDED = 0, 5, 10, 16, 26, 30, 38
+AT_CB = {1: 14, 3: 41}
 
 
 def tile_list_kernl_tanh_none_kernel(
@@ -99,6 +101,8 @@ def tile_list_kernl_tanh_none_kernel(
         tab_planes = [tile([P, K_PASSES, 2 * PASS], U8, "tab_planes%d" % u) for u in range(2)]
         for u in range(2):
             nc.gpsimd.memset(tab_planes[u][:].rearrange("p d j -> p (d j)").bitcast(I32), 0)
+        spread_scales = tile([P, PASS], U8, "spread_scales")
+        nc.gpsimd.memset(spread_scales[0:SPREAD_AT, :].bitcast(I32), 0)
         identity = tile([P, P], F32, "identity")
         nc.vector.memset(identity[:], 0.0)
         make_identity(nc, identity[:], nomemset=True)
@@ -107,10 +111,6 @@ def tile_list_kernl_tanh_none_kernel(
             nc.tensor.transpose(turned[:, i, :], rows[:].rearrange("p (q i) -> p i q", i=PACK)[:, i, :], identity[:])
         cols = tile([P, 2 * GROUPS, PACK], F32, "cols")
         nc.scalar.copy(cols[:], turned[:, :, 0 : 2 * GROUPS * ROW_STEP : ROW_STEP].rearrange("p i r -> p r i"))
-        cw_own = []
-        for w, width in enumerate((8, 4, 1)):
-            cw_own.append(tile_at([P, width * KIB // 4], F32, "cw_own%d" % w, AT_CW[w])[:, 0:PACK])
-            nc.gpsimd.tensor_copy(cw_own[w], cols[:, w, :])
 
         def pick_scales(dst, first, count):
             nc.vector.tensor_copy(dst, scale_table[:].indirect(group_offsets(first, count)))
@@ -120,27 +120,36 @@ def tile_list_kernl_tanh_none_kernel(
                 dst.rearrange("p (a i q) -> p a i q", i=PACK, q=P), src.rearrange("p (a q i) -> p a i q", i=PACK, q=P)
             )
 
-        def place_scales(dst, src):
-            rows_a_quad = 4 * K_PASSES
+        def place_scales(dst, src, first, rows_a_quad):
             for quad in (0, 2, 1, 3):
-                at = FIRST_LIVE + rows_a_quad * quad
+                at = first + rows_a_quad * quad
                 nc.sync.dma_start(
                     out=dst[32 * quad : 32 * quad + 4, :, :].bitcast(I32), in_=src[at : at + rows_a_quad, :].bitcast(I32)
                 )
 
-        picked01 = tile_at([P, 6 * KIB], U8, "picked01", AT_X_RIGHT0 - 1)[:, 0 : 2 * PASS]
-        picked2 = tile([P, PASS], U8, "picked2")
+        picked01 = tile_at([P, 8 * KIB], U8, "picked01", AT_X_RIGHT0 - 1)[:, 0 : 2 * PASS]
+        picked23 = tile([P, 2 * PASS], U8, "picked23")
         sorted01 = tile([P, 2 * PASS], U8, "sorted01")
         pick_scales(picked01, 0, 2)
-        pick_scales(picked2[:], 2, 1)
+        pick_scales(picked23[:, 0:PASS], 2, 1)
         sort_scales(sorted01[:], picked01)
-        place_scales(tab_planes[0], sorted01)
+        pick_scales(picked23[:, PASS : 2 * PASS], 3, 1)
+        place_scales(tab_planes[0], sorted01, FIRST_LIVE, 4 * K_PASSES)
         x_raw[0, 1] = tile_at([P, PACK, HALF], F32, "x_right0", AT_X_RIGHT0)[:]
-        x_third = by_slot(tile_at([P, 5 * KIB // 4], F32, "x_third", AT_X_THIRD)[:, 0 : PACK * QUARTER])
+        x_third = by_slot(tile_at([P, 7 * KIB // 4], F32, "x_third", AT_X_THIRD)[:, 0 : PACK * QUARTER])
         x_fourth = by_slot(tile_at([P, 5 * KIB // 4], F32, "x_fourth", AT_X_FOURTH)[:, 0 : PACK * QUARTER])
         nc.sync.dma_start(out=x_raw[0, 1], in_=x_rows[0][:, :, HALF:M])
         nc.sync.dma_start(out=x_third, in_=x_rows[1][:, :, HALF : HALF + QUARTER])
         nc.sync.dma_start(out=x_fourth, in_=x_rows[1][:, :, HALF + QUARTER : M])
+        nc.sync.dma_start(
+            out=spread_scales[SPREAD_AT:P, :].bitcast(I32),
+            in_=picked23[FIRST_LIVE:P, :].bitcast(I32).rearrange("p (a w) -> p a w", a=2),
+        )
+
+        cb_own = {}
+        for a in (1, 3):
+            cb_own[a] = tile_at([P, 2 * KIB // 4], F32, "cb_own%d" % a, AT_CB[a])[:, 0:PACK]
+            nc.scalar.copy(cb_own[a], turned[:, :, (GROUPS + a) * ROW_STEP])
 
         x_codes = [tile([P, M], U32, "x_codes%d" % d) for d in range(K_PASSES)]
         x_planes = [tile([P, M], U8, "x_planes%d" % d) for d in range(K_PASSES)]
@@ -172,9 +181,13 @@ def tile_list_kernl_tanh_none_kernel(
         h_planes = {}
         units_done = []
 
-        def first_stage(a, at, name, kib=None):
+        def first_stage(a, at, name, kib=None, spare=0, bias=None):
             shape = [P, PACK, at.stop - at.start]
-            dst = tile(shape, F32, name) if kib is None else tile_at(shape, F32, name, kib)
+            if kib is None:
+                dst = tile(shape, F32, name)
+            else:
+                dst = by_slot(tile_at([P, PACK * shape[2] + spare], F32, name, kib)[:, 0 : PACK * shape[2]])
+            bias = cols[:, GROUPS + a, :] if bias is None else bias
             for i in range(PACK):
                 number = (PACK * len(units_done) + i) % DOT_BANKS
                 dots = bank([P, shape[2]], "dots_%s_%d" % (name, i), number)
@@ -190,7 +203,7 @@ def tile_list_kernl_tanh_none_kernel(
                         start=(d == 0),
                         stop=(d == K_PASSES - 1),
                     )
-                nc.scalar.activation(dst[:, i, :], dots[:], TANH, bias=cols[:, GROUPS + a, i : i + 1])
+                nc.scalar.activation(dst[:, i, :], dots[:], TANH, bias=bias[:, i : i + 1])
             units_done.append(name)
             return dst
 
@@ -198,22 +211,32 @@ def tile_list_kernl_tanh_none_kernel(
             weights = turned[:, :, ROW_STEP * a].unsqueeze(1).unsqueeze(3).to_broadcast([P, src.shape[2] // RUN, PACK, RUN])
             nc.vector.tensor_tensor(interleaved(dst), planes(src), weights, MULT)
 
-        def weigh_shared(dst, src, a, w):
+        def weigh_shared(dst, src, a, w, kib):
             side = GPSIMD_COLS[w]
             nc.gpsimd.tensor_tensor(
                 dst[:, 0 : side * PACK].rearrange("p (m i) -> p m i", i=PACK),
                 src[:, :, 0:side].rearrange("p i m -> p m i"),
-                cw_own[w].unsqueeze(1).to_broadcast([P, side, PACK]),
+                cols[:, a, :].unsqueeze(1).to_broadcast([P, side, PACK]),
                 MULT,
             )
-            weigh_on_vector(dst[:, side * PACK :], src[:, :, side:HALF], a)
+            rest = tile_at([P, (HALF - side) * PACK], BF16, "rest%d" % w, kib)
+            weigh_on_vector(rest[:], src[:, :, side:HALF], a)
+            pieces = [(0, dst[:, 0 : QUARTER * PACK])]
+            if side > QUARTER:
+                pieces.append((QUARTER, dst[:, QUARTER * PACK : side * PACK]))
+            return [(side, rest[:])] + pieces
 
-        def quantise_h(key, src, codes=None, plane=None):
-            width = src.shape[1] // PACK
+        def quantise_h(key, pieces, codes=None, plane_at=None):
+            width = sum(src.shape[1] for at, src in pieces) // PACK
             name = "%d%d" % key
             h_codes[key] = codes if codes is not None else tile([P, width], U32, "h_codes" + name)
-            h_planes[key] = plane if plane is not None else tile([P, width], U8, "h_plane" + name)
-            nc.vector.quantize_mx(out=h_codes[key][:].bitcast(FP8X4), scales=h_planes[key][:], in_=src)
+            if plane_at is None:
+                h_planes[key] = tile([P, width], U8, "h_plane" + name)
+            else:
+                h_planes[key] = tile_at([P, width], U8, "h_plane" + name, plane_at)
+            for at, src in pieces:
+                to = slice(at, at + src.shape[1] // PACK)
+                nc.vector.quantize_mx(out=h_codes[key][:, to].bitcast(FP8X4), scales=h_planes[key][:, to], in_=src)
 
         words_shape, codes_shape, grouped_shape = [P, PASS], [P, K_PASSES * 2 * PASS], [P, HALF * PACK]
         left, right = slice(0, HALF), slice(HALF, M)
@@ -225,25 +248,22 @@ def tile_list_kernl_tanh_none_kernel(
         cast_x(1, 0)
         quantise_x(1, 0)
         part_words(1, tile_at(codes_shape, U8, "tab_codes1", AT_X_LEFT1))
-        picked3 = tile_at([P, PASS], U8, "picked3", AT_X_LEFT1 + 3)
-        pick_scales(picked3[:], 3, 1)
+        gather_words(2, tile_at(words_shape, U32, "picked_words2", AT_X_LEFT1 + 2))
         cast_x(0, 1)
-        x_grouped[1, 1] = tile(grouped_shape, BF16, "x_grouped11", tag="picked_words1")
-        nc.scalar.copy(interleaved(x_grouped[1, 1][:, 0 : QUARTER * PACK]), planes(x_third))
+        third_grouped = tile([P, QUARTER * PACK], BF16, "third_grouped")
+        fourth_grouped = tile([P, QUARTER * PACK], BF16, "fourth_grouped", tag="picked_words1")
+        nc.scalar.copy(interleaved(third_grouped[:]), planes(x_third))
         nc.gpsimd.tensor_scalar(
-            x_grouped[1, 1][:, QUARTER * PACK :].rearrange("p (m i) -> p m i", i=PACK),
-            x_fourth.rearrange("p i m -> p m i"),
-            1.0,
-            0.0,
-            MULT,
-            ADD,
+            fourth_grouped[:].rearrange("p (m i) -> p m i", i=PACK), x_fourth.rearrange("p i m -> p m i"), 1.0, 0.0, MULT, ADD
         )
         quantise_x(0, 1)
-        quantise_x(1, 1)
-        sorted23 = tile_at([P, 2 * PASS], U8, "sorted23", AT_X_FOURTH + 4)
-        sort_scales(sorted23[:, 0:PASS], picked2[:])
-        sort_scales(sorted23[:, PASS : 2 * PASS], picked3[:])
-        place_scales(tab_planes[1], sorted23)
+        for u, src in enumerate((third_grouped, fourth_grouped)):
+            at = slice(HALF + u * QUARTER, HALF + (u + 1) * QUARTER)
+            nc.vector.quantize_mx(out=x_codes[1][:, at].bitcast(FP8X4), scales=x_planes[1][:, at], in_=src[:])
+        sorted23 = tile([P, PASS], U8, "sorted23")
+        sort_scales(sorted23[:], spread_scales[:])
+        place_scales(tab_planes[1][:].rearrange("p d (a w) -> p (d a) w", a=2), sorted23, SPREAD_AT, 8 * K_PASSES)
+        part_words(2, tile_at(codes_shape, U8, "tab_codes2", AT_X_FOURTH))
 
         al_planes = sorted23[:, 0:N]
         al_codes = tile([P, GROUPS, N], I32, "al_codes", tag="x_grouped10")
@@ -254,52 +274,50 @@ def tile_list_kernl_tanh_none_kernel(
             )
         nc.sync.dma_start(out=al_codes[:], in_=al_words.rearrange("a p n i -> p a (n i)").bitcast(I32))
 
-        gather_words(2, tile_at(words_shape, U32, "picked_words2", AT_X_FOURTH))
-        gather_words(3, tile_at(words_shape, U32, "picked_words3", AT_X_FOURTH + 2))
-        kern00 = first_stage(0, left, "kern00", AT_X_THIRD)
-        kern10 = first_stage(1, left, "kern10", AT_X_THIRD + 4)
+        kern00 = first_stage(0, left, "kern00", AT_X_THIRD, 2 * KIB // 4)
+        kern10 = first_stage(1, left, "kern10", AT_X_THIRD + 6, bias=cb_own[1])
         kern01 = first_stage(0, right, "kern01")
-        kern11 = first_stage(1, right, "kern11")
+        kern11 = first_stage(1, right, "kern11", AT_KERN11)
+        kern2 = first_stage(2, slice(0, M), "kern2", AT_KERN2)
         grouped00 = tile_at(grouped_shape, BF16, "grouped00", AT_X_LEFT1 + 3)
-        weigh_shared(grouped00, kern00, 0, 0)
+        pieces00 = weigh_shared(grouped00, kern00, 0, 0, AT_X_FOURTH + 4)
+        gather_words(3, tile_at(words_shape, U32, "picked_words3", AT_X_FOURTH + 2))
+        grouped10 = tile(grouped_shape, BF16, "grouped10")
+        weigh_on_vector(grouped10[:], kern10[:], 1)
 
-        part_words(2, tile_at(codes_shape, U8, "tab_codes2", AT_CW[0]))
-        part_words(3, tile_at(codes_shape, U8, "tab_codes3", AT_CW[0] + 2))
-        quantise_h((0, 0), grouped00[:])
+        part_words(3, tile_at(codes_shape, U8, "tab_codes3", AT_X_THIRD - 1))
+        quantise_h((1, 0), [(0, grouped10[:])], tile_at([P, HALF], U32, "h_codes10", AT_X_THIRD + 2))
+        quantise_h((0, 0), pieces00, tile_at([P, HALF], U32, "h_codes00", AT_X_THIRD + 5), AT_CB[1])
 
-        grouped01 = tile_at(grouped_shape, BF16, "grouped01", AT_CW[0] + 6)
-        weigh_on_vector(grouped01[:], kern01[:], 0)
-        grouped10 = tile_at(grouped_shape, BF16, "grouped10", AT_X_LEFT1 + 3)
-        weigh_shared(grouped10, kern10, 1, 1)
-        grouped11 = tile_at(grouped_shape, BF16, "grouped11", AT_CW[0] + 4)
-        weigh_on_vector(grouped11[:], kern11[:], 1)
-
-        quantise_h((0, 1), grouped01[:], tile_at([P, HALF], U32, "h_codes01", AT_CW[1] + 1))
-        quantise_h((1, 1), grouped11[:], tile_at([P, HALF], U32, "h_codes11", AT_CW[1]))
-        quantise_h((1, 0), grouped10[:])
-
-        kern2 = first_stage(2, slice(0, M), "kern2")
-        kern30 = first_stage(3, left, "kern30")
+        kern30 = first_stage(3, left, "kern30", bias=cb_own[3])
         kern31 = first_stage(3, right, "kern31")
-        grouped20 = tile_at(grouped_shape, BF16, "grouped20", AT_CW[1] + 2)
+        grouped01 = tile_at(grouped_shape, BF16, "grouped01", AT_X_THIRD + 3)
+        weigh_on_vector(grouped01[:], kern01[:], 0)
+        grouped11 = tile_at(grouped_shape, BF16, "grouped11", AT_X_LEFT1 + 3)
+        pieces11 = weigh_shared(grouped11, kern11, 1, 1, AT_X_THIRD + 6)
+
+        quantise_h((0, 1), [(0, grouped01[:])], tile_at([P, HALF], U32, "h_codes01", AT_KERN11))
+        quantise_h((1, 1), pieces11, tile_at([P, HALF], U32, "h_codes11", AT_KERN11 + 3))
+
+        grouped20 = tile_at(grouped_shape, BF16, "grouped20", AT_KERN11 + 1)
         weigh_on_vector(grouped20[:], kern2[:, :, left], 2)
         grouped21 = tile_at(grouped_shape, BF16, "grouped21", AT_X_LEFT1 + 3)
-        weigh_shared(grouped21, kern2[:, :, right], 2, 2)
+        pieces21 = weigh_shared(grouped21, kern2[:, :, right], 2, 2, AT_X_THIRD + 7)
         grouped30 = tile(grouped_shape, BF16, "grouped30")
         weigh_on_vector(grouped30[:], kern30[:], 3)
-        rounded = tile([P, PACK, HALF], BF16, "rounded")
+        rounded = tile_at([P, PACK, QUARTER], BF16, "rounded", AT_ROUNDED)
         for i in range(PACK):
-            nc.scalar.activation(rounded[:, i, :], kern31[:, i, :], COPY, scale=cols[:, 3, i : i + 1])
+            nc.scalar.activation(rounded[:, i, :], kern31[:, i, QUARTER:HALF], COPY, scale=cols[:, 3, i : i + 1])
 
-        quantise_h((2, 0), grouped20[:], tile_at([P, HALF], U32, "h_codes20", AT_CW[2]))
-        quantise_h((3, 0), grouped30[:])
-        quantise_h((2, 1), grouped21[:])
+        quantise_h((2, 0), [(0, grouped20[:])], tile_at([P, HALF], U32, "h_codes20", AT_KERN2), AT_CB[3])
+        quantise_h((3, 0), [(0, grouped30[:])])
         third = tile([P, QUARTER * PACK], BF16, "third")
         fourth = tile([P, QUARTER * PACK], BF16, "fourth")
-        nc.vector.tensor_copy(interleaved(third[:]), planes(rounded[:, :, 0:QUARTER]))
-        nc.scalar.copy(interleaved(fourth[:]), planes(rounded[:, :, QUARTER:HALF]))
-        quantise_h((3, 2), third[:])
-        quantise_h((3, 3), fourth[:])
+        weigh_on_vector(third[:], kern31[:, :, 0:QUARTER], 3)
+        nc.scalar.copy(interleaved(fourth[:]), planes(rounded[:]))
+        quantise_h((2, 1), pieces21, tile_at([P, HALF], U32, "h_codes21", AT_KERN2 + 1), AT_CB[3] + 0.5)
+        quantise_h((3, 2), [(0, third[:])])
+        quantise_h((3, 3), [(0, fourth[:])])
 
         y_left = bank([P, 2, HALF], "y_left", 0)
         y_third = bank([P, 2, QUARTER], "y_third", 1)
@@ -346,7 +364,7 @@ def tile_list_kernl_tanh_none_kernel(
 
         out_rows = out.rearrange("(g p) m -> p g m", p=P)
         for g in range(2):
-            result_left = keep.tile([P, HALF], F32, name="result_left%d" % g)
+            result_left = tile_at([P, HALF], F32, "result_left%d" % g, AT_ROUNDED - 0.5 + g)
             nc.scalar.copy(result_left[:], y_left[:, g, :])
             nc.sync.dma_start(out=out_rows[:, g, 0:HALF], in_=result_left[:])
         result_third = keep.tile([P, 2, QUARTER], F32, name="result_third")

@@ -17,7 +17,6 @@ FP4X4 = mybir.dt.float4_e2m1fn_x4
 TANH = mybir.ActivationFunctionType.Tanh
 COPY = mybir.ActivationFunctionType.Copy
 MULT = mybir.AluOpType.mult
-ADD = mybir.AluOpType.add
 
 P = 128
 PACK = 4
@@ -251,11 +250,9 @@ def tile_list_kernl_tanh_none_kernel(
         gather_words(2, tile_at(words_shape, U32, "picked_words2", AT_X_LEFT1 + 2))
         cast_x(0, 1)
         third_grouped = tile([P, QUARTER * PACK], BF16, "third_grouped")
-        fourth_grouped = tile([P, QUARTER * PACK], BF16, "fourth_grouped", tag="picked_words1")
+        fourth_grouped = tile([P, QUARTER * PACK], BF16, "fourth_grouped")
         nc.scalar.copy(interleaved(third_grouped[:]), planes(x_third))
-        nc.gpsimd.tensor_scalar(
-            fourth_grouped[:].rearrange("p (m i) -> p m i", i=PACK), x_fourth.rearrange("p i m -> p m i"), 1.0, 0.0, MULT, ADD
-        )
+        nc.vector.tensor_copy(interleaved(fourth_grouped[:]), planes(x_fourth))
         quantise_x(0, 1)
         for u, src in enumerate((third_grouped, fourth_grouped)):
             at = slice(HALF + u * QUARTER, HALF + (u + 1) * QUARTER)
@@ -305,17 +302,17 @@ def tile_list_kernl_tanh_none_kernel(
         pieces21 = weigh_shared(grouped21, kern2[:, :, right], 2, 2, AT_X_THIRD + 7)
         grouped30 = tile(grouped_shape, BF16, "grouped30")
         weigh_on_vector(grouped30[:], kern30[:], 3)
-        rounded = tile_at([P, PACK, QUARTER], BF16, "rounded", AT_ROUNDED)
+        rounded = tile_at([P, PACK, HALF], BF16, "rounded", AT_ROUNDED)
         for i in range(PACK):
-            nc.scalar.activation(rounded[:, i, :], kern31[:, i, QUARTER:HALF], COPY, scale=cols[:, 3, i : i + 1])
+            nc.scalar.activation(rounded[:, i, :], kern31[:, i, :], COPY, scale=cols[:, 3, i : i + 1])
 
         quantise_h((2, 0), [(0, grouped20[:])], tile_at([P, HALF], U32, "h_codes20", AT_KERN2), AT_CB[3])
         quantise_h((3, 0), [(0, grouped30[:])])
         third = tile([P, QUARTER * PACK], BF16, "third")
         fourth = tile([P, QUARTER * PACK], BF16, "fourth")
-        weigh_on_vector(third[:], kern31[:, :, 0:QUARTER], 3)
-        nc.scalar.copy(interleaved(fourth[:]), planes(rounded[:]))
         quantise_h((2, 1), pieces21, tile_at([P, HALF], U32, "h_codes21", AT_KERN2 + 1), AT_CB[3] + 0.5)
+        nc.vector.tensor_copy(interleaved(third[:]), planes(rounded[:, :, 0:QUARTER]))
+        nc.scalar.copy(interleaved(fourth[:]), planes(rounded[:, :, QUARTER:HALF]))
         quantise_h((3, 2), [(0, third[:])])
         quantise_h((3, 3), [(0, fourth[:])])
 
@@ -364,7 +361,7 @@ def tile_list_kernl_tanh_none_kernel(
 
         out_rows = out.rearrange("(g p) m -> p g m", p=P)
         for g in range(2):
-            result_left = tile_at([P, HALF], F32, "result_left%d" % g, AT_ROUNDED - 0.5 + g)
+            result_left = tile_at([P, HALF], F32, "result_left%d" % g, AT_ROUNDED + g)
             nc.scalar.copy(result_left[:], y_left[:, g, :])
             nc.sync.dma_start(out=out_rows[:, g, 0:HALF], in_=result_left[:])
         result_third = keep.tile([P, 2, QUARTER], F32, name="result_third")

@@ -17,6 +17,7 @@ FP4X4 = mybir.dt.float4_e2m1fn_x4
 TANH = mybir.ActivationFunctionType.Tanh
 COPY = mybir.ActivationFunctionType.Copy
 MULT = mybir.AluOpType.mult
+ADD = mybir.AluOpType.add
 
 P = 128
 PACK = 4
@@ -135,8 +136,8 @@ def tile_list_kernl_tanh_none_kernel(
         pick_scales(picked23[:, PASS : 2 * PASS], 3, 1)
         place_scales(tab_planes[0], sorted01, FIRST_LIVE, 4 * K_PASSES)
         x_raw[0, 1] = tile_at([P, PACK, HALF], F32, "x_right0", AT_X_RIGHT0)[:]
-        x_third = by_slot(tile_at([P, 7 * KIB // 4], F32, "x_third", AT_X_THIRD)[:, 0 : PACK * QUARTER])
-        x_fourth = by_slot(tile_at([P, 5 * KIB // 4], F32, "x_fourth", AT_X_FOURTH)[:, 0 : PACK * QUARTER])
+        x_fourth = by_slot(tile_at([P, 7 * KIB // 4], F32, "x_fourth", AT_X_THIRD)[:, 0 : PACK * QUARTER])
+        x_third = by_slot(tile_at([P, 5 * KIB // 4], F32, "x_third", AT_X_FOURTH)[:, 0 : PACK * QUARTER])
         nc.sync.dma_start(out=x_raw[0, 1], in_=x_rows[0][:, :, HALF:M])
         nc.sync.dma_start(out=x_third, in_=x_rows[1][:, :, HALF : HALF + QUARTER])
         nc.sync.dma_start(out=x_fourth, in_=x_rows[1][:, :, HALF + QUARTER : M])
@@ -248,15 +249,22 @@ def tile_list_kernl_tanh_none_kernel(
         quantise_x(1, 0)
         part_words(1, tile_at(codes_shape, U8, "tab_codes1", AT_X_LEFT1))
         gather_words(2, tile_at(words_shape, U32, "picked_words2", AT_X_LEFT1 + 2))
-        cast_x(0, 1)
-        third_grouped = tile([P, QUARTER * PACK], BF16, "third_grouped")
-        fourth_grouped = tile([P, QUARTER * PACK], BF16, "fourth_grouped")
-        nc.scalar.copy(interleaved(third_grouped[:]), planes(x_third))
-        nc.vector.tensor_copy(interleaved(fourth_grouped[:]), planes(x_fourth))
-        quantise_x(0, 1)
-        for u, src in enumerate((third_grouped, fourth_grouped)):
+        quarters = {}
+        quarters[0, 0] = tile([P, QUARTER * PACK], BF16, "x_quarter00", tag="picked_words1")
+        nc.gpsimd.tensor_scalar(
+            quarters[0, 0][:].rearrange("p (m i) -> p m i", i=PACK),
+            x_raw[0, 1][:, :, 0:QUARTER].rearrange("p i m -> p m i"),
+            1.0,
+            0.0,
+            MULT,
+            ADD,
+        )
+        for key, src in (((0, 1), x_raw[0, 1][:, :, QUARTER:HALF]), ((1, 0), x_third), ((1, 1), x_fourth)):
+            quarters[key] = tile([P, QUARTER * PACK], BF16, "x_quarter%d%d" % key)
+            nc.scalar.copy(interleaved(quarters[key][:]), planes(src))
+        for d, u in ((0, 1), (1, 0), (0, 0), (1, 1)):
             at = slice(HALF + u * QUARTER, HALF + (u + 1) * QUARTER)
-            nc.vector.quantize_mx(out=x_codes[1][:, at].bitcast(FP8X4), scales=x_planes[1][:, at], in_=src[:])
+            nc.vector.quantize_mx(out=x_codes[d][:, at].bitcast(FP8X4), scales=x_planes[d][:, at], in_=quarters[d, u][:])
         sorted23 = tile([P, PASS], U8, "sorted23")
         sort_scales(sorted23[:], spread_scales[:])
         place_scales(tab_planes[1][:].rearrange("p d (a w) -> p (d a) w", a=2), sorted23, SPREAD_AT, 8 * K_PASSES)

@@ -33,10 +33,10 @@ FIRST_LIVE = P - SCALE_ROWS
 DOT_BANKS = 7
 ROW_STEP = 4
 KIB = 1024
+SCALAR_COLS = 192
 SPREAD_AT = 64
-GPSIMD_COLS = (192, 128, 192)
 AT_X_LEFT1, AT_X_FOURTH, AT_X_RIGHT0, AT_X_THIRD, AT_KERN11, AT_KERN2, AT_ROUNDED = 0, 5, 10, 16, 26, 30, 38
-AT_CB = {1: 14, 3: 41}
+AT_CB = {0: 14, 3: 41}
 
 
 def tile_list_kernl_tanh_none_kernel(
@@ -147,7 +147,7 @@ def tile_list_kernl_tanh_none_kernel(
         )
 
         cb_own = {}
-        for a in (1, 3):
+        for a in (0, 3):
             cb_own[a] = tile_at([P, 2 * KIB // 4], F32, "cb_own%d" % a, AT_CB[a])[:, 0:PACK]
             nc.scalar.copy(cb_own[a], turned[:, :, (GROUPS + a) * ROW_STEP])
 
@@ -211,20 +211,13 @@ def tile_list_kernl_tanh_none_kernel(
             weights = turned[:, :, ROW_STEP * a].unsqueeze(1).unsqueeze(3).to_broadcast([P, src.shape[2] // RUN, PACK, RUN])
             nc.vector.tensor_tensor(interleaved(dst), planes(src), weights, MULT)
 
-        def weigh_shared(dst, src, a, w, kib):
-            side = GPSIMD_COLS[w]
+        def weigh_on_gpsimd(dst, src, a):
             nc.gpsimd.tensor_tensor(
-                dst[:, 0 : side * PACK].rearrange("p (m i) -> p m i", i=PACK),
-                src[:, :, 0:side].rearrange("p i m -> p m i"),
-                cols[:, a, :].unsqueeze(1).to_broadcast([P, side, PACK]),
+                dst.rearrange("p (m i) -> p m i", i=PACK),
+                src.rearrange("p i m -> p m i"),
+                cols[:, a, :].unsqueeze(1).to_broadcast([P, src.shape[2], PACK]),
                 MULT,
             )
-            rest = tile_at([P, (HALF - side) * PACK], BF16, "rest%d" % w, kib)
-            weigh_on_vector(rest[:], src[:, :, side:HALF], a)
-            pieces = [(0, dst[:, 0 : QUARTER * PACK])]
-            if side > QUARTER:
-                pieces.append((QUARTER, dst[:, QUARTER * PACK : side * PACK]))
-            return [(side, rest[:])] + pieces
 
         def quantise_h(key, pieces, codes=None, plane_at=None):
             width = sum(src.shape[1] for at, src in pieces) // PACK
@@ -280,53 +273,52 @@ def tile_list_kernl_tanh_none_kernel(
         nc.sync.dma_start(out=al_codes[:], in_=al_words.rearrange("a p n i -> p a (n i)").bitcast(I32))
 
         kern00 = first_stage(0, left, "kern00", AT_X_THIRD, 2 * KIB // 4)
-        kern10 = first_stage(1, left, "kern10", AT_X_THIRD + 6, bias=cb_own[1])
-        kern01 = first_stage(0, right, "kern01")
-        kern11 = first_stage(1, right, "kern11", AT_KERN11)
-        kern2 = first_stage(2, slice(0, M), "kern2", AT_KERN2)
+        kern10 = first_stage(1, left, "kern10", AT_X_THIRD + 6)
+        kern01 = first_stage(0, right, "kern01", bias=cb_own[0])
+        kern11 = first_stage(1, right, "kern11", AT_KERN2)
+        kern20 = first_stage(2, left, "kern20")
+        kern21 = first_stage(2, right, "kern21")
         grouped00 = tile_at(grouped_shape, BF16, "grouped00", AT_X_LEFT1 + 3)
-        pieces00 = weigh_shared(grouped00, kern00, 0, 0, AT_X_FOURTH + 4)
+        weigh_on_gpsimd(grouped00[:], kern00, 0)
         gather_words(3, tile_at(words_shape, U32, "picked_words3", AT_X_FOURTH + 2))
         grouped10 = tile(grouped_shape, BF16, "grouped10")
         weigh_on_vector(grouped10[:], kern10[:], 1)
+        grouped01 = tile(grouped_shape, BF16, "grouped01")
+        weigh_on_vector(grouped01[:], kern01[:], 0)
 
         part_words(3, tile_at(codes_shape, U8, "tab_codes3", AT_X_THIRD - 1))
-        quantise_h((1, 0), [(0, grouped10[:])], tile_at([P, HALF], U32, "h_codes10", AT_X_THIRD + 2))
-        quantise_h((0, 0), pieces00, tile_at([P, HALF], U32, "h_codes00", AT_X_THIRD + 5), AT_CB[1])
+        quantise_h((1, 0), [(0, grouped10[:])], tile_at([P, HALF], U32, "h_codes10", AT_X_THIRD + 2), AT_CB[0])
+        quantise_h((0, 1), [(0, grouped01[:])], tile_at([P, HALF], U32, "h_codes01", AT_X_THIRD + 3))
+        quantise_h((0, 0), [(0, grouped00[:])], plane_at=AT_CB[0] + 0.5)
 
         kern30 = first_stage(3, left, "kern30", bias=cb_own[3])
         kern31 = first_stage(3, right, "kern31")
-        grouped01 = tile_at(grouped_shape, BF16, "grouped01", AT_X_THIRD + 3)
-        weigh_on_vector(grouped01[:], kern01[:], 0)
         grouped11 = tile_at(grouped_shape, BF16, "grouped11", AT_X_LEFT1 + 3)
-        pieces11 = weigh_shared(grouped11, kern11, 1, 1, AT_X_THIRD + 6)
-
-        quantise_h((0, 1), [(0, grouped01[:])], tile_at([P, HALF], U32, "h_codes01", AT_KERN11))
-        quantise_h((1, 1), pieces11, tile_at([P, HALF], U32, "h_codes11", AT_KERN11 + 3))
-
-        grouped20 = tile_at(grouped_shape, BF16, "grouped20", AT_KERN11 + 1)
-        weigh_on_vector(grouped20[:], kern2[:, :, left], 2)
-        grouped21 = tile_at(grouped_shape, BF16, "grouped21", AT_X_LEFT1 + 3)
-        pieces21 = weigh_shared(grouped21, kern2[:, :, right], 2, 2, AT_X_THIRD + 7)
+        weigh_on_gpsimd(grouped11[:], kern11, 1)
+        grouped20 = tile_at(grouped_shape, BF16, "grouped20", AT_X_THIRD + 4)
+        weigh_on_vector(grouped20[:], kern20[:], 2)
+        grouped21 = tile(grouped_shape, BF16, "grouped21")
+        weigh_on_vector(grouped21[:], kern21[:], 2)
         grouped30 = tile(grouped_shape, BF16, "grouped30")
         weigh_on_vector(grouped30[:], kern30[:], 3)
-        rounded = tile_at([P, PACK, HALF], BF16, "rounded", AT_ROUNDED)
+        rounded = tile_at([P, PACK, SCALAR_COLS], BF16, "rounded", AT_ROUNDED)
         for i in range(PACK):
-            nc.scalar.activation(rounded[:, i, :], kern31[:, i, :], COPY, scale=cols[:, 3, i : i + 1])
-
-        quantise_h((2, 0), [(0, grouped20[:])], tile_at([P, HALF], U32, "h_codes20", AT_KERN2), AT_CB[3])
-        quantise_h((3, 0), [(0, grouped30[:])])
-        third = tile([P, QUARTER * PACK], BF16, "third")
+            nc.scalar.activation(rounded[:, i, :], kern31[:, i, HALF - SCALAR_COLS : HALF], COPY, scale=cols[:, 3, i : i + 1])
         fourth = tile([P, QUARTER * PACK], BF16, "fourth")
-        quantise_h((2, 1), pieces21, tile_at([P, HALF], U32, "h_codes21", AT_KERN2 + 1), AT_CB[3] + 0.5)
-        nc.vector.tensor_copy(interleaved(third[:]), planes(rounded[:, :, 0:QUARTER]))
-        nc.scalar.copy(interleaved(fourth[:]), planes(rounded[:, :, QUARTER:HALF]))
+        nc.scalar.copy(interleaved(fourth[:]), planes(rounded[:, :, SCALAR_COLS - QUARTER :]))
+
+        for u, (key, src) in enumerate((((2, 0), grouped20), ((3, 0), grouped30), ((1, 1), grouped11))):
+            quantise_h(key, [(0, src[:])], tile_at([P, HALF], U32, "h_codes%d%d" % key, AT_KERN2 + u), AT_CB[3] + u / 4)
+        third = tile([P, QUARTER * PACK], BF16, "third", tag="grouped30")
+        own = HALF - SCALAR_COLS
+        weigh_on_vector(third[:, 0 : own * PACK], kern31[:, :, 0:own], 3)
+        nc.vector.tensor_copy(interleaved(third[:, own * PACK :]), planes(rounded[:, :, 0 : QUARTER - own]))
+        quantise_h((2, 1), [(0, grouped21[:])], tile_at([P, HALF], U32, "h_codes21", AT_KERN2 + 3), AT_CB[3] + 0.75)
         quantise_h((3, 2), [(0, third[:])])
         quantise_h((3, 3), [(0, fourth[:])])
 
-        y_left = bank([P, 2, HALF], "y_left", 0)
-        y_third = bank([P, 2, QUARTER], "y_third", 1)
-        y_fourth = [bank([P, QUARTER], "y_fourth%d" % g, 2 + g) for g in range(2)]
+        y_left = bank([P, 2, HALF], "y_left", 4)
+        y_right = {(u, g): bank([P, QUARTER], "y_right%d%d" % (u, g), (5 + 2 * u + g) % DOT_BANKS) for u in range(2) for g in range(2)}
         last = GROUPS - 1
 
         def add_pass(dst, a, g, key, cols_of_h, start, stop):
@@ -347,36 +339,29 @@ def tile_list_kernl_tanh_none_kernel(
         def quarter_of(a, u):
             return ((a, 2 + u), slice(0, QUARTER)) if a == last else ((a, 1), slice(u * QUARTER, (u + 1) * QUARTER))
 
-        def add_third(a):
-            key, cols_of_h = quarter_of(a, 0)
+        def add_quarter(a, u):
+            key, cols_of_h = quarter_of(a, u)
             for g in range(2):
-                add_pass(y_third[:, g, :], a, g, key, cols_of_h, a == 0 and g == 0, a == last and g == 1)
+                add_pass(y_right[u, g][:], a, g, key, cols_of_h, a == 0, a == last)
 
-        def add_fourth(a):
-            key, cols_of_h = quarter_of(a, 1)
-            for g in range(2):
-                add_pass(y_fourth[g][:], a, g, key, cols_of_h, a == 0, a == last)
-
-        for a in (0, 1):
+        add_left(0)
+        for u in range(2):
+            add_quarter(0, u)
+        for a in (1, 2, 3):
             add_left(a)
-            add_third(a)
-            add_fourth(a)
-        for a in (2, 3):
-            add_left(a)
-        for a in (2, 3):
-            add_third(a)
-            add_fourth(a)
+        for a in (1, 2, 3):
+            for u in range(2):
+                add_quarter(a, u)
 
         out_rows = out.rearrange("(g p) m -> p g m", p=P)
         for g in range(2):
-            result_left = tile_at([P, HALF], F32, "result_left%d" % g, AT_ROUNDED + g)
+            result_left = tile_at([P, HALF], F32, "result_left%d" % g, AT_ROUNDED - 0.5 + g)
             nc.scalar.copy(result_left[:], y_left[:, g, :])
             nc.sync.dma_start(out=out_rows[:, g, 0:HALF], in_=result_left[:])
-        result_third = keep.tile([P, 2, QUARTER], F32, name="result_third")
-        nc.scalar.copy(result_third[:], y_third[:])
-        nc.sync.dma_start(out=out_rows[:, :, HALF : HALF + QUARTER], in_=result_third[:])
-        result_fourth = [keep.tile([P, QUARTER], F32, name="result_fourth%d" % g) for g in range(2)]
-        nc.scalar.copy(result_fourth[0][:], y_fourth[0][:])
-        nc.scalar.dma_start(out=out_rows[:, 0, HALF + QUARTER : M], in_=result_fourth[0][:])
-        nc.vector.tensor_copy(result_fourth[1][:], y_fourth[1][:])
-        nc.sync.dma_start(out=out_rows[:, 1, HALF + QUARTER : M], in_=result_fourth[1][:])
+        for u in range(2):
+            at = slice(HALF + u * QUARTER, HALF + (u + 1) * QUARTER)
+            result = [keep.tile([P, QUARTER], F32, name="result_right%d%d" % (u, g)) for g in range(2)]
+            nc.scalar.copy(result[0][:], y_right[u, 0][:])
+            (nc.sync, nc.scalar)[u].dma_start(out=out_rows[:, 0, at], in_=result[0][:])
+            nc.vector.tensor_copy(result[1][:], y_right[u, 1][:])
+            nc.sync.dma_start(out=out_rows[:, 1, at], in_=result[1][:])

@@ -317,8 +317,8 @@ def tile_list_kernl_tanh_none_kernel(
         quantise_h((3, 2), [(0, third[:])])
         quantise_h((3, 3), [(0, fourth[:])])
 
-        y_left = bank([P, 2, HALF], "y_left", 4)
-        y_right = {(u, g): bank([P, QUARTER], "y_right%d%d" % (u, g), (5 + 2 * u + g) % DOT_BANKS) for u in range(2) for g in range(2)}
+        y_left = bank([P, 2, HALF], "y_left", 0)
+        y_right = {(u, g): bank([P, QUARTER], "y_right%d%d" % (u, g), 1 + 2 * u + g) for u in range(2) for g in range(2)}
         last = GROUPS - 1
 
         def add_pass(dst, a, g, key, cols_of_h, start, stop):

@@ -28,6 +28,7 @@ HALF = M // 2
 QUARTER = M // 4
 LIST_COLS = PASS // 16
 RUN = 4
+PAIR = 2
 SCALE_ROWS = K // 32
 FIRST_LIVE = P - SCALE_ROWS
 DOT_BANKS = 7
@@ -98,8 +99,8 @@ def tile_list_kernl_tanh_none_kernel(
                 out=rows[first : first + GROUPS * ROW_STEP : ROW_STEP, :], in_=vec.rearrange("(a j) -> a j", a=GROUPS)
             )
         nc.vector.memset(scale_table[0:FIRST_LIVE, :].bitcast(I32), 0)
-        tab_planes = [tile([P, K_PASSES, 2 * PASS], U8, "tab_planes%d" % u) for u in range(2)]
-        for u in range(2):
+        tab_planes = [tile([P, K_PASSES, w * PASS], U8, "tab_planes%d" % u) for u, w in enumerate((1, 1, 2))]
+        for u in range(3):
             nc.gpsimd.memset(tab_planes[u][:].rearrange("p d j -> p (d j)").bitcast(I32), 0)
         spread_scales = tile([P, PASS], U8, "spread_scales")
         nc.gpsimd.memset(spread_scales[0:SPREAD_AT, :].bitcast(I32), 0)
@@ -134,7 +135,7 @@ def tile_list_kernl_tanh_none_kernel(
         pick_scales(picked23[:, 0:PASS], 2, 1)
         sort_scales(sorted01[:], picked01)
         pick_scales(picked23[:, PASS : 2 * PASS], 3, 1)
-        place_scales(tab_planes[0], sorted01, FIRST_LIVE, 4 * K_PASSES)
+        place_scales(tab_planes[0], sorted01[:, 0:PASS], FIRST_LIVE, 4 * K_PASSES)
         x_raw[0, 1] = tile_at([P, PACK, HALF], F32, "x_right0", AT_X_RIGHT0)[:]
         x_fourth = by_slot(tile_at([P, 7 * KIB // 4], F32, "x_fourth", AT_X_THIRD)[:, 0 : PACK * QUARTER])
         x_third = by_slot(tile_at([P, 5 * KIB // 4], F32, "x_third", AT_X_FOURTH)[:, 0 : PACK * QUARTER])
@@ -145,13 +146,21 @@ def tile_list_kernl_tanh_none_kernel(
             out=spread_scales[SPREAD_AT:P, :].bitcast(I32),
             in_=picked23[FIRST_LIVE:P, :].bitcast(I32).rearrange("p (a w) -> p a w", a=2),
         )
+        place_scales(tab_planes[1], sorted01[:, PASS : 2 * PASS], FIRST_LIVE, 4 * K_PASSES)
 
         cb_own = {}
         for a in (0, 3):
             cb_own[a] = tile_at([P, 2 * KIB // 4], F32, "cb_own%d" % a, AT_CB[a])[:, 0:PACK]
             nc.scalar.copy(cb_own[a], turned[:, :, (GROUPS + a) * ROW_STEP])
 
-        x_codes = [tile([P, M], U32, "x_codes%d" % d) for d in range(K_PASSES)]
+        codes_left = [tile([P, HALF], U32, "x_codes_left%d" % d) for d in range(K_PASSES)]
+        codes_right = [tile([P, HALF], U32, "x_codes_right0"), tile([P, HALF], U32, "x_codes_right1")]
+
+        def x_codes(d, at):
+            if at.start < HALF:
+                return codes_left[d][:, at].bitcast(FP8X4)
+            return codes_right[d][:, at.start - HALF : at.stop - HALF].bitcast(FP8X4)
+
         x_planes = [tile([P, M], U8, "x_planes%d" % d) for d in range(K_PASSES)]
         x_grouped = {}
 
@@ -161,7 +170,7 @@ def tile_list_kernl_tanh_none_kernel(
 
         def quantise_x(d, h):
             at = slice(h * HALF, (h + 1) * HALF)
-            nc.vector.quantize_mx(out=x_codes[d][:, at].bitcast(FP8X4), scales=x_planes[d][:, at], in_=x_grouped[d, h][:])
+            nc.vector.quantize_mx(out=x_codes(d, at), scales=x_planes[d][:, at], in_=x_grouped[d, h][:])
 
         picked_words = {}
         tab_codes = {}
@@ -189,16 +198,16 @@ def tile_list_kernl_tanh_none_kernel(
                 dst = by_slot(tile_at([P, PACK * shape[2] + spare], F32, name, kib)[:, 0 : PACK * shape[2]])
             bias = cols[:, GROUPS + a, :] if bias is None else bias
             for i in range(PACK):
-                number = (PACK * len(units_done) + i) % DOT_BANKS
+                number = (PACK * (len(units_done) - (len(units_done) > 1)) + i) % DOT_BANKS
                 dots = bank([P, shape[2]], "dots_%s_%d" % (name, i), number)
                 for d in range(K_PASSES):
                     word = (d * PACK + i) * 2 * P
-                    byte = (a % 2) * PASS + i * P
+                    byte = (a == 3) * PASS + i * P
                     nc.tensor.matmul_mx(
                         out=dots[:],
                         lhsT=tab_codes[a][:, word : word + 2 * P].bitcast(FP4X4),
-                        lhsT_scale=tab_planes[a // 2][:, d, byte : byte + P],
-                        rhs=x_codes[d][:, at].bitcast(FP8X4),
+                        lhsT_scale=tab_planes[min(a, 2)][:, d, byte : byte + P],
+                        rhs=x_codes(d, at),
                         rhs_scale=x_planes[d][:, at],
                         start=(d == 0),
                         stop=(d == K_PASSES - 1),
@@ -213,9 +222,9 @@ def tile_list_kernl_tanh_none_kernel(
 
         def weigh_on_gpsimd(dst, src, a):
             nc.gpsimd.tensor_tensor(
-                dst.rearrange("p (m i) -> p m i", i=PACK),
-                src.rearrange("p i m -> p m i"),
-                cols[:, a, :].unsqueeze(1).to_broadcast([P, src.shape[2], PACK]),
+                dst.rearrange("p (c e i) -> p c i e", e=PAIR, i=PACK),
+                src.rearrange("p i (c e) -> p c i e", e=PAIR),
+                cols[:, a, :].unsqueeze(1).unsqueeze(3).to_broadcast([P, src.shape[2] // PAIR, PACK, PAIR]),
                 MULT,
             )
 
@@ -245,8 +254,8 @@ def tile_list_kernl_tanh_none_kernel(
         quarters = {}
         quarters[0, 0] = tile([P, QUARTER * PACK], BF16, "x_quarter00", tag="picked_words1")
         nc.gpsimd.tensor_scalar(
-            quarters[0, 0][:].rearrange("p (m i) -> p m i", i=PACK),
-            x_raw[0, 1][:, :, 0:QUARTER].rearrange("p i m -> p m i"),
+            quarters[0, 0][:].rearrange("p (c e i) -> p c i e", e=PAIR, i=PACK),
+            x_raw[0, 1][:, :, 0:QUARTER].rearrange("p i (c e) -> p c i e", e=PAIR),
             1.0,
             0.0,
             MULT,
@@ -257,10 +266,10 @@ def tile_list_kernl_tanh_none_kernel(
             nc.scalar.copy(interleaved(quarters[key][:]), planes(src))
         for d, u in ((0, 1), (1, 0), (0, 0), (1, 1)):
             at = slice(HALF + u * QUARTER, HALF + (u + 1) * QUARTER)
-            nc.vector.quantize_mx(out=x_codes[d][:, at].bitcast(FP8X4), scales=x_planes[d][:, at], in_=quarters[d, u][:])
+            nc.vector.quantize_mx(out=x_codes(d, at), scales=x_planes[d][:, at], in_=quarters[d, u][:])
         sorted23 = tile([P, PASS], U8, "sorted23")
         sort_scales(sorted23[:], spread_scales[:])
-        place_scales(tab_planes[1][:].rearrange("p d (a w) -> p (d a) w", a=2), sorted23, SPREAD_AT, 8 * K_PASSES)
+        place_scales(tab_planes[2][:].rearrange("p d (a w) -> p (d a) w", a=2), sorted23, SPREAD_AT, 8 * K_PASSES)
         part_words(2, tile_at(codes_shape, U8, "tab_codes2", AT_X_FOURTH))
 
         al_planes = sorted23[:, 0:N]
@@ -317,8 +326,8 @@ def tile_list_kernl_tanh_none_kernel(
         quantise_h((3, 2), [(0, third[:])])
         quantise_h((3, 3), [(0, fourth[:])])
 
-        y_left = bank([P, 2, HALF], "y_left", 0)
-        y_right = {(u, g): bank([P, QUARTER], "y_right%d%d" % (u, g), 1 + 2 * u + g) for u in range(2) for g in range(2)}
+        y_left = bank([P, 2, HALF], "y_left", 3)
+        y_right = {(u, g): bank([P, QUARTER], "y_right%d%d" % (u, g), (4 + 2 * u + g) % DOT_BANKS) for u in range(2) for g in range(2)}
         last = GROUPS - 1
 
         def add_pass(dst, a, g, key, cols_of_h, start, stop):

from contextlib import ExitStack

import concourse.mybir as mybir
from concourse.masks import make_identity

K, M, N, J, T = 1024, 512, 256, 2048, 4096
FLOPS = 2 * K * J * M + 2 * J * N * M

F32 = mybir.dt.float32
BF16 = mybir.dt.bfloat16
I32 = mybir.dt.int32
U32 = mybir.dt.uint32
U16 = mybir.dt.uint16
U8 = mybir.dt.uint8
FP8X4 = mybir.dt.float8_e4m3fn_x4
FP4X4 = mybir.dt.float4_e2m1fn_x4
TANH = mybir.ActivationFunctionType.Tanh
COPY = mybir.ActivationFunctionType.Copy
MULT = mybir.AluOpType.mult
ADD = mybir.AluOpType.add

P = 128
PACK = 4
PASS = P * PACK
K_PASSES = K // PASS
GROUPS = J // PASS
HALF = M // 2
QUARTER = M // 4
LIST_COLS = PASS // 16
RUN = 4
PAIR = 2
SCALE_ROWS = K // 32
FIRST_LIVE = P - SCALE_ROWS
DOT_BANKS = 7
ROW_STEP = 4
KIB = 1024
SCALAR_COLS = 192
SPREAD_AT = 64
AT_X_LEFT1, AT_X_FOURTH, AT_X_RIGHT0, AT_X_THIRD, AT_KERN11, AT_KERN2, AT_ROUNDED = 0, 5, 10, 16, 26, 30, 38
AT_CB = {0: 14, 3: 41}


def tile_list_kernl_tanh_none_kernel(
    tc, x, tab_words, tab_scales, cw, cb, al_words, al_scales, offs, out
):
    nc = tc.nc
    with ExitStack() as ctx:
        keep = ctx.enter_context(tc.tile_pool(name="keep", bufs=1))
        reused = ctx.enter_context(tc.tile_pool(name="reused", bufs=1))
        psum = ctx.enter_context(tc.psum_pool(name="psum", bufs=1))

        def tile(shape, dtype, name, tag=None):
            return keep.tile(shape, dtype, name=name, tag=tag or name, align_bytes=64)

        def tile_at(shape, dtype, name, kib):
            return reused.tile(shape, dtype, name=name, align_bytes=64, offset=int(kib * KIB))

        def bank(shape, name, number):
            return psum.tile(shape, F32, name=name, tag="bank%d" % number)

        def interleaved(ap):
            return ap.rearrange("p (c e i) -> p c i e", e=RUN, i=PACK)

        def planes(ap):
            return ap.rearrange("p i (c e) -> p c i e", e=RUN)

        def by_slot(ap):
            return ap.rearrange("p (i m) -> p i m", i=PACK)

        def group_offsets(first, count):
            return offsets[:, first * LIST_COLS : (first + count) * LIST_COLS]

        scale_table = tile([P, T], U8, "scale_table")
        offsets = keep.tile([P, J // 16], U16, name="offsets")
        nc.sync.dma_start(offsets[:], offs)
        nc.sync.dma_start(
            out=scale_table[FIRST_LIVE:P, :].bitcast(I32),
            in_=tab_scales.bitcast(I32).rearrange("d q w -> q d w"),
        )
        word_table = tile([P, T], I32, "word_table")
        nc.sync.dma_start(out=word_table[:], in_=tab_words[0].rearrange("p t b -> p (t b)").bitcast(I32))
        x_rows = x.rearrange("(d p i) m -> d p i m", p=P, i=PACK)
        x_raw = {}
        x_raw[0, 0] = tile([P, PACK, HALF], F32, "x_left0")[:]
        x_raw[1, 0] = tile_at([P, PACK, HALF], F32, "x_left1", AT_X_LEFT1)[:]
        for d in range(K_PASSES):
            nc.sync.dma_start(out=x_raw[d, 0], in_=x_rows[d][:, :, 0:HALF])

        warm = keep.tile([P, 8], F32, name="warm")
        nc.vector.memset(warm[:], 0.0)
        warm_out = keep.tile([P, 8], F32, name="warm_out")
        nc.scalar.activation(warm_out[:], warm[:], TANH)

        rows = tile([P, PASS], F32, "rows")
        nc.gpsimd.memset(rows[:], 0.0)
        for r, vec in enumerate((cw, cb)):
            first = r * GROUPS * ROW_STEP
            nc.gpsimd.dma_start(
                out=rows[first : first + GROUPS * ROW_STEP : ROW_STEP, :], in_=vec.rearrange("(a j) -> a j", a=GROUPS)
            )
        nc.vector.memset(scale_table[0:FIRST_LIVE, :].bitcast(I32), 0)
        tab_planes = [tile([P, K_PASSES, w * PASS], U8, "tab_planes%d" % u) for u, w in enumerate((1, 1, 2))]
        for u in range(3):
            nc.gpsimd.memset(tab_planes[u][:].rearrange("p d j -> p (d j)").bitcast(I32), 0)
        spread_scales = tile([P, PASS], U8, "spread_scales")
        nc.gpsimd.memset(spread_scales[0:SPREAD_AT, :].bitcast(I32), 0)
        identity = tile([P, P], F32, "identity")
        nc.vector.memset(identity[:], 0.0)
        make_identity(nc, identity[:], nomemset=True)
        turned = bank([P, PACK, P], "turned", DOT_BANKS)
        for i in range(PACK):
            nc.tensor.transpose(turned[:, i, :], rows[:].rearrange("p (q i) -> p i q", i=PACK)[:, i, :], identity[:])
        cols = tile([P, 2 * GROUPS, PACK], F32, "cols")
        nc.scalar.copy(cols[:], turned[:, :, 0 : 2 * GROUPS * ROW_STEP : ROW_STEP].rearrange("p i r -> p r i"))

        def pick_scales(dst, first, count):
            nc.vector.tensor_copy(dst, scale_table[:].indirect(group_offsets(first, count)))

        def sort_scales(dst, src):
            nc.vector.tensor_copy(
                dst.rearrange("p (a i q) -> p a i q", i=PACK, q=P), src.rearrange("p (a q i) -> p a i q", i=PACK, q=P)
            )

        def place_scales(dst, src, first, rows_a_quad):
            for quad in (0, 2, 1, 3):
                at = first + rows_a_quad * quad
                nc.sync.dma_start(
                    out=dst[32 * quad : 32 * quad + 4, :, :].bitcast(I32), in_=src[at : at + rows_a_quad, :].bitcast(I32)
                )

        picked01 = tile_at([P, 8 * KIB], U8, "picked01", AT_X_RIGHT0 - 1)[:, 0 : 2 * PASS]
        picked23 = tile([P, 2 * PASS], U8, "picked23")
        sorted01 = tile([P, 2 * PASS], U8, "sorted01")
        pick_scales(picked01, 0, 2)
        pick_scales(picked23[:, 0:PASS], 2, 1)
        sort_scales(sorted01[:], picked01)
        pick_scales(picked23[:, PASS : 2 * PASS], 3, 1)
        place_scales(tab_planes[0], sorted01[:, 0:PASS], FIRST_LIVE, 4 * K_PASSES)
        x_raw[0, 1] = tile_at([P, PACK, HALF], F32, "x_right0", AT_X_RIGHT0)[:]
        x_fourth = by_slot(tile_at([P, 7 * KIB // 4], F32, "x_fourth", AT_X_THIRD)[:, 0 : PACK * QUARTER])
        x_third = by_slot(tile_at([P, 5 * KIB // 4], F32, "x_third", AT_X_FOURTH)[:, 0 : PACK * QUARTER])
        nc.sync.dma_start(out=x_raw[0, 1], in_=x_rows[0][:, :, HALF:M])
        nc.sync.dma_start(out=x_third, in_=x_rows[1][:, :, HALF : HALF + QUARTER])
        nc.sync.dma_start(out=x_fourth, in_=x_rows[1][:, :, HALF + QUARTER : M])
        nc.sync.dma_start(
            out=spread_scales[SPREAD_AT:P, :].bitcast(I32),
            in_=picked23[FIRST_LIVE:P, :].bitcast(I32).rearrange("p (a w) -> p a w", a=2),
        )
        place_scales(tab_planes[1], sorted01[:, PASS : 2 * PASS], FIRST_LIVE, 4 * K_PASSES)

        cb_own = {}
        for a in (0, 3):
            cb_own[a] = tile_at([P, 2 * KIB // 4], F32, "cb_own%d" % a, AT_CB[a])[:, 0:PACK]
            nc.scalar.copy(cb_own[a], turned[:, :, (GROUPS + a) * ROW_STEP])

        codes_left = [tile([P, HALF], U32, "x_codes_left%d" % d) for d in range(K_PASSES)]
        codes_right = [tile([P, HALF], U32, "x_codes_right0"), tile([P, HALF], U32, "x_codes_right1")]

        def x_codes(d, at):
            if at.start < HALF:
                return codes_left[d][:, at].bitcast(FP8X4)
            return codes_right[d][:, at.start - HALF : at.stop - HALF].bitcast(FP8X4)

        x_planes = [tile([P, M], U8, "x_planes%d" % d) for d in range(K_PASSES)]
        x_grouped = {}

        def cast_x(d, h):
            x_grouped[d, h] = tile([P, HALF * PACK], BF16, "x_grouped%d%d" % (d, h))
            nc.scalar.copy(interleaved(x_grouped[d, h][:]), planes(x_raw[d, h]))

        def quantise_x(d, h):
            at = slice(h * HALF, (h + 1) * HALF)
            nc.vector.quantize_mx(out=x_codes(d, at), scales=x_planes[d][:, at], in_=x_grouped[d, h][:])

        picked_words = {}
        tab_codes = {}

        def gather_words(a, dst):
            picked_words[a] = dst
            nc.vector.tensor_copy(dst[:], word_table[:].bitcast(U32).indirect(group_offsets(a, 1)))

        def part_words(a, dst):
            tab_codes[a] = dst
            nc.vector.tensor_copy(
                dst[:].bitcast(U16).rearrange("p (d h l q) -> p d h q l", d=2, h=2, l=2),
                picked_words[a][:].bitcast(U16).rearrange("p (q h l d) -> p d h q l", d=2, h=2, l=2),
            )

        h_codes = {}
        h_planes = {}
        units_done = []

        def first_stage(a, at, name, kib=None, spare=0, bias=None):
            shape = [P, PACK, at.stop - at.start]
            if kib is None:
                dst = tile(shape, F32, name)
            else:
                dst = by_slot(tile_at([P, PACK * shape[2] + spare], F32, name, kib)[:, 0 : PACK * shape[2]])
            bias = cols[:, GROUPS + a, :] if bias is None else bias
            for i in range(PACK):
                number = (PACK * (len(units_done) - (len(units_done) > 1)) + i) % DOT_BANKS
                dots = bank([P, shape[2]], "dots_%s_%d" % (name, i), number)
                for d in range(K_PASSES):
                    word = (d * PACK + i) * 2 * P
                    byte = (a == 3) * PASS + i * P
                    nc.tensor.matmul_mx(
                        out=dots[:],
                        lhsT=tab_codes[a][:, word : word + 2 * P].bitcast(FP4X4),
                        lhsT_scale=tab_planes[min(a, 2)][:, d, byte : byte + P],
                        rhs=x_codes(d, at),
                        rhs_scale=x_planes[d][:, at],
                        start=(d == 0),
                        stop=(d == K_PASSES - 1),
                    )
                nc.scalar.activation(dst[:, i, :], dots[:], TANH, bias=bias[:, i : i + 1])
            units_done.append(name)
            return dst

        def weigh_on_vector(dst, src, a):
            weights = turned[:, :, ROW_STEP * a].unsqueeze(1).unsqueeze(3).to_broadcast([P, src.shape[2] // RUN, PACK, RUN])
            nc.vector.tensor_tensor(interleaved(dst), planes(src), weights, MULT)

        def weigh_on_gpsimd(dst, src, a):
            nc.gpsimd.tensor_tensor(
                dst.rearrange("p (c e i) -> p c i e", e=PAIR, i=PACK),
                src.rearrange("p i (c e) -> p c i e", e=PAIR),
                cols[:, a, :].unsqueeze(1).unsqueeze(3).to_broadcast([P, src.shape[2] // PAIR, PACK, PAIR]),
                MULT,
            )

        def quantise_h(key, pieces, codes=None, plane_at=None):
            width = sum(src.shape[1] for at, src in pieces) // PACK
            name = "%d%d" % key
            h_codes[key] = codes if codes is not None else tile([P, width], U32, "h_codes" + name)
            if plane_at is None:
                h_planes[key] = tile([P, width], U8, "h_plane" + name)
            else:
                h_planes[key] = tile_at([P, width], U8, "h_plane" + name, plane_at)
            for at, src in pieces:
                to = slice(at, at + src.shape[1] // PACK)
                nc.vector.quantize_mx(out=h_codes[key][:, to].bitcast(FP8X4), scales=h_planes[key][:, to], in_=src)

        words_shape, codes_shape, grouped_shape = [P, PASS], [P, K_PASSES * 2 * PASS], [P, HALF * PACK]
        left, right = slice(0, HALF), slice(HALF, M)
        gather_words(0, tile(words_shape, U32, "picked_words0"))
        gather_words(1, tile(words_shape, U32, "picked_words1"))
        cast_x(0, 0)
        quantise_x(0, 0)
        part_words(0, tile(codes_shape, U8, "tab_codes0", tag="x_left0"))
        cast_x(1, 0)
        quantise_x(1, 0)
        part_words(1, tile_at(codes_shape, U8, "tab_codes1", AT_X_LEFT1))
        gather_words(2, tile_at(words_shape, U32, "picked_words2", AT_X_LEFT1 + 2))
        quarters = {}
        quarters[0, 0] = tile([P, QUARTER * PACK], BF16, "x_quarter00", tag="picked_words1")
        nc.gpsimd.tensor_scalar(
            quarters[0, 0][:].rearrange("p (c e i) -> p c i e", e=PAIR, i=PACK),
            x_raw[0, 1][:, :, 0:QUARTER].rearrange("p i (c e) -> p c i e", e=PAIR),
            1.0,
            0.0,
            MULT,
            ADD,
        )
        for key, src in (((0, 1), x_raw[0, 1][:, :, QUARTER:HALF]), ((1, 0), x_third), ((1, 1), x_fourth)):
            quarters[key] = tile([P, QUARTER * PACK], BF16, "x_quarter%d%d" % key)
            nc.scalar.copy(interleaved(quarters[key][:]), planes(src))
        for d, u in ((0, 1), (1, 0), (0, 0), (1, 1)):
            at = slice(HALF + u * QUARTER, HALF + (u + 1) * QUARTER)
            nc.vector.quantize_mx(out=x_codes(d, at), scales=x_planes[d][:, at], in_=quarters[d, u][:])
        sorted23 = tile([P, PASS], U8, "sorted23")
        sort_scales(sorted23[:], spread_scales[:])
        place_scales(tab_planes[2][:].rearrange("p d (a w) -> p (d a) w", a=2), sorted23, SPREAD_AT, 8 * K_PASSES)
        part_words(2, tile_at(codes_shape, U8, "tab_codes2", AT_X_FOURTH))

        al_planes = sorted23[:, 0:N]
        al_codes = tile([P, GROUPS, N], I32, "al_codes", tag="x_grouped10")
        for quad in range(4):
            nc.sync.dma_start(
                out=al_planes[32 * quad : 32 * quad + 16, :].bitcast(I32),
                in_=al_scales[:, 4 * quad : 4 * quad + 4, :].bitcast(I32),
            )
        nc.sync.dma_start(out=al_codes[:], in_=al_words.rearrange("a p n i -> p a (n i)").bitcast(I32))

        kern00 = first_stage(0, left, "kern00", AT_X_THIRD, 2 * KIB // 4)
        kern10 = first_stage(1, left, "kern10", AT_X_THIRD + 6)
        kern01 = first_stage(0, right, "kern01", bias=cb_own[0])
        kern11 = first_stage(1, right, "kern11", AT_KERN2)
        kern20 = first_stage(2, left, "kern20")
        kern21 = first_stage(2, right, "kern21")
        grouped00 = tile_at(grouped_shape, BF16, "grouped00", AT_X_LEFT1 + 3)
        weigh_on_gpsimd(grouped00[:], kern00, 0)
        gather_words(3, tile_at(words_shape, U32, "picked_words3", AT_X_FOURTH + 2))
        grouped10 = tile(grouped_shape, BF16, "grouped10")
        weigh_on_vector(grouped10[:], kern10[:], 1)
        grouped01 = tile(grouped_shape, BF16, "grouped01")
        weigh_on_vector(grouped01[:], kern01[:], 0)

        part_words(3, tile_at(codes_shape, U8, "tab_codes3", AT_X_THIRD - 1))
        quantise_h((1, 0), [(0, grouped10[:])], tile_at([P, HALF], U32, "h_codes10", AT_X_THIRD + 2), AT_CB[0])
        quantise_h((0, 1), [(0, grouped01[:])], tile_at([P, HALF], U32, "h_codes01", AT_X_THIRD + 3))
        quantise_h((0, 0), [(0, grouped00[:])], plane_at=AT_CB[0] + 0.5)

        kern30 = first_stage(3, left, "kern30", bias=cb_own[3])
        kern31 = first_stage(3, right, "kern31")
        grouped11 = tile_at(grouped_shape, BF16, "grouped11", AT_X_LEFT1 + 3)
        weigh_on_gpsimd(grouped11[:], kern11, 1)
        grouped20 = tile_at(grouped_shape, BF16, "grouped20", AT_X_THIRD + 4)
        weigh_on_vector(grouped20[:], kern20[:], 2)
        grouped21 = tile(grouped_shape, BF16, "grouped21")
        weigh_on_vector(grouped21[:], kern21[:], 2)
        grouped30 = tile(grouped_shape, BF16, "grouped30")
        weigh_on_vector(grouped30[:], kern30[:], 3)
        rounded = tile_at([P, PACK, SCALAR_COLS], BF16, "rounded", AT_ROUNDED)
        for i in range(PACK):
            nc.scalar.activation(rounded[:, i, :], kern31[:, i, HALF - SCALAR_COLS : HALF], COPY, scale=cols[:, 3, i : i + 1])
        fourth = tile([P, QUARTER * PACK], BF16, "fourth")
        nc.scalar.copy(interleaved(fourth[:]), planes(rounded[:, :, SCALAR_COLS - QUARTER :]))

        for u, (key, src) in enumerate((((2, 0), grouped20), ((3, 0), grouped30), ((1, 1), grouped11))):
            quantise_h(key, [(0, src[:])], tile_at([P, HALF], U32, "h_codes%d%d" % key, AT_KERN2 + u), AT_CB[3] + u / 4)
        third = tile([P, QUARTER * PACK], BF16, "third", tag="grouped30")
        own = HALF - SCALAR_COLS
        weigh_on_vector(third[:, 0 : own * PACK], kern31[:, :, 0:own], 3)
        nc.vector.tensor_copy(interleaved(third[:, own * PACK :]), planes(rounded[:, :, 0 : QUARTER - own]))
        quantise_h((2, 1), [(0, grouped21[:])], tile_at([P, HALF], U32, "h_codes21", AT_KERN2 + 3), AT_CB[3] + 0.75)
        quantise_h((3, 2), [(0, third[:])])
        quantise_h((3, 3), [(0, fourth[:])])

        y_left = bank([P, 2, HALF], "y_left", 3)
        y_right = {(u, g): bank([P, QUARTER], "y_right%d%d" % (u, g), (4 + 2 * u + g) % DOT_BANKS) for u in range(2) for g in range(2)}
        last = GROUPS - 1

        def add_pass(dst, a, g, key, cols_of_h, start, stop):
            nc.tensor.matmul_mx(
                out=dst,
                lhsT=al_codes[:, a, g * P : (g + 1) * P].bitcast(FP8X4),
                lhsT_scale=al_planes[4 * a : P, g * P : (g + 1) * P],
                rhs=h_codes[key][:, cols_of_h].bitcast(FP8X4),
                rhs_scale=h_planes[key][:, cols_of_h],
                start=start,
                stop=stop,
            )

        def add_left(a):
            for g in range(2):
                add_pass(y_left[:, g, :], a, g, (a, 0), slice(0, HALF), a == 0 and g == 0, a == last and g == 1)

        def quarter_of(a, u):
            return ((a, 2 + u), slice(0, QUARTER)) if a == last else ((a, 1), slice(u * QUARTER, (u + 1) * QUARTER))

        def add_quarter(a, u):
            key, cols_of_h = quarter_of(a, u)
            for g in range(2):
                add_pass(y_right[u, g][:], a, g, key, cols_of_h, a == 0, a == last)

        add_left(0)
        for u in range(2):
            add_quarter(0, u)
        for a in (1, 2, 3):
            add_left(a)
        for a in (1, 2, 3):
            for u in range(2):
                add_quarter(a, u)

        out_rows = out.rearrange("(g p) m -> p g m", p=P)
        for g in range(2):
            result_left = tile_at([P, HALF], F32, "result_left%d" % g, AT_ROUNDED - 0.5 + g)
            nc.scalar.copy(result_left[:], y_left[:, g, :])
            nc.sync.dma_start(out=out_rows[:, g, 0:HALF], in_=result_left[:])
        for u in range(2):
            at = slice(HALF + u * QUARTER, HALF + (u + 1) * QUARTER)
            result = [keep.tile([P, QUARTER], F32, name="result_right%d%d" % (u, g)) for g in range(2)]
            nc.scalar.copy(result[0][:], y_right[u, 0][:])
            (nc.sync, nc.scalar)[u].dma_start(out=out_rows[:, 0, at], in_=result[0][:])
            nc.vector.tensor_copy(result[1][:], y_right[u, 1][:])
            nc.sync.dma_start(out=out_rows[:, 1, at], in_=result[1][:])
